import numpy as np
import ml_dtypes


def mxq(x, axis, fmt="e4m3"):
    dtype, down = {"e4m3": (ml_dtypes.float8_e4m3fn, 7), "e5m2": (ml_dtypes.float8_e5m2, 14)}[fmt]
    v = np.moveaxis(np.asarray(x, np.float32).astype(ml_dtypes.bfloat16).astype(np.float64), axis, -1)
    blocks = v.reshape(v.shape[:-1] + (-1, 32))
    amax = np.abs(blocks).max(-1, keepdims=True)
    byte = np.maximum(np.where(amax > 0, np.frexp(amax)[1] - 1 + 127, 0) - down, 1)
    scale = np.exp2(byte - 127.0)
    codes = (blocks / scale).astype(np.float32).astype(dtype).astype(np.float64)
    return np.moveaxis((codes * scale).reshape(v.shape), -1, axis)


WIDE = False


def mx_kscale(k):
    if not WIDE:
        return np.ones(k)
    levels = np.array([10, -10, 5, -5, 0])
    if k % 512:
        return np.exp2(np.random.permutation(np.resize(levels, k // 32))).repeat(32)
    a = np.empty((k // 512, 16))
    for p in range(k // 512):
        a[p, :8] = np.random.permutation(np.resize(levels, 8))
        for g in range(8):
            far = levels[np.abs(levels - a[p, g]) >= 10]
            a[p, g + 8] = far[np.random.randint(len(far))]
    return np.exp2(a.ravel()).repeat(32)


def f64(x):
    return np.asarray(x).astype(np.float64)


def striped(idx):
    return np.tile(idx.reshape(-1, 16).T, (8, 1)).astype(np.uint16)


def unstriped(offs):
    return offs[:16].T.reshape(-1).astype(np.int64)


E2M1 = np.array([0.0, 0.5, 1.0, 1.5, 2.0, 3.0, 4.0, 6.0, -0.0, -0.5, -1.0, -1.5, -2.0, -3.0, -4.0, -6.0])


def pack_weight(w, fmt):
    k, n = w.shape
    w = f64(np.asarray(w, np.float32).astype(ml_dtypes.bfloat16)).reshape(k // 32, 32, n)
    amax = np.abs(w).max(1)
    if fmt == "e4m3":
        byte = np.frexp(amax)[1] - 1 + 127 - 7
    else:
        mant, ex = np.frexp(amax / 6.0)
        byte = np.where(mant > 0.5, ex, ex - 1) + 127
    byte = np.clip(np.where(amax > 0, byte, 1), 1, 254)
    scaled = (w * np.exp2(127.0 - byte)[:, None, :]).reshape(k, n).astype(np.float32)
    by_word = np.ascontiguousarray(scaled.reshape(k // 512, 128, 4, n).transpose(0, 1, 3, 2))
    if fmt == "e4m3":
        words = by_word.astype(ml_dtypes.float8_e4m3fn).view(np.uint8)
    else:
        c = by_word.astype(ml_dtypes.float4_e2m1fn).view(np.uint8) & 0xF
        words = (c[..., 0::2] | (c[..., 1::2] << 4)).reshape(k // 512, 128, 2 * n)
    return np.ascontiguousarray(words), np.ascontiguousarray(byte.astype(np.uint8).reshape(k // 512, 16, n))


def unpack_weight(words, scales, fmt):
    g, _, n = scales.shape
    words = np.ascontiguousarray(words).reshape(g, 128, n, -1)
    if fmt == "e4m3":
        vals = words.view(ml_dtypes.float8_e4m3fn).astype(np.float64)
    else:
        nib = np.empty((g, 128, n, 4), np.uint8)
        nib[..., 0::2] = words & 0xF
        nib[..., 1::2] = words >> 4
        vals = E2M1[nib]
    vals = vals * np.repeat(np.exp2(scales.astype(np.float64) - 127.0), 8, axis=1)[..., None]
    return vals.transpose(0, 1, 3, 2).reshape(g * 512, n)


def relu(v):
    return np.maximum(v, 0.0)


def d_relu(v):
    return (v > 0).astype(np.float64)


K, T, E, C, H, N = 512, 768, 6, 256, 512, 1024


def by_expert(wq, xq):
    return np.concatenate([wq[e].T @ xq[:, e * C:(e + 1) * C] for e in range(E)], axis=1)


def setup_inputs():
    n = np.random.standard_normal
    s = mx_kscale(N)[:, None]
    u = mx_kscale(H)
    first = np.random.permutation(np.repeat(np.arange(E), T // E))
    second = (first + 1 + np.random.permutation(np.repeat(np.arange(E - 1), -(-T // (E - 1)))[:T])) % E
    while np.bincount(second, minlength=E).max() != T // E:
        load = np.bincount(second, minlength=E); hi, lo = int(load.argmax()), int(load.argmin())
        t = np.flatnonzero((second == hi) & (first != lo))[0]; second[t] = lo
    slot_token = np.empty(E * C, np.int64); pos = np.empty((2, T), np.int64); fill = np.zeros(E, np.int64)
    place = np.stack([np.random.permutation(C) for _ in range(E)])
    for r, deal in enumerate((first, second)):
        for t in np.random.permutation(T):
            e = deal[t]; j = e * C + place[e, fill[e]]; fill[e] += 1; slot_token[j] = t; pos[r, t] = j
    g = np.random.uniform(0.2, 0.8, T)
    w_slot = np.empty(E * C); w_slot[pos[0]] = g; w_slot[pos[1]] = 1.0 - g
    dy = pack_weight(n((N, T)) * s, "e4m3")
    w2 = [pack_weight(m, "e2m1") for m in n((E, N, H)) / np.sqrt(N) / s[None] * u[None, None, :]]
    w1 = [pack_weight(m, "e2m1") for m in n((E, H, K)) / np.sqrt(H) / u[None, :, None]]
    w3 = [pack_weight(m, "e2m1") for m in n((E, H, K)) / np.sqrt(H) / u[None, :, None]]
    return {
        "dy_words": dy[0],
        "dy_scales": dy[1],
        "a1": n((H, E * C)).astype(np.float32),
        "a3": n((H, E * C)).astype(np.float32),
        "w2_words": np.stack([m[0] for m in w2]),
        "w2_scales": np.stack([m[1] for m in w2]),
        "w1_words": np.stack([m[0] for m in w1]),
        "w1_scales": np.stack([m[1] for m in w1]),
        "w3_words": np.stack([m[0] for m in w3]),
        "w3_scales": np.stack([m[1] for m in w3]),
        "gate": np.tile(w_slot, (H, 1)).astype(np.float32),
        "offs": striped(slot_token),
        "pos1": striped(pos[0]),
        "pos2": striped(pos[1]),
    }


def reference(dy_words, dy_scales, a1, a3, w2_words, w2_scales, w1_words, w1_scales, w3_words, w3_scales, gate, offs, pos1, pos2):
    idx = unstriped(offs)
    w2 = np.stack([unpack_weight(w2_words[e], w2_scales[e], "e2m1") for e in range(E)])
    w1 = np.stack([unpack_weight(w1_words[e], w1_scales[e], "e2m1") for e in range(E)])
    w3 = np.stack([unpack_weight(w3_words[e], w3_scales[e], "e2m1") for e in range(E)])
    gq = unpack_weight(dy_words, dy_scales, "e4m3")[:, idx]
    dh = f64(gate) * by_expert(w2, gq)
    da1 = dh * f64(a3) * d_relu(f64(a1))
    da3 = dh * relu(f64(a1))
    dx = by_expert(w1, mxq(da1, 0, "e4m3")) + by_expert(w3, mxq(da3, 0, "e4m3"))
    return dx[:, unstriped(pos1)] + dx[:, unstriped(pos2)]

@@ -1,0 +1,259 @@
+from contextlib import ExitStack
+
+import concourse.mybir as mybir
+from concourse.masks import make_identity
+
+K, T, E, C, H, N = 512, 768, 6, 256, 512, 1024
+S = E * C
+FLOPS = 2 * S * (N * H + 2 * H * K)
+BYTES = (N * T + N * T // 32 + 2 * 4 * H * S + E * (N * H + 2 * H * K) // 2 + E * (N * H + 2 * H * K) // 32
+         + 4 * S + 2 * 128 * (S + 2 * T) // 16 + 4 * K * T)
+
+F32 = mybir.dt.float32
+BF16 = mybir.dt.bfloat16
+I32 = mybir.dt.int32
+U32 = mybir.dt.uint32
+U16 = mybir.dt.uint16
+U8 = mybir.dt.uint8
+FP8X4 = mybir.dt.float8_e4m3fn_x4
+FP4X4 = mybir.dt.float4_e2m1fn_x4
+ALU = mybir.AluOpType
+ACT = mybir.ActivationFunctionType
+
+P = 128
+PACK = 4
+PASSES = N // (P * PACK)
+TILES = S // P
+KT = K // P
+PAIR = 2 * C
+RUN = 4
+LAG = 2
+A_CHUNKS = ((0, 1), (1, 2), (2, 3), (3, 4), (4, 5), (5, 6))
+VECTOR_TILES = (11,)
+
+
+def tile_moe_bdx_glu_relu_kernel(
+    tc, dy_words, dy_scales, a1, a3, w2_words, w2_scales, w1_words, w1_scales, w3_words, w3_scales,
+    gate, offs, pos1, pos2, out,
+):
+    nc = tc.nc
+    with ExitStack() as ctx:
+        keep = ctx.enter_context(tc.tile_pool(name="keep", bufs=1))
+        ring = ctx.enter_context(tc.tile_pool(name="ring", bufs=3))
+        psum = ctx.enter_context(tc.psum_pool(name="psum", bufs=2))
+
+        def held(shape, dtype, name):
+            return keep.tile(shape, dtype, name=name, align_bytes=64)
+
+        offs_sb = keep.tile([P, S // 16], U16, name="offs_sb")
+        pos1_sb = keep.tile([P, T // 16], U16, name="pos1_sb")
+        pos2_sb = keep.tile([P, T // 16], U16, name="pos2_sb")
+        dyw = [held([P, T], I32, "dyw%d" % o) for o in range(PASSES)]
+        dys = held([P, T], U8, "dys")
+        gw = [[held([P, PAIR], U32, "gw%d_%d" % (o, g)) for g in range(E // 2)] for o in range(PASSES)]
+        gs = held([P, S], U8, "gs")
+        gs1 = held([P, S], U8, "gs1")
+        w2 = [held([P, 2 * PASSES, 2 * H], U8, "w2_%d" % g) for g in range(E // 2)]
+        w1 = [held([P, 2, 2 * K], U8, "w1_%d" % g) for g in range(E // 2)]
+        w3 = [held([P, 2, 2 * K], U8, "w3_%d" % g) for g in range(E // 2)]
+        w2s = held([P, E * PASSES, H], U8, "w2s")
+        w1s = held([P, E, K], U8, "w1s")
+        w3s = held([P, E, K], U8, "w3s")
+        dx = held([P, KT, S], F32, "dx")
+        gate_rows = held([P, P], F32, "gate_rows")
+        gate_col = held([P, TILES], F32, "gate_col")
+        ident = held([P, P], F32, "ident")
+
+        nc.vector.memset(dys[:].bitcast(I32), 0)
+        nc.vector.memset(w2s[:].rearrange("p a n -> p (a n)").bitcast(I32), 0)
+        nc.vector.memset(gs1[:].bitcast(I32), 0)
+        make_identity(nc, ident[:])
+        nc.gpsimd.memset(w1s[:].rearrange("p a n -> p (a n)").bitcast(I32), 0)
+        nc.gpsimd.memset(w3s[:].rearrange("p a n -> p (a n)").bitcast(I32), 0)
+
+        def load_scale_rows(queue, plane, scales):
+            rows = scales.rearrange("e s f n -> f (e s) n").bitcast(I32)
+            for q in range(4):
+                queue.dma_start(plane[32 * q : 32 * q + 4].bitcast(I32), rows[4 * q : 4 * q + 4])
+
+        def load_words(tile, words, g):
+            nc.sync.dma_start(tile[g][:].bitcast(I32), words[2 * g : 2 * g + 2].rearrange("e s p n -> p (e s) n").bitcast(I32))
+
+        a1_of, a3_of = {}, {}
+
+        def load_saved(c):
+            e0, e1 = A_CHUNKS[c]
+            for tiles, saved, name in ((a1_of, a1, "a1"), (a3_of, a3, "a3")):
+                tile = held([P, PACK, (e1 - e0) * C], F32, "%s_%d" % (name, c))
+                nc.sync.dma_start(tile[:], saved.rearrange("(p t) s -> p t s", t=PACK)[:, :, e0 * C : e1 * C])
+                for e in range(e0, e1):
+                    tiles[e] = tile[:, :, (e - e0) * C : (e - e0 + 1) * C]
+
+        nc.sync.dma_start(offs_sb[:], offs)
+        for q in range(4):
+            nc.sync.dma_start(
+                dys[32 * q : 32 * q + 4 * PASSES, :].bitcast(I32), dy_scales[:, 4 * q : 4 * q + 4, :].bitcast(I32)
+            )
+        for o in range(PASSES):
+            nc.sync.dma_start(dyw[o][:], dy_words[o].rearrange("p t d -> p (t d)").bitcast(I32))
+        load_scale_rows(nc.sync, w2s, w2_scales)
+        load_scale_rows(nc.gpsimd, w1s, w1_scales)
+        load_scale_rows(nc.gpsimd, w3s, w3_scales)
+        nc.sync.dma_start(gate_rows[:], gate.rearrange("h (j s) -> (h j) s", s=P)[0:P, :])
+        load_words(w2, w2_words, 0)
+        load_words(w2, w2_words, 1)
+        load_saved(0)
+        load_words(w2, w2_words, 2)
+        load_saved(1)
+        load_words(w1, w1_words, 0)
+        load_words(w3, w3_words, 0)
+        load_saved(2)
+        load_saved(3)
+        load_words(w1, w1_words, 1)
+        load_words(w3, w3_words, 1)
+        load_saved(4)
+        load_saved(5)
+        load_words(w1, w1_words, 2)
+        load_words(w3, w3_words, 2)
+        nc.sync.dma_start(pos1_sb[:], pos1)
+        nc.sync.dma_start(pos2_sb[:], pos2)
+
+        gate_ps = psum.tile([P, PACK, P], F32, name="gate_ps", tag="turned", bufs=4)
+        nc.tensor.transpose(gate_ps[:, 0, :], gate_rows[:], ident[:])
+        nc.scalar.copy(gate_col[:], gate_ps[:, 0, 0:TILES])
+
+        for g in range(E // 2):
+            nc.vector.tensor_copy(
+                gs[:, g * PAIR : (g + 1) * PAIR], dys[:].indirect(offs_sb[:, g * PAIR // 16 : (g + 1) * PAIR // 16])
+            )
+        for q in range(4):
+            nc.scalar.dma_start(gs1[32 * q : 32 * q + 4, :].bitcast(I32), gs[32 * q + 4 : 32 * q + 8, :].bitcast(I32))
+        for g in range(E // 2):
+            for o in range(PASSES):
+                nc.vector.tensor_copy(
+                    gw[o][g][:], dyw[o][:].bitcast(U32).indirect(offs_sb[:, g * PAIR // 16 : (g + 1) * PAIR // 16])
+                )
+        g_scales = (gs, gs1)
+
+        dh_rows, dh_cols, relu, live, da, codes = {}, {}, {}, {}, {}, {}
+
+        def first_product(e):
+            for j in (2 * e, 2 * e + 1):
+                acc = psum.tile([P, H], F32, name="acc1", tag="first", bufs=2)
+                for o in range(PASSES):
+                    nc.tensor.matmul_mx(
+                        out=acc[:],
+                        lhsT=gw[o][e // 2][:, (j % 4) * P : (j % 4 + 1) * P].bitcast(FP8X4),
+                        lhsT_scale=g_scales[o][:, j * P : (j + 1) * P],
+                        rhs=w2[e // 2][:, (e % 2) * PASSES + o, :].bitcast(FP4X4),
+                        rhs_scale=w2s[:, e * PASSES + o, :],
+                        start=(o == 0),
+                        stop=(o == PASSES - 1),
+                    )
+                dh_rows[j] = ring.tile([P, PACK, P], F32, name="dh_rows", tag="dh_rows", bufs=TILES, align_bytes=64)
+                nc.scalar.activation(
+                    dh_rows[j][:], acc[:].rearrange("s (m t) -> s t m", t=PACK), ACT.Copy, scale=gate_col[:, j : j + 1]
+                )
+
+        def rectify(e):
+            relu[e] = ring.tile([P, PACK, C], F32, name="relu", tag="relu", bufs=3, align_bytes=64)
+            nc.scalar.activation(relu[e][:], a1_of[e], ACT.Relu)
+
+        def turn(e):
+            for j in (2 * e, 2 * e + 1):
+                dh_cols[j] = psum.tile([P, PACK, P], F32, name="dh_cols", tag="turned", bufs=4)
+                for t in range(PACK):
+                    nc.tensor.transpose(dh_cols[j][:, t, :], dh_rows[j][:, t, :], ident[:])
+
+        def half(view, j):
+            return view[:, :, (j % 2) * P : (j % 2 + 1) * P]
+
+        def in_runs(view):
+            return view.rearrange("p t (c i) -> p c t i", i=RUN)
+
+        def mask(j):
+            da[j] = ring.tile([P, 2, P * PACK], BF16, name="da", tag="da", bufs=4, align_bytes=64)
+            live[j] = ring.tile([P, PACK, P], F32, name="live", tag="live", bufs=3, align_bytes=64)
+            nc.vector.scalar_tensor_tensor(
+                live[j][:], half(a1_of[j // 2], j), 0.0, dh_cols[j][:], ALU.is_gt, ALU.mult
+            )
+            if j not in VECTOR_TILES:
+                nc.gpsimd.tensor_tensor(
+                    da[j][:, 0, :].rearrange("p (c i t) -> p c t i", i=2, t=PACK),
+                    live[j][:].rearrange("p t (c i) -> p c t i", i=2),
+                    half(a3_of[j // 2], j).rearrange("p t (c i) -> p c t i", i=2),
+                    ALU.mult,
+                )
+
+        def products(j):
+            nc.vector.tensor_tensor(
+                da[j][:, 1, :].rearrange("p (c i t) -> p c t i", i=RUN, t=PACK),
+                in_runs(dh_cols[j][:]),
+                in_runs(half(relu[j // 2][:], j)),
+                ALU.mult,
+            )
+            if j in VECTOR_TILES:
+                nc.vector.tensor_tensor(
+                    da[j][:, 0, :].rearrange("p (c i t) -> p c t i", i=RUN, t=PACK),
+                    in_runs(live[j][:]),
+                    in_runs(half(a3_of[j // 2], j)),
+                    ALU.mult,
+                )
+
+        def quantise(j):
+            words = ring.tile([P, 2 * P], U32, name="da_words", tag="da_words", bufs=8, align_bytes=64)
+            scales = ring.tile([P, 2 * P], U8, name="da_scales", tag="da_scales", bufs=8, align_bytes=64)
+            nc.vector.quantize_mx(
+                out=words[:].bitcast(FP8X4), scales=scales[:], in_=da[j][:].rearrange("p w n -> p (w n)")
+            )
+            codes[j] = (words, scales)
+
+        def second_product(j):
+            e = j // 2
+            words, scales = codes[j]
+            acc = psum.tile([P, KT, P], F32, name="acc2", tag="second", bufs=2)
+            for kt in range(KT):
+                for which, (w, ws) in enumerate(((w1, w1s), (w3, w3s))):
+                    nc.tensor.matmul_mx(
+                        out=acc[:, kt, :],
+                        lhsT=w[e // 2][:, e % 2, 2 * P * kt : 2 * P * (kt + 1)].bitcast(FP4X4),
+                        lhsT_scale=ws[:, e, P * kt : P * (kt + 1)],
+                        rhs=words[:, which * P : (which + 1) * P].bitcast(FP8X4),
+                        rhs_scale=scales[:, which * P : (which + 1) * P],
+                        start=(which == 0),
+                        stop=(which == 1),
+                    )
+            nc.scalar.copy(dx[:, :, j * P : (j + 1) * P], acc[:])
+
+        first_product(0)
+        rectify(0)
+        turn(0)
+        first_product(1)
+        rectify(1)
+        for e in range(2, E):
+            first_product(e)
+        for j in range(TILES + LAG):
+            e = j // 2
+            if j % 2 == 0 and e + 1 < E:
+                turn(e + 1)
+            if j < TILES:
+                mask(j)
+            if j >= LAG:
+                quantise(j - LAG)
+            if j < TILES:
+                products(j)
+            if j % 2 == 1 and e + 2 < E:
+                rectify(e + 2)
+            if j >= LAG:
+                second_product(j - LAG)
+
+        pieces = [(kt, 0, T) for kt in range(KT - 1)] + [(KT - 1, 0, T // 2), (KT - 1, T // 2, T)]
+        for kt, t0, t1 in pieces:
+            first = ring.tile([P, t1 - t0], F32, name="first", tag="first", bufs=2, align_bytes=64)
+            second = ring.tile([P, t1 - t0], F32, name="second", tag="second", bufs=2, align_bytes=64)
+            total = ring.tile([P, t1 - t0], F32, name="total", tag="total", bufs=3, align_bytes=64)
+            nc.vector.tensor_copy(first[:], dx[:, kt, :].indirect(pos1_sb[:, t0 // 16 : t1 // 16]))
+            nc.vector.tensor_copy(second[:], dx[:, kt, :].indirect(pos2_sb[:, t0 // 16 : t1 // 16]))
+            adder = nc.vector if (kt, t1) == (KT - 1, T) else nc.gpsimd
+            adder.tensor_tensor(total[:], first[:], second[:], ALU.add)
+            nc.sync.dma_start(out[kt * P : (kt + 1) * P, t0:t1], total[:])

@@ -27,9 +27,7 @@ TILES = S // P
 KT = K // P
 PAIR = 2 * C
 RUN = 4
-LAG = 2
 A_CHUNKS = ((0, 1), (1, 2), (2, 3), (3, 4), (4, 5), (5, 6))
-VECTOR_TILES = (11,)
 
 
 def tile_moe_bdx_glu_relu_kernel(
@@ -171,34 +169,19 @@ def tile_moe_bdx_glu_relu_kernel(
         def in_runs(view):
             return view.rearrange("p t (c i) -> p c t i", i=RUN)
 
-        def mask(j):
-            da[j] = ring.tile([P, 2, P * PACK], BF16, name="da", tag="da", bufs=4, align_bytes=64)
-            live[j] = ring.tile([P, PACK, P], F32, name="live", tag="live", bufs=3, align_bytes=64)
-            nc.vector.scalar_tensor_tensor(
-                live[j][:], half(a1_of[j // 2], j), 0.0, dh_cols[j][:], ALU.is_gt, ALU.mult
-            )
-            if j not in VECTOR_TILES:
-                nc.gpsimd.tensor_tensor(
-                    da[j][:, 0, :].rearrange("p (c i t) -> p c t i", i=2, t=PACK),
-                    live[j][:].rearrange("p t (c i) -> p c t i", i=2),
-                    half(a3_of[j // 2], j).rearrange("p t (c i) -> p c t i", i=2),
-                    ALU.mult,
-                )
+        def mask(e):
+            live[e] = ring.tile([P, PACK, C], F32, name="live", tag="live", bufs=3, align_bytes=64)
+            nc.vector.scalar_tensor_tensor(live[e][:], a1_of[e], 0.0, a3_of[e], ALU.is_gt, ALU.mult)
 
-        def products(j):
+        def product(j, which):
+            if which == 0:
+                da[j] = ring.tile([P, 2, P * PACK], BF16, name="da", tag="da", bufs=4, align_bytes=64)
             nc.vector.tensor_tensor(
-                da[j][:, 1, :].rearrange("p (c i t) -> p c t i", i=RUN, t=PACK),
+                da[j][:, which, :].rearrange("p (c i t) -> p c t i", i=RUN, t=PACK),
                 in_runs(dh_cols[j][:]),
-                in_runs(half(relu[j // 2][:], j)),
+                in_runs(half((live, relu)[which][j // 2][:], j)),
                 ALU.mult,
             )
-            if j in VECTOR_TILES:
-                nc.vector.tensor_tensor(
-                    da[j][:, 0, :].rearrange("p (c i t) -> p c t i", i=RUN, t=PACK),
-                    in_runs(live[j][:]),
-                    in_runs(half(a3_of[j // 2], j)),
-                    ALU.mult,
-                )
 
         def quantise(j):
             words = ring.tile([P, 2 * P], U32, name="da_words", tag="da_words", bufs=8, align_bytes=64)
@@ -208,11 +191,11 @@ def tile_moe_bdx_glu_relu_kernel(
             )
             codes[j] = (words, scales)
 
-        def second_product(j):
+        def second_product(j, kt0, kt1):
             e = j // 2
             words, scales = codes[j]
             acc = psum.tile([P, KT, P], F32, name="acc2", tag="second", bufs=2)
-            for kt in range(KT):
+            for kt in range(kt0, kt1):
                 for which, (w, ws) in enumerate(((w1, w1s), (w3, w3s))):
                     nc.tensor.matmul_mx(
                         out=acc[:, kt, :],
@@ -223,7 +206,7 @@ def tile_moe_bdx_glu_relu_kernel(
                         start=(which == 0),
                         stop=(which == 1),
                     )
-            nc.scalar.copy(dx[:, :, j * P : (j + 1) * P], acc[:])
+            nc.scalar.copy(dx[:, kt0:kt1, j * P : (j + 1) * P], acc[:, kt0:kt1, :])
 
         first_product(0)
         rectify(0)
@@ -232,20 +215,25 @@ def tile_moe_bdx_glu_relu_kernel(
         rectify(1)
         for e in range(2, E):
             first_product(e)
-        for j in range(TILES + LAG):
+        mask(0)
+        for j in range(TILES + 1):
             e = j // 2
             if j % 2 == 0 and e + 1 < E:
                 turn(e + 1)
             if j < TILES:
-                mask(j)
-            if j >= LAG:
-                quantise(j - LAG)
+                product(j, 0)
+            if j >= 1:
+                quantise(j - 1)
             if j < TILES:
-                products(j)
+                product(j, 1)
+            if j % 2 == 0 and e + 1 < E:
+                mask(e + 1)
             if j % 2 == 1 and e + 2 < E:
                 rectify(e + 2)
-            if j >= LAG:
-                second_product(j - LAG)
+            if 1 <= j < TILES:
+                second_product(j - 1, 0, KT)
+        second_product(TILES - 1, 0, 1)
+        second_product(TILES - 1, 1, KT)
 
         pieces = [(kt, 0, T) for kt in range(KT - 1)] + [(KT - 1, 0, T // 2), (KT - 1, T // 2, T)]
         for kt, t0, t1 in pieces:

@@ -27,6 +27,8 @@ TILES = S // P
 KT = K // P
 PAIR = 2 * C
 RUN = 4
+POOL_RUN = 2
+AHEAD = 2
 A_CHUNKS = ((0, 1), (1, 2), (2, 3), (3, 4), (4, 5), (5, 6))
 
 
@@ -124,8 +126,8 @@ def tile_moe_bdx_glu_relu_kernel(
             nc.vector.tensor_copy(
                 gs[:, g * PAIR : (g + 1) * PAIR], dys[:].indirect(offs_sb[:, g * PAIR // 16 : (g + 1) * PAIR // 16])
             )
-        for q in range(4):
-            nc.scalar.dma_start(gs1[32 * q : 32 * q + 4, :].bitcast(I32), gs[32 * q + 4 : 32 * q + 8, :].bitcast(I32))
+        for cols in (slice(0, PAIR), slice(PAIR, S)):
+            nc.scalar.dma_start(gs1[0:100, cols].bitcast(I32), gs[4:104, cols].bitcast(I32))
         for g in range(E // 2):
             for o in range(PASSES):
                 nc.vector.tensor_copy(
@@ -133,7 +135,7 @@ def tile_moe_bdx_glu_relu_kernel(
                 )
         g_scales = (gs, gs1)
 
-        dh_rows, dh_cols, relu, live, da, codes = {}, {}, {}, {}, {}, {}
+        dh_rows, dh_cols, relu, live, masked, da, codes = {}, {}, {}, {}, {}, {}, {}
 
         def first_product(e):
             for j in (2 * e, 2 * e + 1):
@@ -170,7 +172,7 @@ def tile_moe_bdx_glu_relu_kernel(
             return view.rearrange("p t (c i) -> p c t i", i=RUN)
 
         def mask(e):
-            live[e] = ring.tile([P, PACK, C], F32, name="live", tag="live", bufs=3, align_bytes=64)
+            live[e] = ring.tile([P, PACK, C], F32, name="live", tag="live", bufs=AHEAD, align_bytes=64)
             nc.vector.scalar_tensor_tensor(live[e][:], a1_of[e], 0.0, a3_of[e], ALU.is_gt, ALU.mult)
 
         def product(j, which):
@@ -180,6 +182,21 @@ def tile_moe_bdx_glu_relu_kernel(
                 da[j][:, which, :].rearrange("p (c i t) -> p c t i", i=RUN, t=PACK),
                 in_runs(dh_cols[j][:]),
                 in_runs(half((live, relu)[which][j // 2][:], j)),
+                ALU.mult,
+            )
+
+        def masked_dh(j):
+            da[j] = ring.tile([P, 2, P * PACK], BF16, name="da", tag="da", bufs=4, align_bytes=64)
+            masked[j] = ring.tile([P, PACK, P], F32, name="masked", tag="masked", bufs=3, align_bytes=64)
+            nc.vector.scalar_tensor_tensor(
+                masked[j][:], half(a1_of[j // 2], j), 0.0, dh_cols[j][:], ALU.is_gt, ALU.mult
+            )
+
+        def times_a3(engine, run, j):
+            engine.tensor_tensor(
+                da[j][:, 0, :].rearrange("p (c i t) -> p c t i", i=run, t=PACK),
+                masked[j][:].rearrange("p t (c i) -> p c t i", i=run),
+                half(a3_of[j // 2], j).rearrange("p t (c i) -> p c t i", i=run),
                 ALU.mult,
             )
 
@@ -216,22 +233,42 @@ def tile_moe_bdx_glu_relu_kernel(
         for e in range(2, E):
             first_product(e)
         mask(0)
-        for j in range(TILES + 1):
-            e = j // 2
-            if j % 2 == 0 and e + 1 < E:
+        for e in range(E):
+            lo, hi = 2 * e, 2 * e + 1
+            if e + 1 < E:
                 turn(e + 1)
-            if j < TILES:
-                product(j, 0)
-            if j >= 1:
-                quantise(j - 1)
-            if j < TILES:
-                product(j, 1)
-            if j % 2 == 0 and e + 1 < E:
-                mask(e + 1)
-            if j % 2 == 1 and e + 2 < E:
+            if e < AHEAD:
+                product(lo, 0)
+                if e > 0:
+                    quantise(lo - 1)
+                product(lo, 1)
+                if e + 1 < AHEAD:
+                    mask(e + 1)
+                if e > 0:
+                    second_product(lo - 1, 0, KT)
+                product(hi, 0)
+                quantise(lo)
+                product(hi, 1)
+                if e + 1 == AHEAD:
+                    quantise(hi)
+            else:
+                masked_dh(lo)
+                times_a3(nc.gpsimd, POOL_RUN, lo)
+                product(lo, 1)
+                masked_dh(hi)
+                product(hi, 1)
+                if e + 1 < E:
+                    times_a3(nc.vector, RUN, hi)
+                    quantise(lo)
+                else:
+                    quantise(lo)
+                    times_a3(nc.vector, RUN, hi)
+                quantise(hi)
+            if e + 2 < E:
                 rectify(e + 2)
-            if 1 <= j < TILES:
-                second_product(j - 1, 0, KT)
+            second_product(lo, 0, KT)
+            if AHEAD <= e + 1 < E:
+                second_product(hi, 0, KT)
         second_product(TILES - 1, 0, 1)
         second_product(TILES - 1, 1, KT)
 

@@ -27,9 +27,9 @@ TILES = S // P
 KT = K // P
 PAIR = 2 * C
 RUN = 4
-POOL_RUN = 2
-AHEAD = 2
-A_CHUNKS = ((0, 1), (1, 2), (2, 3), (3, 4), (4, 5), (5, 6))
+QUANT_GROUPS = ((0, 4), (4, 8), (8, 10), (10, 11), (11, 12))
+BANK_GROUPS = ((0, 4), (4, 8), (8, 12))
+FIRST_BANK_GROUPS = ((0, 4), (4, 8), (8, 11), (11, 12))
 
 
 def tile_moe_bdx_glu_relu_kernel(
@@ -59,35 +59,31 @@ def tile_moe_bdx_glu_relu_kernel(
         w2s = held([P, E * PASSES, H], U8, "w2s")
         w1s = held([P, E, K], U8, "w1s")
         w3s = held([P, E, K], U8, "w3s")
-        dx = held([P, KT, S], F32, "dx")
+        a1_sb = [held([P, PACK, PAIR], F32, "a1_%d" % g) for g in range(E // 2)]
+        a3_sb = [held([P, PACK, PAIR], F32, "a3_%d" % g) for g in range(E // 2)]
+        dx = [held([P, S], F32, "dx%d" % kt) for kt in range(KT)]
         gate_rows = held([P, P], F32, "gate_rows")
         gate_col = held([P, TILES], F32, "gate_col")
         ident = held([P, P], F32, "ident")
 
-        nc.vector.memset(dys[:].bitcast(I32), 0)
+        nc.gpsimd.memset(dys[:].bitcast(I32), 0)
         nc.vector.memset(w2s[:].rearrange("p a n -> p (a n)").bitcast(I32), 0)
+        nc.gpsimd.memset(gate_rows[:], 0.0)
         nc.vector.memset(gs1[:].bitcast(I32), 0)
         make_identity(nc, ident[:])
         nc.gpsimd.memset(w1s[:].rearrange("p a n -> p (a n)").bitcast(I32), 0)
         nc.gpsimd.memset(w3s[:].rearrange("p a n -> p (a n)").bitcast(I32), 0)
 
-        def load_scale_rows(queue, plane, scales):
+        def load_scale_rows(plane, scales):
             rows = scales.rearrange("e s f n -> f (e s) n").bitcast(I32)
-            for q in range(4):
-                queue.dma_start(plane[32 * q : 32 * q + 4].bitcast(I32), rows[4 * q : 4 * q + 4])
+            for r in range(4):
+                nc.sync.dma_start(plane[r:P:32].bitcast(I32), rows[r:16:4])
 
         def load_words(tile, words, g):
             nc.sync.dma_start(tile[g][:].bitcast(I32), words[2 * g : 2 * g + 2].rearrange("e s p n -> p (e s) n").bitcast(I32))
 
-        a1_of, a3_of = {}, {}
-
-        def load_saved(c):
-            e0, e1 = A_CHUNKS[c]
-            for tiles, saved, name in ((a1_of, a1, "a1"), (a3_of, a3, "a3")):
-                tile = held([P, PACK, (e1 - e0) * C], F32, "%s_%d" % (name, c))
-                nc.sync.dma_start(tile[:], saved.rearrange("(p t) s -> p t s", t=PACK)[:, :, e0 * C : e1 * C])
-                for e in range(e0, e1):
-                    tiles[e] = tile[:, :, (e - e0) * C : (e - e0 + 1) * C]
+        def load_saved(tile, saved, g):
+            nc.sync.dma_start(tile[g][:], saved.rearrange("(p t) s -> p t s", t=PACK)[:, :, g * PAIR : (g + 1) * PAIR])
 
         nc.sync.dma_start(offs_sb[:], offs)
         for q in range(4):
@@ -96,25 +92,18 @@ def tile_moe_bdx_glu_relu_kernel(
             )
         for o in range(PASSES):
             nc.sync.dma_start(dyw[o][:], dy_words[o].rearrange("p t d -> p (t d)").bitcast(I32))
-        load_scale_rows(nc.sync, w2s, w2_scales)
-        load_scale_rows(nc.gpsimd, w1s, w1_scales)
-        load_scale_rows(nc.gpsimd, w3s, w3_scales)
-        nc.sync.dma_start(gate_rows[:], gate.rearrange("h (j s) -> (h j) s", s=P)[0:P, :])
-        load_words(w2, w2_words, 0)
-        load_words(w2, w2_words, 1)
-        load_saved(0)
-        load_words(w2, w2_words, 2)
-        load_saved(1)
-        load_words(w1, w1_words, 0)
-        load_words(w3, w3_words, 0)
-        load_saved(2)
-        load_saved(3)
-        load_words(w1, w1_words, 1)
-        load_words(w3, w3_words, 1)
-        load_saved(4)
-        load_saved(5)
-        load_words(w1, w1_words, 2)
-        load_words(w3, w3_words, 2)
+        nc.scalar.dma_start(gate_rows[0:TILES, :], gate[0].rearrange("(j s) -> j s", s=P))
+        for g in range(E // 2):
+            load_saved(a1_sb, a1, g)
+            if g == 0:
+                load_scale_rows(w2s, w2_scales)
+            load_words(w2, w2_words, g)
+            load_saved(a3_sb, a3, g)
+        load_scale_rows(w1s, w1_scales)
+        load_scale_rows(w3s, w3_scales)
+        for g in range(E // 2):
+            load_words(w1, w1_words, g)
+            load_words(w3, w3_words, g)
         nc.sync.dma_start(pos1_sb[:], pos1)
         nc.sync.dma_start(pos2_sb[:], pos2)
 
@@ -122,163 +111,134 @@ def tile_moe_bdx_glu_relu_kernel(
         nc.tensor.transpose(gate_ps[:, 0, :], gate_rows[:], ident[:])
         nc.scalar.copy(gate_col[:], gate_ps[:, 0, 0:TILES])
 
+        def pair_offsets(g):
+            return offs_sb[:, g * PAIR // 16 : (g + 1) * PAIR // 16]
+
+        def gather_words(o, g):
+            nc.vector.tensor_copy(gw[o][g][:], dyw[o][:].bitcast(U32).indirect(pair_offsets(g)))
+
         for g in range(E // 2):
-            nc.vector.tensor_copy(
-                gs[:, g * PAIR : (g + 1) * PAIR], dys[:].indirect(offs_sb[:, g * PAIR // 16 : (g + 1) * PAIR // 16])
-            )
-        for cols in (slice(0, PAIR), slice(PAIR, S)):
-            nc.scalar.dma_start(gs1[0:100, cols].bitcast(I32), gs[4:104, cols].bitcast(I32))
+            nc.vector.tensor_copy(gs[:, g * PAIR : (g + 1) * PAIR], dys[:].indirect(pair_offsets(g)))
+        nc.gpsimd.dma_start(gs1[0:100, :].bitcast(I32), gs[4:104, :].bitcast(I32))
         for g in range(E // 2):
             for o in range(PASSES):
-                nc.vector.tensor_copy(
-                    gw[o][g][:], dyw[o][:].bitcast(U32).indirect(offs_sb[:, g * PAIR // 16 : (g + 1) * PAIR // 16])
-                )
+                gather_words(o, g)
         g_scales = (gs, gs1)
 
-        dh_rows, dh_cols, relu, live, masked, da, codes = {}, {}, {}, {}, {}, {}, {}
+        dh_rows, dh_cols, mask, da, words, scales = {}, {}, {}, {}, {}, {}
 
-        def first_product(e):
-            for j in (2 * e, 2 * e + 1):
-                acc = psum.tile([P, H], F32, name="acc1", tag="first", bufs=2)
-                for o in range(PASSES):
-                    nc.tensor.matmul_mx(
-                        out=acc[:],
-                        lhsT=gw[o][e // 2][:, (j % 4) * P : (j % 4 + 1) * P].bitcast(FP8X4),
-                        lhsT_scale=g_scales[o][:, j * P : (j + 1) * P],
-                        rhs=w2[e // 2][:, (e % 2) * PASSES + o, :].bitcast(FP4X4),
-                        rhs_scale=w2s[:, e * PASSES + o, :],
-                        start=(o == 0),
-                        stop=(o == PASSES - 1),
-                    )
-                dh_rows[j] = ring.tile([P, PACK, P], F32, name="dh_rows", tag="dh_rows", bufs=TILES, align_bytes=64)
-                nc.scalar.activation(
-                    dh_rows[j][:], acc[:].rearrange("s (m t) -> s t m", t=PACK), ACT.Copy, scale=gate_col[:, j : j + 1]
+        def first_product(j):
+            e = j // 2
+            acc = psum.tile([P, H], F32, name="acc1", tag="first", bufs=2)
+            for o in range(PASSES):
+                nc.tensor.matmul_mx(
+                    out=acc[:],
+                    lhsT=gw[o][e // 2][:, (j % 4) * P : (j % 4 + 1) * P].bitcast(FP8X4),
+                    lhsT_scale=g_scales[o][:, j * P : (j + 1) * P],
+                    rhs=w2[e // 2][:, (e % 2) * PASSES + o, :].bitcast(FP4X4),
+                    rhs_scale=w2s[:, e * PASSES + o, :],
+                    start=(o == 0),
+                    stop=(o == PASSES - 1),
                 )
+            dh_rows[j] = ring.tile([P, PACK, P], F32, name="dh_rows", tag="dh_rows", bufs=8, align_bytes=64)
+            nc.scalar.activation(
+                dh_rows[j][:], acc[:].rearrange("s (m t) -> s t m", t=PACK), ACT.Copy, scale=gate_col[:, j : j + 1]
+            )
+
+        def expert_of(tiles, e):
+            return tiles[e // 2][:, :, (e % 2) * C : (e % 2 + 1) * C]
+
+        def tile_of(tiles, j):
+            return tiles[j // 4][:, :, (j % 4) * P : (j % 4 + 1) * P]
 
         def rectify(e):
-            relu[e] = ring.tile([P, PACK, C], F32, name="relu", tag="relu", bufs=3, align_bytes=64)
-            nc.scalar.activation(relu[e][:], a1_of[e], ACT.Relu)
+            nc.scalar.activation(expert_of(a1_sb, e), expert_of(a1_sb, e), ACT.Relu)
+            mask[e] = ring.tile([P, PACK, C], BF16, name="mask", tag="mask", bufs=E, align_bytes=64)
+            nc.scalar.activation(mask[e][:], expert_of(a1_sb, e), ACT.Sign)
 
-        def turn(e):
-            for j in (2 * e, 2 * e + 1):
-                dh_cols[j] = psum.tile([P, PACK, P], F32, name="dh_cols", tag="turned", bufs=4)
-                for t in range(PACK):
-                    nc.tensor.transpose(dh_cols[j][:, t, :], dh_rows[j][:, t, :], ident[:])
+        def mask_a3(j):
+            nc.gpsimd.tensor_tensor(
+                tile_of(a3_sb, j), tile_of(a3_sb, j), mask[j // 2][:, :, (j % 2) * P : (j % 2 + 1) * P], ALU.mult
+            )
 
-        def half(view, j):
-            return view[:, :, (j % 2) * P : (j % 2 + 1) * P]
+        def turn(j):
+            dh_cols[j] = psum.tile([P, PACK, P], F32, name="dh_cols", tag="turned", bufs=4)
+            for t in range(PACK):
+                nc.tensor.transpose(dh_cols[j][:, t, :], dh_rows[j][:, t, :], ident[:])
 
         def in_runs(view):
             return view.rearrange("p t (c i) -> p c t i", i=RUN)
 
-        def mask(e):
-            live[e] = ring.tile([P, PACK, C], F32, name="live", tag="live", bufs=AHEAD, align_bytes=64)
-            nc.vector.scalar_tensor_tensor(live[e][:], a1_of[e], 0.0, a3_of[e], ALU.is_gt, ALU.mult)
+        group_of = {}
+        for j0, j1 in QUANT_GROUPS:
+            da[j0] = held([P, j1 - j0, 2, P * PACK], BF16, "da%d" % j0)
+            words[j0] = held([P, j1 - j0, 2, P], U32, "da_words%d" % j0)
+            scales[j0] = held([P, j1 - j0, 2, P], U8, "da_scales%d" % j0)
+            for j in range(j0, j1):
+                group_of[j] = j0
 
         def product(j, which):
-            if which == 0:
-                da[j] = ring.tile([P, 2, P * PACK], BF16, name="da", tag="da", bufs=4, align_bytes=64)
+            j0 = group_of[j]
             nc.vector.tensor_tensor(
-                da[j][:, which, :].rearrange("p (c i t) -> p c t i", i=RUN, t=PACK),
+                da[j0][:, j - j0, which, :].rearrange("p (c i t) -> p c t i", i=RUN, t=PACK),
                 in_runs(dh_cols[j][:]),
-                in_runs(half((live, relu)[which][j // 2][:], j)),
+                in_runs(tile_of((a3_sb, a1_sb)[which], j)),
                 ALU.mult,
             )
 
-        def masked_dh(j):
-            da[j] = ring.tile([P, 2, P * PACK], BF16, name="da", tag="da", bufs=4, align_bytes=64)
-            masked[j] = ring.tile([P, PACK, P], F32, name="masked", tag="masked", bufs=3, align_bytes=64)
-            nc.vector.scalar_tensor_tensor(
-                masked[j][:], half(a1_of[j // 2], j), 0.0, dh_cols[j][:], ALU.is_gt, ALU.mult
-            )
-
-        def times_a3(engine, run, j):
-            engine.tensor_tensor(
-                da[j][:, 0, :].rearrange("p (c i t) -> p c t i", i=run, t=PACK),
-                masked[j][:].rearrange("p t (c i) -> p c t i", i=run),
-                half(a3_of[j // 2], j).rearrange("p t (c i) -> p c t i", i=run),
-                ALU.mult,
-            )
-
-        def quantise(j):
-            words = ring.tile([P, 2 * P], U32, name="da_words", tag="da_words", bufs=8, align_bytes=64)
-            scales = ring.tile([P, 2 * P], U8, name="da_scales", tag="da_scales", bufs=8, align_bytes=64)
+        def quantise(j0):
             nc.vector.quantize_mx(
-                out=words[:].bitcast(FP8X4), scales=scales[:], in_=da[j][:].rearrange("p w n -> p (w n)")
+                out=words[j0][:].rearrange("p j w n -> p (j w n)").bitcast(FP8X4),
+                scales=scales[j0][:].rearrange("p j w n -> p (j w n)"),
+                in_=da[j0][:].rearrange("p j w n -> p (j w n)"),
             )
-            codes[j] = (words, scales)
 
-        def second_product(j, kt0, kt1):
-            e = j // 2
-            words, scales = codes[j]
-            acc = psum.tile([P, KT, P], F32, name="acc2", tag="second", bufs=2)
-            for kt in range(kt0, kt1):
+        def second_product(kt, j0, j1):
+            acc = psum.tile([P, j1 - j0, P], F32, name="acc2", tag="second", bufs=2)
+            for j in range(j0, j1):
+                e = j // 2
                 for which, (w, ws) in enumerate(((w1, w1s), (w3, w3s))):
                     nc.tensor.matmul_mx(
-                        out=acc[:, kt, :],
+                        out=acc[:, j - j0, :],
                         lhsT=w[e // 2][:, e % 2, 2 * P * kt : 2 * P * (kt + 1)].bitcast(FP4X4),
                         lhsT_scale=ws[:, e, P * kt : P * (kt + 1)],
-                        rhs=words[:, which * P : (which + 1) * P].bitcast(FP8X4),
-                        rhs_scale=scales[:, which * P : (which + 1) * P],
+                        rhs=words[group_of[j]][:, j - group_of[j], which, :].bitcast(FP8X4),
+                        rhs_scale=scales[group_of[j]][:, j - group_of[j], which, :],
                         start=(which == 0),
                         stop=(which == 1),
                     )
-            nc.scalar.copy(dx[:, kt0:kt1, j * P : (j + 1) * P], acc[:, kt0:kt1, :])
+            nc.scalar.copy(dx[kt][:, j0 * P : j1 * P], acc[:].rearrange("p j s -> p (j s)"))
 
-        first_product(0)
-        rectify(0)
-        turn(0)
-        first_product(1)
-        rectify(1)
-        for e in range(2, E):
-            first_product(e)
-        mask(0)
+        due = []
         for e in range(E):
-            lo, hi = 2 * e, 2 * e + 1
-            if e + 1 < E:
-                turn(e + 1)
-            if e < AHEAD:
-                product(lo, 0)
-                if e > 0:
-                    quantise(lo - 1)
-                product(lo, 1)
-                if e + 1 < AHEAD:
-                    mask(e + 1)
-                if e > 0:
-                    second_product(lo - 1, 0, KT)
-                product(hi, 0)
-                quantise(lo)
-                product(hi, 1)
-                if e + 1 == AHEAD:
-                    quantise(hi)
-            else:
-                masked_dh(lo)
-                times_a3(nc.gpsimd, POOL_RUN, lo)
-                product(lo, 1)
-                masked_dh(hi)
-                product(hi, 1)
-                if e + 1 < E:
-                    times_a3(nc.vector, RUN, hi)
-                    quantise(lo)
-                else:
-                    quantise(lo)
-                    times_a3(nc.vector, RUN, hi)
-                quantise(hi)
-            if e + 2 < E:
-                rectify(e + 2)
-            second_product(lo, 0, KT)
-            if AHEAD <= e + 1 < E:
-                second_product(hi, 0, KT)
-        second_product(TILES - 1, 0, 1)
-        second_product(TILES - 1, 1, KT)
+            tiles = (2 * e, 2 * e + 1)
+            rectify(e)
+            for j in tiles:
+                first_product(j)
+            for j in tiles:
+                mask_a3(j)
+                turn(j)
+            for j in tiles:
+                product(j, 1)
+                for j0 in due:
+                    quantise(j0)
+                due = []
+                product(j, 0)
+                due = [j0 for j0, j1 in QUANT_GROUPS if j1 == j + 1]
+        quantise(TILES - 1)
+        for kt in range(KT):
+            for j0, j1 in (FIRST_BANK_GROUPS if kt == 0 else BANK_GROUPS):
+                second_product(kt, j0, j1)
 
-        pieces = [(kt, 0, T) for kt in range(KT - 1)] + [(KT - 1, 0, T // 2), (KT - 1, T // 2, T)]
+        pieces = [(kt, 0, T) for kt in range(KT - 1)] + [(KT - 1, 0, 512), (KT - 1, 512, T)]
         for kt, t0, t1 in pieces:
             first = ring.tile([P, t1 - t0], F32, name="first", tag="first", bufs=2, align_bytes=64)
-            second = ring.tile([P, t1 - t0], F32, name="second", tag="second", bufs=2, align_bytes=64)
             total = ring.tile([P, t1 - t0], F32, name="total", tag="total", bufs=3, align_bytes=64)
-            nc.vector.tensor_copy(first[:], dx[:, kt, :].indirect(pos1_sb[:, t0 // 16 : t1 // 16]))
-            nc.vector.tensor_copy(second[:], dx[:, kt, :].indirect(pos2_sb[:, t0 // 16 : t1 // 16]))
-            adder = nc.vector if (kt, t1) == (KT - 1, T) else nc.gpsimd
-            adder.tensor_tensor(total[:], first[:], second[:], ALU.add)
+            nc.vector.tensor_copy(first[:], dx[kt][:].indirect(pos1_sb[:, t0 // 16 : t1 // 16]))
+            if (kt, t1) == (KT - 1, T):
+                nc.vector.tensor_tensor(total[:], dx[kt][:].indirect(pos2_sb[:, t0 // 16 : t1 // 16]), first[:], ALU.add)
+            else:
+                second = ring.tile([P, t1 - t0], F32, name="second", tag="second", bufs=2, align_bytes=64)
+                nc.vector.tensor_copy(second[:], dx[kt][:].indirect(pos2_sb[:, t0 // 16 : t1 // 16]))
+                nc.gpsimd.tensor_tensor(total[:], first[:], second[:], ALU.add)
             nc.sync.dma_start(out[kt * P : (kt + 1) * P, t0:t1], total[:])

@@ -68,9 +68,9 @@ def tile_moe_bdx_glu_relu_kernel(
 
         nc.gpsimd.memset(dys[:].bitcast(I32), 0)
         nc.vector.memset(w2s[:].rearrange("p a n -> p (a n)").bitcast(I32), 0)
-        nc.gpsimd.memset(gate_rows[:], 0.0)
         nc.vector.memset(gs1[:].bitcast(I32), 0)
         make_identity(nc, ident[:])
+        nc.scalar.activation(gate_rows[:], ident[:], ACT.Copy, scale=0.0)
         nc.gpsimd.memset(w1s[:].rearrange("p a n -> p (a n)").bitcast(I32), 0)
         nc.gpsimd.memset(w3s[:].rearrange("p a n -> p (a n)").bitcast(I32), 0)
 
@@ -119,7 +119,7 @@ def tile_moe_bdx_glu_relu_kernel(
 
         for g in range(E // 2):
             nc.vector.tensor_copy(gs[:, g * PAIR : (g + 1) * PAIR], dys[:].indirect(pair_offsets(g)))
-        nc.gpsimd.dma_start(gs1[0:100, :].bitcast(I32), gs[4:104, :].bitcast(I32))
+        nc.scalar.dma_start(gs1[0:100, :].bitcast(I32), gs[4:104, :].bitcast(I32))
         for g in range(E // 2):
             for o in range(PASSES):
                 gather_words(o, g)
@@ -235,10 +235,5 @@ def tile_moe_bdx_glu_relu_kernel(
             first = ring.tile([P, t1 - t0], F32, name="first", tag="first", bufs=2, align_bytes=64)
             total = ring.tile([P, t1 - t0], F32, name="total", tag="total", bufs=3, align_bytes=64)
             nc.vector.tensor_copy(first[:], dx[kt][:].indirect(pos1_sb[:, t0 // 16 : t1 // 16]))
-            if (kt, t1) == (KT - 1, T):
-                nc.vector.tensor_tensor(total[:], dx[kt][:].indirect(pos2_sb[:, t0 // 16 : t1 // 16]), first[:], ALU.add)
-            else:
-                second = ring.tile([P, t1 - t0], F32, name="second", tag="second", bufs=2, align_bytes=64)
-                nc.vector.tensor_copy(second[:], dx[kt][:].indirect(pos2_sb[:, t0 // 16 : t1 // 16]))
-                nc.gpsimd.tensor_tensor(total[:], first[:], second[:], ALU.add)
+            nc.vector.tensor_tensor(total[:], dx[kt][:].indirect(pos2_sb[:, t0 // 16 : t1 // 16]), first[:], ALU.add)
             nc.sync.dma_start(out[kt * P : (kt + 1) * P, t0:t1], total[:])

@@ -29,7 +29,7 @@ PAIR = 2 * C
 RUN = 4
 QUANT_GROUPS = ((0, 4), (4, 8), (8, 10), (10, 11), (11, 12))
 BANK_GROUPS = ((0, 4), (4, 8), (8, 12))
-FIRST_BANK_GROUPS = ((0, 4), (4, 8), (8, 11), (11, 12))
+FIRST_BANK_GROUPS = ((0, 4), (4, 8), (8, 10), (10, 12))
 
 
 def tile_moe_bdx_glu_relu_kernel(
@@ -48,11 +48,10 @@ def tile_moe_bdx_glu_relu_kernel(
         offs_sb = keep.tile([P, S // 16], U16, name="offs_sb")
         pos1_sb = keep.tile([P, T // 16], U16, name="pos1_sb")
         pos2_sb = keep.tile([P, T // 16], U16, name="pos2_sb")
-        dyw = [held([P, T], I32, "dyw%d" % o) for o in range(PASSES)]
+        dyw = held([P, PASSES, T], I32, "dyw")
         dys = held([P, T], U8, "dys")
         gw = [[held([P, PAIR], U32, "gw%d_%d" % (o, g)) for g in range(E // 2)] for o in range(PASSES)]
-        gs = held([P, S], U8, "gs")
-        gs1 = held([P, S], U8, "gs1")
+        gs = [[held([P, cols], U8, "gs%d_%d" % (o, cols)) for cols in (PAIR, S - PAIR)] for o in range(PASSES)]
         w2 = [held([P, 2 * PASSES, 2 * H], U8, "w2_%d" % g) for g in range(E // 2)]
         w1 = [held([P, 2, 2 * K], U8, "w1_%d" % g) for g in range(E // 2)]
         w3 = [held([P, 2, 2 * K], U8, "w3_%d" % g) for g in range(E // 2)]
@@ -68,10 +67,11 @@ def tile_moe_bdx_glu_relu_kernel(
 
         nc.gpsimd.memset(dys[:].bitcast(I32), 0)
         nc.vector.memset(w2s[:].rearrange("p a n -> p (a n)").bitcast(I32), 0)
-        nc.vector.memset(gs1[:].bitcast(I32), 0)
-        make_identity(nc, ident[:])
-        nc.scalar.activation(gate_rows[:], ident[:], ACT.Copy, scale=0.0)
+        for plane in gs[1]:
+            nc.vector.memset(plane[:].bitcast(I32), 0)
+        nc.gpsimd.memset(gate_rows[:], 0.0)
         nc.gpsimd.memset(w1s[:].rearrange("p a n -> p (a n)").bitcast(I32), 0)
+        make_identity(nc, ident[:])
         nc.gpsimd.memset(w3s[:].rearrange("p a n -> p (a n)").bitcast(I32), 0)
 
         def load_scale_rows(plane, scales):
@@ -90,13 +90,26 @@ def tile_moe_bdx_glu_relu_kernel(
             nc.sync.dma_start(
                 dys[32 * q : 32 * q + 4 * PASSES, :].bitcast(I32), dy_scales[:, 4 * q : 4 * q + 4, :].bitcast(I32)
             )
-        for o in range(PASSES):
-            nc.sync.dma_start(dyw[o][:], dy_words[o].rearrange("p t d -> p (t d)").bitcast(I32))
-        nc.scalar.dma_start(gate_rows[0:TILES, :], gate[0].rearrange("(j s) -> j s", s=P))
-        for g in range(E // 2):
+        nc.sync.dma_start(dyw[:], dy_words.rearrange("o p t d -> p o (t d)").bitcast(I32))
+        load_saved(a1_sb, a1, 0)
+        nc.sync.dma_start(gate_rows[0:TILES, :], gate[0].rearrange("(j s) -> j s", s=P))
+        load_scale_rows(w2s, w2_scales)
+        load_words(w2, w2_words, 0)
+
+        def pair_offsets(g):
+            return offs_sb[:, g * PAIR // 16 : (g + 1) * PAIR // 16]
+
+        def move_second_pass(part):
+            nc.sync.dma_start(gs[1][part][0:100, :].bitcast(I32), gs[0][part][4:104, :].bitcast(I32))
+
+        nc.vector.tensor_copy(gs[0][0][:], dys[:].indirect(pair_offsets(0)))
+        move_second_pass(0)
+        load_saved(a3_sb, a3, 0)
+        for g in range(1, E // 2):
+            nc.vector.tensor_copy(gs[0][1][:, (g - 1) * PAIR : g * PAIR], dys[:].indirect(pair_offsets(g)))
+        move_second_pass(1)
+        for g in range(1, E // 2):
             load_saved(a1_sb, a1, g)
-            if g == 0:
-                load_scale_rows(w2s, w2_scales)
             load_words(w2, w2_words, g)
             load_saved(a3_sb, a3, g)
         load_scale_rows(w1s, w1_scales)
@@ -107,40 +120,35 @@ def tile_moe_bdx_glu_relu_kernel(
         nc.sync.dma_start(pos1_sb[:], pos1)
         nc.sync.dma_start(pos2_sb[:], pos2)
 
+        for g in range(E // 2):
+            for o in range(PASSES):
+                nc.vector.tensor_copy(gw[o][g][:], dyw[:, o, :].bitcast(U32).indirect(pair_offsets(g)))
+
         gate_ps = psum.tile([P, PACK, P], F32, name="gate_ps", tag="turned", bufs=4)
         nc.tensor.transpose(gate_ps[:, 0, :], gate_rows[:], ident[:])
         nc.scalar.copy(gate_col[:], gate_ps[:, 0, 0:TILES])
 
-        def pair_offsets(g):
-            return offs_sb[:, g * PAIR // 16 : (g + 1) * PAIR // 16]
+        def gathered_scales(o, j):
+            if j < 4:
+                return gs[o][0][:, j * P : (j + 1) * P]
+            return gs[o][1][:, (j - 4) * P : (j - 3) * P]
 
-        def gather_words(o, g):
-            nc.vector.tensor_copy(gw[o][g][:], dyw[o][:].bitcast(U32).indirect(pair_offsets(g)))
-
-        for g in range(E // 2):
-            nc.vector.tensor_copy(gs[:, g * PAIR : (g + 1) * PAIR], dys[:].indirect(pair_offsets(g)))
-        nc.scalar.dma_start(gs1[0:100, :].bitcast(I32), gs[4:104, :].bitcast(I32))
-        for g in range(E // 2):
-            for o in range(PASSES):
-                gather_words(o, g)
-        g_scales = (gs, gs1)
-
-        dh_rows, dh_cols, mask, da, words, scales = {}, {}, {}, {}, {}, {}
+        dh_rows, dh_cols, relu, mask, live, da, words, scales = {}, {}, {}, {}, {}, {}, {}, {}
 
         def first_product(j):
             e = j // 2
-            acc = psum.tile([P, H], F32, name="acc1", tag="first", bufs=2)
+            acc = psum.tile([P, H], F32, name="acc1", tag="sums", bufs=4)
             for o in range(PASSES):
                 nc.tensor.matmul_mx(
                     out=acc[:],
                     lhsT=gw[o][e // 2][:, (j % 4) * P : (j % 4 + 1) * P].bitcast(FP8X4),
-                    lhsT_scale=g_scales[o][:, j * P : (j + 1) * P],
+                    lhsT_scale=gathered_scales(o, j),
                     rhs=w2[e // 2][:, (e % 2) * PASSES + o, :].bitcast(FP4X4),
                     rhs_scale=w2s[:, e * PASSES + o, :],
                     start=(o == 0),
                     stop=(o == PASSES - 1),
                 )
-            dh_rows[j] = ring.tile([P, PACK, P], F32, name="dh_rows", tag="dh_rows", bufs=8, align_bytes=64)
+            dh_rows[j] = ring.tile([P, PACK, P], F32, name="dh_rows", tag="dh_rows", bufs=6, align_bytes=64)
             nc.scalar.activation(
                 dh_rows[j][:], acc[:].rearrange("s (m t) -> s t m", t=PACK), ACT.Copy, scale=gate_col[:, j : j + 1]
             )
@@ -151,15 +159,18 @@ def tile_moe_bdx_glu_relu_kernel(
         def tile_of(tiles, j):
             return tiles[j // 4][:, :, (j % 4) * P : (j % 4 + 1) * P]
 
+        def half(view, j):
+            return view[:, :, (j % 2) * P : (j % 2 + 1) * P]
+
         def rectify(e):
-            nc.scalar.activation(expert_of(a1_sb, e), expert_of(a1_sb, e), ACT.Relu)
-            mask[e] = ring.tile([P, PACK, C], BF16, name="mask", tag="mask", bufs=E, align_bytes=64)
-            nc.scalar.activation(mask[e][:], expert_of(a1_sb, e), ACT.Sign)
+            relu[e] = ring.tile([P, PACK, C], F32, name="relu", tag="relu", bufs=3, align_bytes=64)
+            nc.scalar.activation(relu[e][:], expert_of(a1_sb, e), ACT.Relu)
+            mask[e] = ring.tile([P, PACK, C], BF16, name="mask", tag="mask", bufs=3, align_bytes=64)
+            nc.scalar.activation(mask[e][:], relu[e][:], ACT.Sign)
 
         def mask_a3(j):
-            nc.gpsimd.tensor_tensor(
-                tile_of(a3_sb, j), tile_of(a3_sb, j), mask[j // 2][:, :, (j % 2) * P : (j % 2 + 1) * P], ALU.mult
-            )
+            live[j] = ring.tile([P, PACK, P], F32, name="live", tag="live", bufs=6, align_bytes=64)
+            nc.gpsimd.tensor_tensor(live[j][:], tile_of(a3_sb, j), half(mask[j // 2][:], j), ALU.mult)
 
         def turn(j):
             dh_cols[j] = psum.tile([P, PACK, P], F32, name="dh_cols", tag="turned", bufs=4)
@@ -182,7 +193,7 @@ def tile_moe_bdx_glu_relu_kernel(
             nc.vector.tensor_tensor(
                 da[j0][:, j - j0, which, :].rearrange("p (c i t) -> p c t i", i=RUN, t=PACK),
                 in_runs(dh_cols[j][:]),
-                in_runs(tile_of((a3_sb, a1_sb)[which], j)),
+                in_runs(half(relu[j // 2][:], j) if which else live[j][:]),
                 ALU.mult,
             )
 
@@ -194,7 +205,7 @@ def tile_moe_bdx_glu_relu_kernel(
             )
 
         def second_product(kt, j0, j1):
-            acc = psum.tile([P, j1 - j0, P], F32, name="acc2", tag="second", bufs=2)
+            acc = psum.tile([P, j1 - j0, P], F32, name="acc2", tag="sums", bufs=4)
             for j in range(j0, j1):
                 e = j // 2
                 for which, (w, ws) in enumerate(((w1, w1s), (w3, w3s))):
@@ -224,16 +235,22 @@ def tile_moe_bdx_glu_relu_kernel(
                     quantise(j0)
                 due = []
                 product(j, 0)
-                due = [j0 for j0, j1 in QUANT_GROUPS if j1 == j + 1]
+                due = [j0 for j0, j1 in QUANT_GROUPS if j1 == j + 1 and j0 < TILES - 2]
+        quantise(TILES - 2)
         quantise(TILES - 1)
         for kt in range(KT):
             for j0, j1 in (FIRST_BANK_GROUPS if kt == 0 else BANK_GROUPS):
                 second_product(kt, j0, j1)
 
-        pieces = [(kt, 0, T) for kt in range(KT - 1)] + [(KT - 1, 0, 512), (KT - 1, 512, T)]
-        for kt, t0, t1 in pieces:
-            first = ring.tile([P, t1 - t0], F32, name="first", tag="first", bufs=2, align_bytes=64)
-            total = ring.tile([P, t1 - t0], F32, name="total", tag="total", bufs=3, align_bytes=64)
-            nc.vector.tensor_copy(first[:], dx[kt][:].indirect(pos1_sb[:, t0 // 16 : t1 // 16]))
-            nc.vector.tensor_tensor(total[:], dx[kt][:].indirect(pos2_sb[:, t0 // 16 : t1 // 16]), first[:], ALU.add)
-            nc.sync.dma_start(out[kt * P : (kt + 1) * P, t0:t1], total[:])
+        for kt in range(KT):
+            halves = (slice(0, T // 2), slice(T // 2, T))
+            first = {}
+            for h, cols in enumerate(halves):
+                first[h] = ring.tile([P, T // 2], F32, name="first", tag="first", bufs=4, align_bytes=64)
+                nc.vector.tensor_copy(first[h][:], dx[kt][:].indirect(pos1_sb[:, cols.start // 16 : cols.stop // 16]))
+            for h, cols in enumerate(halves):
+                total = ring.tile([P, T // 2], F32, name="total", tag="total", bufs=4, align_bytes=64)
+                nc.vector.tensor_tensor(
+                    total[:], dx[kt][:].indirect(pos2_sb[:, cols.start // 16 : cols.stop // 16]), first[h][:], ALU.add
+                )
+                nc.sync.dma_start(out[kt * P : (kt + 1) * P, cols], total[:])

@@ -26,9 +26,11 @@ PASSES = N // (P * PACK)
 TILES = S // P
 KT = K // P
 PAIR = 2 * C
-RUN = 4
-QUANT_GROUPS = ((0, 4), (4, 8), (8, 10), (10, 11), (11, 12))
+RUN = 2
+POOL_EXPERTS = 4
+QUANT_GROUPS = ((1, 0, 8), (0, 0, 8), (1, 8, 12), (0, 8, 10), (0, 10, 11), (0, 11, 12))
 BANK_GROUPS = ((0, 4), (4, 8), (8, 12))
+K_PARTS = ((0, P), (P, K))
 FIRST_BANK_GROUPS = ((0, 4), (4, 8), (8, 10), (10, 12))
 
 
@@ -53,26 +55,27 @@ def tile_moe_bdx_glu_relu_kernel(
         gw = [[held([P, PAIR], U32, "gw%d_%d" % (o, g)) for g in range(E // 2)] for o in range(PASSES)]
         gs = [[held([P, cols], U8, "gs%d_%d" % (o, cols)) for cols in (PAIR, S - PAIR)] for o in range(PASSES)]
         w2 = [held([P, 2 * PASSES, 2 * H], U8, "w2_%d" % g) for g in range(E // 2)]
-        w1 = [held([P, 2, 2 * K], U8, "w1_%d" % g) for g in range(E // 2)]
-        w3 = [held([P, 2, 2 * K], U8, "w3_%d" % g) for g in range(E // 2)]
+        w1 = [held([P, E, 2 * (k1 - k0)], U8, "w1_%d" % k0) for k0, k1 in K_PARTS]
+        w3 = [held([P, E, 2 * (k1 - k0)], U8, "w3_%d" % k0) for k0, k1 in K_PARTS]
         w2s = held([P, E * PASSES, H], U8, "w2s")
-        w1s = held([P, E, K], U8, "w1s")
-        w3s = held([P, E, K], U8, "w3s")
+        w1s = [held([P, E, k1 - k0], U8, "w1s_%d" % k0) for k0, k1 in K_PARTS]
+        w3s = [held([P, E, k1 - k0], U8, "w3s_%d" % k0) for k0, k1 in K_PARTS]
         a1_sb = [held([P, PACK, PAIR], F32, "a1_%d" % g) for g in range(E // 2)]
-        a3_sb = [held([P, PACK, PAIR], F32, "a3_%d" % g) for g in range(E // 2)]
+        a3_sb = [held([P, PACK, PAIR], F32, "a3_%d" % g) for g in range(POOL_EXPERTS // 2)]
+        a3_late = [held([P, PACK, C], F32, "a3_late%d" % e) for e in range(POOL_EXPERTS, E)]
         dx = [held([P, S], F32, "dx%d" % kt) for kt in range(KT)]
         gate_rows = held([P, P], F32, "gate_rows")
         gate_col = held([P, TILES], F32, "gate_col")
         ident = held([P, P], F32, "ident")
 
         nc.gpsimd.memset(dys[:].bitcast(I32), 0)
+        nc.gpsimd.memset(gate_rows[:], 0.0)
         nc.vector.memset(w2s[:].rearrange("p a n -> p (a n)").bitcast(I32), 0)
         for plane in gs[1]:
             nc.vector.memset(plane[:].bitcast(I32), 0)
-        nc.gpsimd.memset(gate_rows[:], 0.0)
-        nc.gpsimd.memset(w1s[:].rearrange("p a n -> p (a n)").bitcast(I32), 0)
         make_identity(nc, ident[:])
-        nc.gpsimd.memset(w3s[:].rearrange("p a n -> p (a n)").bitcast(I32), 0)
+        for plane in w1s + w3s:
+            nc.gpsimd.memset(plane[:].rearrange("p a n -> p (a n)").bitcast(I32), 0)
 
         def load_scale_rows(plane, scales):
             rows = scales.rearrange("e s f n -> f (e s) n").bitcast(I32)
@@ -82,16 +85,18 @@ def tile_moe_bdx_glu_relu_kernel(
         def load_words(tile, words, g):
             nc.sync.dma_start(tile[g][:].bitcast(I32), words[2 * g : 2 * g + 2].rearrange("e s p n -> p (e s) n").bitcast(I32))
 
-        def load_saved(tile, saved, g):
-            nc.sync.dma_start(tile[g][:], saved.rearrange("(p t) s -> p t s", t=PACK)[:, :, g * PAIR : (g + 1) * PAIR])
+        def load_saved(tiles, saved, n, first=0):
+            cols = tiles[n].shape[2]
+            rows = saved.rearrange("(p t) s -> p t s", t=PACK)
+            nc.sync.dma_start(tiles[n][:], rows[:, :, first + n * cols : first + (n + 1) * cols])
 
         nc.sync.dma_start(offs_sb[:], offs)
         for q in range(4):
             nc.sync.dma_start(
                 dys[32 * q : 32 * q + 4 * PASSES, :].bitcast(I32), dy_scales[:, 4 * q : 4 * q + 4, :].bitcast(I32)
             )
-        nc.sync.dma_start(dyw[:], dy_words.rearrange("o p t d -> p o (t d)").bitcast(I32))
         load_saved(a1_sb, a1, 0)
+        nc.sync.dma_start(dyw[:], dy_words.rearrange("o p t d -> p o (t d)").bitcast(I32))
         nc.sync.dma_start(gate_rows[0:TILES, :], gate[0].rearrange("(j s) -> j s", s=P))
         load_scale_rows(w2s, w2_scales)
         load_words(w2, w2_words, 0)
@@ -108,17 +113,34 @@ def tile_moe_bdx_glu_relu_kernel(
         for g in range(1, E // 2):
             nc.vector.tensor_copy(gs[0][1][:, (g - 1) * PAIR : g * PAIR], dys[:].indirect(pair_offsets(g)))
         move_second_pass(1)
-        for g in range(1, E // 2):
-            load_saved(a1_sb, a1, g)
-            load_words(w2, w2_words, g)
-            load_saved(a3_sb, a3, g)
-        load_scale_rows(w1s, w1_scales)
-        load_scale_rows(w3s, w3_scales)
-        for g in range(E // 2):
-            load_words(w1, w1_words, g)
-            load_words(w3, w3_words, g)
+
+        def load_part_words(tile, packed, h):
+            k0, k1 = K_PARTS[h]
+            nc.sync.dma_start(
+                tile[h][:].bitcast(I32), packed[:, 0, :, 2 * k0 : 2 * k1].rearrange("e p n -> p e n").bitcast(I32)
+            )
+
+        def load_part_scales(plane, rows, h):
+            k0, k1 = K_PARTS[h]
+            load_scale_rows(plane[h], rows[:, :, :, k0:k1])
+
+        load_saved(a1_sb, a1, 1)
         nc.sync.dma_start(pos1_sb[:], pos1)
         nc.sync.dma_start(pos2_sb[:], pos2)
+        load_words(w2, w2_words, 1)
+        load_saved(a3_sb, a3, 1)
+        load_part_scales(w1s, w1_scales, 0)
+        load_saved(a1_sb, a1, 2)
+        load_words(w2, w2_words, 2)
+        load_saved(a3_late, a3, 0, POOL_EXPERTS * C)
+        load_part_scales(w3s, w3_scales, 0)
+        load_part_words(w1, w1_words, 0)
+        load_part_words(w3, w3_words, 0)
+        load_saved(a3_late, a3, 1, POOL_EXPERTS * C)
+        load_part_words(w1, w1_words, 1)
+        load_part_words(w3, w3_words, 1)
+        load_part_scales(w1s, w1_scales, 1)
+        load_part_scales(w3s, w3_scales, 1)
 
         for g in range(E // 2):
             for o in range(PASSES):
@@ -148,7 +170,7 @@ def tile_moe_bdx_glu_relu_kernel(
                     start=(o == 0),
                     stop=(o == PASSES - 1),
                 )
-            dh_rows[j] = ring.tile([P, PACK, P], F32, name="dh_rows", tag="dh_rows", bufs=6, align_bytes=64)
+            dh_rows[j] = ring.tile([P, PACK, P], F32, name="dh_rows", tag="rows", bufs=8, align_bytes=64)
             nc.scalar.activation(
                 dh_rows[j][:], acc[:].rearrange("s (m t) -> s t m", t=PACK), ACT.Copy, scale=gate_col[:, j : j + 1]
             )
@@ -162,82 +184,112 @@ def tile_moe_bdx_glu_relu_kernel(
         def half(view, j):
             return view[:, :, (j % 2) * P : (j % 2 + 1) * P]
 
+        def in_runs(view):
+            return view.rearrange("p t (c i) -> p c t i", i=RUN)
+
         def rectify(e):
-            relu[e] = ring.tile([P, PACK, C], F32, name="relu", tag="relu", bufs=3, align_bytes=64)
-            nc.scalar.activation(relu[e][:], expert_of(a1_sb, e), ACT.Relu)
-            mask[e] = ring.tile([P, PACK, C], BF16, name="mask", tag="mask", bufs=3, align_bytes=64)
-            nc.scalar.activation(mask[e][:], relu[e][:], ACT.Sign)
+            relu[e] = ring.tile([P, PACK, C], F32, name="relu", tag="relu", bufs=4, align_bytes=64)[:]
+            nc.scalar.activation(relu[e], expert_of(a1_sb, e), ACT.Relu)
+            mask[e] = ring.tile([P, PACK, C], BF16, name="mask", tag="mask", bufs=4, align_bytes=64)
+            if e < POOL_EXPERTS:
+                nc.scalar.activation(mask[e][:], relu[e], ACT.Sign)
+            else:
+                woven = mask[e][:].rearrange("p t s -> p (t s)").rearrange("p (c i t) -> p c t i", i=RUN, t=PACK)
+                nc.scalar.activation(woven, in_runs(relu[e]), ACT.Sign)
 
         def mask_a3(j):
-            live[j] = ring.tile([P, PACK, P], F32, name="live", tag="live", bufs=6, align_bytes=64)
-            nc.gpsimd.tensor_tensor(live[j][:], tile_of(a3_sb, j), half(mask[j // 2][:], j), ALU.mult)
+            live[j] = ring.tile([P, PACK, P], F32, name="live", tag="live", bufs=6, align_bytes=64)[:]
+            nc.gpsimd.tensor_tensor(live[j], tile_of(a3_sb, j), half(mask[j // 2][:], j), ALU.mult)
 
         def turn(j):
             dh_cols[j] = psum.tile([P, PACK, P], F32, name="dh_cols", tag="turned", bufs=4)
             for t in range(PACK):
                 nc.tensor.transpose(dh_cols[j][:, t, :], dh_rows[j][:, t, :], ident[:])
 
-        def in_runs(view):
-            return view.rearrange("p t (c i) -> p c t i", i=RUN)
-
-        group_of = {}
-        for j0, j1 in QUANT_GROUPS:
-            da[j0] = held([P, j1 - j0, 2, P * PACK], BF16, "da%d" % j0)
-            words[j0] = held([P, j1 - j0, 2, P], U32, "da_words%d" % j0)
-            scales[j0] = held([P, j1 - j0, 2, P], U8, "da_scales%d" % j0)
+        place = {}
+        for group in QUANT_GROUPS:
+            which, j0, j1 = group
+            da[group] = held([P, j1 - j0, P * PACK], BF16, "da%d_%d" % (which, j0))
+            words[group] = held([P, j1 - j0, P], U32, "da_words%d_%d" % (which, j0))
+            scales[group] = held([P, j1 - j0, P], U8, "da_scales%d_%d" % (which, j0))
             for j in range(j0, j1):
-                group_of[j] = j0
+                place[j, which] = (group, j - j0)
+
+        def unit(tiles, j, which):
+            group, n = place[j, which]
+            return tiles[group][:, n, :]
 
         def product(j, which):
-            j0 = group_of[j]
             nc.vector.tensor_tensor(
-                da[j0][:, j - j0, which, :].rearrange("p (c i t) -> p c t i", i=RUN, t=PACK),
+                unit(da, j, which).rearrange("p (c i t) -> p c t i", i=RUN, t=PACK),
                 in_runs(dh_cols[j][:]),
-                in_runs(half(relu[j // 2][:], j) if which else live[j][:]),
+                in_runs(half(relu[j // 2], j) if which else live[j]),
                 ALU.mult,
             )
 
-        def quantise(j0):
+        def mask_da1(group):
+            which, j0, j1 = group
+            woven = mask[j0 // 2][:].rearrange("p t s -> p (t s)")
+            flat = da[group][:].rearrange("p j n -> p (j n)")
+            first = (j0 % 2) * P * PACK
+            nc.vector.tensor_tensor(flat, flat, woven[:, first : first + (j1 - j0) * P * PACK], ALU.mult)
+
+        def quantise(group):
             nc.vector.quantize_mx(
-                out=words[j0][:].rearrange("p j w n -> p (j w n)").bitcast(FP8X4),
-                scales=scales[j0][:].rearrange("p j w n -> p (j w n)"),
-                in_=da[j0][:].rearrange("p j w n -> p (j w n)"),
+                out=words[group][:].rearrange("p j n -> p (j n)").bitcast(FP8X4),
+                scales=scales[group][:].rearrange("p j n -> p (j n)"),
+                in_=da[group][:].rearrange("p j n -> p (j n)"),
             )
 
         def second_product(kt, j0, j1):
+            part = min(kt, 1)
+            k0 = kt * P - K_PARTS[part][0]
             acc = psum.tile([P, j1 - j0, P], F32, name="acc2", tag="sums", bufs=4)
             for j in range(j0, j1):
                 e = j // 2
                 for which, (w, ws) in enumerate(((w1, w1s), (w3, w3s))):
                     nc.tensor.matmul_mx(
                         out=acc[:, j - j0, :],
-                        lhsT=w[e // 2][:, e % 2, 2 * P * kt : 2 * P * (kt + 1)].bitcast(FP4X4),
-                        lhsT_scale=ws[:, e, P * kt : P * (kt + 1)],
-                        rhs=words[group_of[j]][:, j - group_of[j], which, :].bitcast(FP8X4),
-                        rhs_scale=scales[group_of[j]][:, j - group_of[j], which, :],
+                        lhsT=w[part][:, e, 2 * k0 : 2 * (k0 + P)].bitcast(FP4X4),
+                        lhsT_scale=ws[part][:, e, k0 : k0 + P],
+                        rhs=unit(words, j, which).bitcast(FP8X4),
+                        rhs_scale=unit(scales, j, which),
                         start=(which == 0),
                         stop=(which == 1),
                     )
             nc.scalar.copy(dx[kt][:, j0 * P : j1 * P], acc[:].rearrange("p j s -> p (j s)"))
 
-        due = []
         for e in range(E):
             tiles = (2 * e, 2 * e + 1)
             rectify(e)
             for j in tiles:
                 first_product(j)
             for j in tiles:
-                mask_a3(j)
+                if e < POOL_EXPERTS:
+                    mask_a3(j)
+                else:
+                    live[j] = half(a3_late[e - POOL_EXPERTS][:], j)
                 turn(j)
-            for j in tiles:
-                product(j, 1)
-                for j0 in due:
-                    quantise(j0)
-                due = []
-                product(j, 0)
-                due = [j0 for j0, j1 in QUANT_GROUPS if j1 == j + 1 and j0 < TILES - 2]
-        quantise(TILES - 2)
-        quantise(TILES - 1)
+            if e < POOL_EXPERTS:
+                for j in tiles:
+                    product(j, 1)
+                    product(j, 0)
+        pool_da3, pool_da1, late_da3, fifth_da1, tenth_da1, last_da1 = QUANT_GROUPS
+        quantise(pool_da3)
+        quantise(pool_da1)
+        for j in range(2 * POOL_EXPERTS, TILES):
+            product(j, 1)
+        for j in (8, 9):
+            product(j, 0)
+        quantise(late_da3)
+        mask_da1(fifth_da1)
+        product(10, 0)
+        quantise(fifth_da1)
+        product(11, 0)
+        mask_da1(tenth_da1)
+        mask_da1(last_da1)
+        quantise(tenth_da1)
+        quantise(last_da1)
         for kt in range(KT):
             for j0, j1 in (FIRST_BANK_GROUPS if kt == 0 else BANK_GROUPS):
                 second_product(kt, j0, j1)
@@ -246,10 +298,10 @@ def tile_moe_bdx_glu_relu_kernel(
             halves = (slice(0, T // 2), slice(T // 2, T))
             first = {}
             for h, cols in enumerate(halves):
-                first[h] = ring.tile([P, T // 2], F32, name="first", tag="first", bufs=4, align_bytes=64)
+                first[h] = ring.tile([P, T // 2], F32, name="first", tag="rows", bufs=8, align_bytes=64)
                 nc.vector.tensor_copy(first[h][:], dx[kt][:].indirect(pos1_sb[:, cols.start // 16 : cols.stop // 16]))
             for h, cols in enumerate(halves):
-                total = ring.tile([P, T // 2], F32, name="total", tag="total", bufs=4, align_bytes=64)
+                total = ring.tile([P, T // 2], F32, name="total", tag="rows", bufs=8, align_bytes=64)
                 nc.vector.tensor_tensor(
                     total[:], dx[kt][:].indirect(pos2_sb[:, cols.start // 16 : cols.stop // 16]), first[h][:], ALU.add
                 )

@@ -57,12 +57,9 @@ def tile_moe_bdx_glu_relu_kernel(
         w2 = [held([P, 2 * PASSES, 2 * H], U8, "w2_%d" % g) for g in range(E // 2)]
         w1 = [held([P, E, 2 * (k1 - k0)], U8, "w1_%d" % k0) for k0, k1 in K_PARTS]
         w3 = [held([P, E, 2 * (k1 - k0)], U8, "w3_%d" % k0) for k0, k1 in K_PARTS]
-        w2s = held([P, E * PASSES, H], U8, "w2s")
+        w2s = [held([P, 2 * PASSES, H], U8, "w2s_%d" % g) for g in range(E // 2)]
         w1s = [held([P, E, k1 - k0], U8, "w1s_%d" % k0) for k0, k1 in K_PARTS]
         w3s = [held([P, E, k1 - k0], U8, "w3s_%d" % k0) for k0, k1 in K_PARTS]
-        a1_sb = [held([P, PACK, PAIR], F32, "a1_%d" % g) for g in range(E // 2)]
-        a3_sb = [held([P, PACK, PAIR], F32, "a3_%d" % g) for g in range(POOL_EXPERTS // 2)]
-        a3_late = [held([P, PACK, C], F32, "a3_late%d" % e) for e in range(POOL_EXPERTS, E)]
         dx = [held([P, S], F32, "dx%d" % kt) for kt in range(KT)]
         gate_rows = held([P, P], F32, "gate_rows")
         gate_col = held([P, TILES], F32, "gate_col")
@@ -70,7 +67,8 @@ def tile_moe_bdx_glu_relu_kernel(
 
         nc.gpsimd.memset(dys[:].bitcast(I32), 0)
         nc.gpsimd.memset(gate_rows[:], 0.0)
-        nc.vector.memset(w2s[:].rearrange("p a n -> p (a n)").bitcast(I32), 0)
+        for plane in w2s:
+            nc.vector.memset(plane[:].rearrange("p a n -> p (a n)").bitcast(I32), 0)
         for plane in gs[1]:
             nc.vector.memset(plane[:].bitcast(I32), 0)
         make_identity(nc, ident[:])
@@ -85,21 +83,27 @@ def tile_moe_bdx_glu_relu_kernel(
         def load_words(tile, words, g):
             nc.sync.dma_start(tile[g][:].bitcast(I32), words[2 * g : 2 * g + 2].rearrange("e s p n -> p (e s) n").bitcast(I32))
 
-        def load_saved(tiles, saved, n, first=0):
-            cols = tiles[n].shape[2]
-            rows = saved.rearrange("(p t) s -> p t s", t=PACK)
-            nc.sync.dma_start(tiles[n][:], rows[:, :, first + n * cols : first + (n + 1) * cols])
+        a1_of, a3_of = {}, {}
+
+        def load_saved(views, saved, name, e0, e1):
+            tile = held([P, PACK, (e1 - e0) * C], F32, "%s_%d" % (name, e0))
+            nc.sync.dma_start(tile[:], saved.rearrange("(p t) s -> p t s", t=PACK)[:, :, e0 * C : e1 * C])
+            for e in range(e0, e1):
+                views[e] = tile[:, :, (e - e0) * C : (e - e0 + 1) * C]
+
+        def load_w2(g):
+            load_scale_rows(w2s[g], w2_scales[2 * g : 2 * g + 2])
+            load_words(w2, w2_words, g)
 
         nc.sync.dma_start(offs_sb[:], offs)
         for q in range(4):
             nc.sync.dma_start(
                 dys[32 * q : 32 * q + 4 * PASSES, :].bitcast(I32), dy_scales[:, 4 * q : 4 * q + 4, :].bitcast(I32)
             )
-        load_saved(a1_sb, a1, 0)
+        load_saved(a1_of, a1, "a1", 0, 2)
         nc.sync.dma_start(dyw[:], dy_words.rearrange("o p t d -> p o (t d)").bitcast(I32))
         nc.sync.dma_start(gate_rows[0:TILES, :], gate[0].rearrange("(j s) -> j s", s=P))
-        load_scale_rows(w2s, w2_scales)
-        load_words(w2, w2_words, 0)
+        load_w2(0)
 
         def pair_offsets(g):
             return offs_sb[:, g * PAIR // 16 : (g + 1) * PAIR // 16]
@@ -109,7 +113,7 @@ def tile_moe_bdx_glu_relu_kernel(
 
         nc.vector.tensor_copy(gs[0][0][:], dys[:].indirect(pair_offsets(0)))
         move_second_pass(0)
-        load_saved(a3_sb, a3, 0)
+        load_saved(a3_of, a3, "a3", 0, 2)
         for g in range(1, E // 2):
             nc.vector.tensor_copy(gs[0][1][:, (g - 1) * PAIR : g * PAIR], dys[:].indirect(pair_offsets(g)))
         move_second_pass(1)
@@ -124,19 +128,21 @@ def tile_moe_bdx_glu_relu_kernel(
             k0, k1 = K_PARTS[h]
             load_scale_rows(plane[h], rows[:, :, :, k0:k1])
 
-        load_saved(a1_sb, a1, 1)
+        load_saved(a1_of, a1, "a1", 2, 3)
         nc.sync.dma_start(pos1_sb[:], pos1)
         nc.sync.dma_start(pos2_sb[:], pos2)
-        load_words(w2, w2_words, 1)
-        load_saved(a3_sb, a3, 1)
+        load_w2(1)
+        load_saved(a3_of, a3, "a3", 2, 3)
+        load_saved(a1_of, a1, "a1", 3, 4)
+        load_saved(a3_of, a3, "a3", 3, 4)
         load_part_scales(w1s, w1_scales, 0)
-        load_saved(a1_sb, a1, 2)
-        load_words(w2, w2_words, 2)
-        load_saved(a3_late, a3, 0, POOL_EXPERTS * C)
+        load_w2(2)
+        load_saved(a1_of, a1, "a1", 4, 6)
+        load_saved(a3_of, a3, "a3", 4, 5)
         load_part_scales(w3s, w3_scales, 0)
         load_part_words(w1, w1_words, 0)
         load_part_words(w3, w3_words, 0)
-        load_saved(a3_late, a3, 1, POOL_EXPERTS * C)
+        load_saved(a3_of, a3, "a3", 5, 6)
         load_part_words(w1, w1_words, 1)
         load_part_words(w3, w3_words, 1)
         load_part_scales(w1s, w1_scales, 1)
@@ -166,7 +172,7 @@ def tile_moe_bdx_glu_relu_kernel(
                     lhsT=gw[o][e // 2][:, (j % 4) * P : (j % 4 + 1) * P].bitcast(FP8X4),
                     lhsT_scale=gathered_scales(o, j),
                     rhs=w2[e // 2][:, (e % 2) * PASSES + o, :].bitcast(FP4X4),
-                    rhs_scale=w2s[:, e * PASSES + o, :],
+                    rhs_scale=w2s[e // 2][:, (e % 2) * PASSES + o, :],
                     start=(o == 0),
                     stop=(o == PASSES - 1),
                 )
@@ -174,12 +180,6 @@ def tile_moe_bdx_glu_relu_kernel(
             nc.scalar.activation(
                 dh_rows[j][:], acc[:].rearrange("s (m t) -> s t m", t=PACK), ACT.Copy, scale=gate_col[:, j : j + 1]
             )
-
-        def expert_of(tiles, e):
-            return tiles[e // 2][:, :, (e % 2) * C : (e % 2 + 1) * C]
-
-        def tile_of(tiles, j):
-            return tiles[j // 4][:, :, (j % 4) * P : (j % 4 + 1) * P]
 
         def half(view, j):
             return view[:, :, (j % 2) * P : (j % 2 + 1) * P]
@@ -189,7 +189,9 @@ def tile_moe_bdx_glu_relu_kernel(
 
         def rectify(e):
             relu[e] = ring.tile([P, PACK, C], F32, name="relu", tag="relu", bufs=4, align_bytes=64)[:]
-            nc.scalar.activation(relu[e], expert_of(a1_sb, e), ACT.Relu)
+            nc.scalar.activation(relu[e], a1_of[e], ACT.Relu)
+
+        def make_mask(e):
             mask[e] = ring.tile([P, PACK, C], BF16, name="mask", tag="mask", bufs=4, align_bytes=64)
             if e < POOL_EXPERTS:
                 nc.scalar.activation(mask[e][:], relu[e], ACT.Sign)
@@ -199,7 +201,7 @@ def tile_moe_bdx_glu_relu_kernel(
 
         def mask_a3(j):
             live[j] = ring.tile([P, PACK, P], F32, name="live", tag="live", bufs=6, align_bytes=64)[:]
-            nc.gpsimd.tensor_tensor(live[j], tile_of(a3_sb, j), half(mask[j // 2][:], j), ALU.mult)
+            nc.gpsimd.tensor_tensor(live[j], half(a3_of[j // 2], j), half(mask[j // 2][:], j), ALU.mult)
 
         def turn(j):
             dh_cols[j] = psum.tile([P, PACK, P], F32, name="dh_cols", tag="turned", bufs=4)
@@ -247,33 +249,38 @@ def tile_moe_bdx_glu_relu_kernel(
             acc = psum.tile([P, j1 - j0, P], F32, name="acc2", tag="sums", bufs=4)
             for j in range(j0, j1):
                 e = j // 2
-                for which, (w, ws) in enumerate(((w1, w1s), (w3, w3s))):
+                for which, w, ws in ((1, w3, w3s), (0, w1, w1s)):
                     nc.tensor.matmul_mx(
                         out=acc[:, j - j0, :],
                         lhsT=w[part][:, e, 2 * k0 : 2 * (k0 + P)].bitcast(FP4X4),
                         lhsT_scale=ws[part][:, e, k0 : k0 + P],
                         rhs=unit(words, j, which).bitcast(FP8X4),
                         rhs_scale=unit(scales, j, which),
-                        start=(which == 0),
-                        stop=(which == 1),
+                        start=(which == 1),
+                        stop=(which == 0),
                     )
             nc.scalar.copy(dx[kt][:, j0 * P : j1 * P], acc[:].rearrange("p j s -> p (j s)"))
 
-        for e in range(E):
+        for e in range(POOL_EXPERTS):
             tiles = (2 * e, 2 * e + 1)
             rectify(e)
+            make_mask(e)
             for j in tiles:
                 first_product(j)
             for j in tiles:
-                if e < POOL_EXPERTS:
-                    mask_a3(j)
-                else:
-                    live[j] = half(a3_late[e - POOL_EXPERTS][:], j)
+                mask_a3(j)
                 turn(j)
-            if e < POOL_EXPERTS:
-                for j in tiles:
-                    product(j, 1)
-                    product(j, 0)
+            for j in tiles:
+                product(j, 1)
+                product(j, 0)
+        for j in range(2 * POOL_EXPERTS, TILES):
+            first_product(j)
+            turn(j)
+            live[j] = half(a3_of[j // 2], j)
+        for e in range(POOL_EXPERTS, E):
+            rectify(e)
+        for e in range(POOL_EXPERTS, E):
+            make_mask(e)
         pool_da3, pool_da1, late_da3, fifth_da1, tenth_da1, last_da1 = QUANT_GROUPS
         quantise(pool_da3)
         quantise(pool_da1)
@@ -295,13 +302,14 @@ def tile_moe_bdx_glu_relu_kernel(
                 second_product(kt, j0, j1)
 
         for kt in range(KT):
-            halves = (slice(0, T // 2), slice(T // 2, T))
+            cut = T // 2 if kt + 1 < KT else 2 * T // 3
+            halves = (slice(0, cut), slice(cut, T))
             first = {}
             for h, cols in enumerate(halves):
-                first[h] = ring.tile([P, T // 2], F32, name="first", tag="rows", bufs=8, align_bytes=64)
+                first[h] = ring.tile([P, cols.stop - cols.start], F32, name="first", tag="rows", bufs=8, align_bytes=64)
                 nc.vector.tensor_copy(first[h][:], dx[kt][:].indirect(pos1_sb[:, cols.start // 16 : cols.stop // 16]))
             for h, cols in enumerate(halves):
-                total = ring.tile([P, T // 2], F32, name="total", tag="rows", bufs=8, align_bytes=64)
+                total = ring.tile([P, cols.stop - cols.start], F32, name="total", tag="rows", bufs=8, align_bytes=64)
                 nc.vector.tensor_tensor(
                     total[:], dx[kt][:].indirect(pos2_sb[:, cols.start // 16 : cols.stop // 16]), first[h][:], ALU.add
                 )

@@ -22,16 +22,30 @@ ACT = mybir.ActivationFunctionType
 
 P = 128
 PACK = 4
+PER_COLUMN = 16
+QUADRANT = 32
 PASSES = N // (P * PACK)
 TILES = S // P
 KT = K // P
+PAIRS = E // 2
 PAIR = 2 * C
+MOVED_ROWS = 3 * QUADRANT + PACK
 RUN = 2
+
 POOL_EXPERTS = 4
-QUANT_GROUPS = ((1, 0, 8), (0, 0, 8), (1, 8, 12), (0, 8, 10), (0, 10, 11), (0, 11, 12))
+POOL_TILES = 2 * POOL_EXPERTS
+DA1, DA3 = 0, 1
+POOL_DA3 = (DA3, 0, POOL_TILES)
+POOL_DA1 = (DA1, 0, POOL_TILES)
+LATE_DA3 = (DA3, POOL_TILES, TILES)
+FIFTH_EXPERT_DA1 = (DA1, POOL_TILES, TILES - 2)
+NEXT_TO_LAST_DA1 = (DA1, TILES - 2, TILES - 1)
+LAST_DA1 = (DA1, TILES - 1, TILES)
+QUANT_GROUPS = (POOL_DA3, POOL_DA1, LATE_DA3, FIFTH_EXPERT_DA1, NEXT_TO_LAST_DA1, LAST_DA1)
 BANK_GROUPS = ((0, 4), (4, 8), (8, 12))
-K_PARTS = ((0, P), (P, K))
-FIRST_BANK_GROUPS = ((0, 4), (4, 8), (8, 10), (10, 12))
+FIRST_BANK_GROUPS = ((0, 4), (4, 8), (8, 10), (10, 11), (11, 12))
+WORD_PARTS = ((0, P), (P, K))
+SCALE_PARTS = ((0, K // 2), (K // 2, K))
 
 
 def tile_moe_bdx_glu_relu_kernel(
@@ -47,19 +61,25 @@ def tile_moe_bdx_glu_relu_kernel(
         def held(shape, dtype, name):
             return keep.tile(shape, dtype, name=name, align_bytes=64)
 
-        offs_sb = keep.tile([P, S // 16], U16, name="offs_sb")
-        pos1_sb = keep.tile([P, T // 16], U16, name="pos1_sb")
-        pos2_sb = keep.tile([P, T // 16], U16, name="pos2_sb")
+        def bank(shape, name, tag):
+            return psum.tile(shape, F32, name=name, tag=tag, bufs=4)
+
+        def row_tile(shape, name):
+            return ring.tile(shape, F32, name=name, tag="rows", bufs=8, align_bytes=64)
+
+        offs_sb = keep.tile([P, S // PER_COLUMN], U16, name="offs_sb")
+        pos1_sb = keep.tile([P, T // PER_COLUMN], U16, name="pos1_sb")
+        pos2_sb = keep.tile([P, T // PER_COLUMN], U16, name="pos2_sb")
         dyw = held([P, PASSES, T], I32, "dyw")
         dys = held([P, T], U8, "dys")
-        gw = [[held([P, PAIR], U32, "gw%d_%d" % (o, g)) for g in range(E // 2)] for o in range(PASSES)]
+        gw = [[held([P, PAIR], U32, "gw%d_%d" % (o, g)) for g in range(PAIRS)] for o in range(PASSES)]
         gs = [[held([P, cols], U8, "gs%d_%d" % (o, cols)) for cols in (PAIR, S - PAIR)] for o in range(PASSES)]
-        w2 = [held([P, 2 * PASSES, 2 * H], U8, "w2_%d" % g) for g in range(E // 2)]
-        w1 = [held([P, E, 2 * (k1 - k0)], U8, "w1_%d" % k0) for k0, k1 in K_PARTS]
-        w3 = [held([P, E, 2 * (k1 - k0)], U8, "w3_%d" % k0) for k0, k1 in K_PARTS]
-        w2s = [held([P, 2 * PASSES, H], U8, "w2s_%d" % g) for g in range(E // 2)]
-        w1s = [held([P, E, k1 - k0], U8, "w1s_%d" % k0) for k0, k1 in K_PARTS]
-        w3s = [held([P, E, k1 - k0], U8, "w3s_%d" % k0) for k0, k1 in K_PARTS]
+        w2 = [held([P, 2 * PASSES, 2 * H], U8, "w2_%d" % g) for g in range(PAIRS)]
+        w1 = [held([P, E, 2 * (k1 - k0)], U8, "w1_%d" % k0) for k0, k1 in WORD_PARTS]
+        w3 = [held([P, E, 2 * (k1 - k0)], U8, "w3_%d" % k0) for k0, k1 in WORD_PARTS]
+        w2s = [held([P, 2 * PASSES, H], U8, "w2s_%d" % g) for g in range(PAIRS)]
+        w1s = [held([P, E, k1 - k0], U8, "w1s_%d" % k0) for k0, k1 in SCALE_PARTS]
+        w3s = [held([P, E, k1 - k0], U8, "w3s_%d" % k0) for k0, k1 in SCALE_PARTS]
         dx = [held([P, S], F32, "dx%d" % kt) for kt in range(KT)]
         gate_rows = held([P, P], F32, "gate_rows")
         gate_col = held([P, TILES], F32, "gate_col")
@@ -75,13 +95,10 @@ def tile_moe_bdx_glu_relu_kernel(
         for plane in w1s + w3s:
             nc.gpsimd.memset(plane[:].rearrange("p a n -> p (a n)").bitcast(I32), 0)
 
-        def load_scale_rows(plane, scales):
-            rows = scales.rearrange("e s f n -> f (e s) n").bitcast(I32)
-            for r in range(4):
-                nc.sync.dma_start(plane[r:P:32].bitcast(I32), rows[r:16:4])
-
-        def load_words(tile, words, g):
-            nc.sync.dma_start(tile[g][:].bitcast(I32), words[2 * g : 2 * g + 2].rearrange("e s p n -> p (e s) n").bitcast(I32))
+        def load_scale_rows(plane, scale_rows):
+            rows = scale_rows.rearrange("e s f n -> f (e s) n").bitcast(I32)
+            for r in range(PACK):
+                nc.sync.dma_start(plane[r:P:QUADRANT].bitcast(I32), rows[r : PACK * PACK : PACK])
 
         a1_of, a3_of = {}, {}
 
@@ -93,40 +110,48 @@ def tile_moe_bdx_glu_relu_kernel(
 
         def load_w2(g):
             load_scale_rows(w2s[g], w2_scales[2 * g : 2 * g + 2])
-            load_words(w2, w2_words, g)
+            nc.sync.dma_start(
+                w2[g][:].bitcast(I32), w2_words[2 * g : 2 * g + 2].rearrange("e s p n -> p (e s) n").bitcast(I32)
+            )
+
+        def load_part_words(tiles, packed, part):
+            k0, k1 = WORD_PARTS[part]
+            nc.sync.dma_start(
+                tiles[part][:].bitcast(I32), packed[:, 0, :, 2 * k0 : 2 * k1].rearrange("e p n -> p e n").bitcast(I32)
+            )
+
+        def load_part_scales(planes, scale_rows, part):
+            k0, k1 = SCALE_PARTS[part]
+            load_scale_rows(planes[part], scale_rows[:, :, :, k0:k1])
+
+        def offsets(list_sb, first, end):
+            return list_sb[:, first // PER_COLUMN : end // PER_COLUMN]
+
+        def pair_offsets(g):
+            return offsets(offs_sb, g * PAIR, (g + 1) * PAIR)
+
+        def move_second_pass(part):
+            nc.sync.dma_start(
+                gs[1][part][0:MOVED_ROWS, :].bitcast(I32), gs[0][part][PACK : PACK + MOVED_ROWS, :].bitcast(I32)
+            )
 
         nc.sync.dma_start(offs_sb[:], offs)
-        for q in range(4):
-            nc.sync.dma_start(
-                dys[32 * q : 32 * q + 4 * PASSES, :].bitcast(I32), dy_scales[:, 4 * q : 4 * q + 4, :].bitcast(I32)
+        for q in range(P // QUADRANT):
+            (nc.sync, nc.scalar)[q % 2].dma_start(
+                dys[QUADRANT * q : QUADRANT * q + PACK * PASSES, :].bitcast(I32),
+                dy_scales[:, PACK * q : PACK * (q + 1), :].bitcast(I32),
             )
         load_saved(a1_of, a1, "a1", 0, 2)
         nc.sync.dma_start(dyw[:], dy_words.rearrange("o p t d -> p o (t d)").bitcast(I32))
         nc.sync.dma_start(gate_rows[0:TILES, :], gate[0].rearrange("(j s) -> j s", s=P))
         load_w2(0)
 
-        def pair_offsets(g):
-            return offs_sb[:, g * PAIR // 16 : (g + 1) * PAIR // 16]
-
-        def move_second_pass(part):
-            nc.sync.dma_start(gs[1][part][0:100, :].bitcast(I32), gs[0][part][4:104, :].bitcast(I32))
-
         nc.vector.tensor_copy(gs[0][0][:], dys[:].indirect(pair_offsets(0)))
         move_second_pass(0)
         load_saved(a3_of, a3, "a3", 0, 2)
-        for g in range(1, E // 2):
+        for g in range(1, PAIRS):
             nc.vector.tensor_copy(gs[0][1][:, (g - 1) * PAIR : g * PAIR], dys[:].indirect(pair_offsets(g)))
         move_second_pass(1)
-
-        def load_part_words(tile, packed, h):
-            k0, k1 = K_PARTS[h]
-            nc.sync.dma_start(
-                tile[h][:].bitcast(I32), packed[:, 0, :, 2 * k0 : 2 * k1].rearrange("e p n -> p e n").bitcast(I32)
-            )
-
-        def load_part_scales(plane, rows, h):
-            k0, k1 = K_PARTS[h]
-            load_scale_rows(plane[h], rows[:, :, :, k0:k1])
 
         load_saved(a1_of, a1, "a1", 2, 3)
         nc.sync.dma_start(pos1_sb[:], pos1)
@@ -148,44 +173,52 @@ def tile_moe_bdx_glu_relu_kernel(
         load_part_scales(w1s, w1_scales, 1)
         load_part_scales(w3s, w3_scales, 1)
 
-        for g in range(E // 2):
+        for g in range(PAIRS):
             for o in range(PASSES):
                 nc.vector.tensor_copy(gw[o][g][:], dyw[:, o, :].bitcast(U32).indirect(pair_offsets(g)))
 
-        gate_ps = psum.tile([P, PACK, P], F32, name="gate_ps", tag="turned", bufs=4)
+        gate_ps = bank([P, PACK, P], "gate_ps", "turned")
         nc.tensor.transpose(gate_ps[:, 0, :], gate_rows[:], ident[:])
         nc.scalar.copy(gate_col[:], gate_ps[:, 0, 0:TILES])
 
-        def gathered_scales(o, j):
-            if j < 4:
-                return gs[o][0][:, j * P : (j + 1) * P]
-            return gs[o][1][:, (j - 4) * P : (j - 3) * P]
+        dh_rows, dh_cols, relu, mask, da1_factor, da, words, scales = {}, {}, {}, {}, {}, {}, {}, {}
 
-        dh_rows, dh_cols, relu, mask, live, da, words, scales = {}, {}, {}, {}, {}, {}, {}, {}
+        def gathered_plane(o, j):
+            if j < PAIR // P:
+                return gs[o][0][:, j * P : (j + 1) * P]
+            return gs[o][1][:, j * P - PAIR : (j + 1) * P - PAIR]
 
         def first_product(j):
-            e = j // 2
-            acc = psum.tile([P, H], F32, name="acc1", tag="sums", bufs=4)
+            g, in_pair, second_expert = j // 4, j % 4, j // 2 % 2
+            acc = bank([P, H], "acc1", "sums")
             for o in range(PASSES):
                 nc.tensor.matmul_mx(
                     out=acc[:],
-                    lhsT=gw[o][e // 2][:, (j % 4) * P : (j % 4 + 1) * P].bitcast(FP8X4),
-                    lhsT_scale=gathered_scales(o, j),
-                    rhs=w2[e // 2][:, (e % 2) * PASSES + o, :].bitcast(FP4X4),
-                    rhs_scale=w2s[e // 2][:, (e % 2) * PASSES + o, :],
+                    lhsT=gw[o][g][:, in_pair * P : (in_pair + 1) * P].bitcast(FP8X4),
+                    lhsT_scale=gathered_plane(o, j),
+                    rhs=w2[g][:, second_expert * PASSES + o, :].bitcast(FP4X4),
+                    rhs_scale=w2s[g][:, second_expert * PASSES + o, :],
                     start=(o == 0),
                     stop=(o == PASSES - 1),
                 )
-            dh_rows[j] = ring.tile([P, PACK, P], F32, name="dh_rows", tag="rows", bufs=8, align_bytes=64)
+            dh_rows[j] = row_tile([P, PACK, P], "dh_rows")
             nc.scalar.activation(
                 dh_rows[j][:], acc[:].rearrange("s (m t) -> s t m", t=PACK), ACT.Copy, scale=gate_col[:, j : j + 1]
             )
 
-        def half(view, j):
-            return view[:, :, (j % 2) * P : (j % 2 + 1) * P]
+        def turn(j):
+            dh_cols[j] = bank([P, PACK, P], "dh_cols", "turned")
+            for t in range(PACK):
+                nc.tensor.transpose(dh_cols[j][:, t, :], dh_rows[j][:, t, :], ident[:])
+
+        def half(expert_view, j):
+            return expert_view[:, :, (j % 2) * P : (j % 2 + 1) * P]
 
         def in_runs(view):
             return view.rearrange("p t (c i) -> p c t i", i=RUN)
+
+        def woven(flat):
+            return flat.rearrange("p (c i t) -> p c t i", i=RUN, t=PACK)
 
         def rectify(e):
             relu[e] = ring.tile([P, PACK, C], F32, name="relu", tag="relu", bufs=4, align_bytes=64)[:]
@@ -196,17 +229,11 @@ def tile_moe_bdx_glu_relu_kernel(
             if e < POOL_EXPERTS:
                 nc.scalar.activation(mask[e][:], relu[e], ACT.Sign)
             else:
-                woven = mask[e][:].rearrange("p t s -> p (t s)").rearrange("p (c i t) -> p c t i", i=RUN, t=PACK)
-                nc.scalar.activation(woven, in_runs(relu[e]), ACT.Sign)
+                nc.scalar.activation(woven(mask[e][:].rearrange("p t s -> p (t s)")), in_runs(relu[e]), ACT.Sign)
 
         def mask_a3(j):
-            live[j] = ring.tile([P, PACK, P], F32, name="live", tag="live", bufs=6, align_bytes=64)[:]
-            nc.gpsimd.tensor_tensor(live[j], half(a3_of[j // 2], j), half(mask[j // 2][:], j), ALU.mult)
-
-        def turn(j):
-            dh_cols[j] = psum.tile([P, PACK, P], F32, name="dh_cols", tag="turned", bufs=4)
-            for t in range(PACK):
-                nc.tensor.transpose(dh_cols[j][:, t, :], dh_rows[j][:, t, :], ident[:])
+            da1_factor[j] = ring.tile([P, PACK, P], F32, name="masked_a3", tag="masked_a3", bufs=6, align_bytes=64)[:]
+            nc.gpsimd.tensor_tensor(da1_factor[j], half(a3_of[j // 2], j), half(mask[j // 2][:], j), ALU.mult)
 
         place = {}
         for group in QUANT_GROUPS:
@@ -217,24 +244,20 @@ def tile_moe_bdx_glu_relu_kernel(
             for j in range(j0, j1):
                 place[j, which] = (group, j - j0)
 
-        def unit(tiles, j, which):
+        def part_of(tiles, j, which):
             group, n = place[j, which]
             return tiles[group][:, n, :]
 
         def product(j, which):
-            nc.vector.tensor_tensor(
-                unit(da, j, which).rearrange("p (c i t) -> p c t i", i=RUN, t=PACK),
-                in_runs(dh_cols[j][:]),
-                in_runs(half(relu[j // 2], j) if which else live[j]),
-                ALU.mult,
-            )
+            factor = half(relu[j // 2], j) if which == DA3 else da1_factor[j]
+            nc.vector.tensor_tensor(woven(part_of(da, j, which)), in_runs(dh_cols[j][:]), in_runs(factor), ALU.mult)
 
         def mask_da1(group):
             which, j0, j1 = group
-            woven = mask[j0 // 2][:].rearrange("p t s -> p (t s)")
             flat = da[group][:].rearrange("p j n -> p (j n)")
             first = (j0 % 2) * P * PACK
-            nc.vector.tensor_tensor(flat, flat, woven[:, first : first + (j1 - j0) * P * PACK], ALU.mult)
+            zero_or_one = mask[j0 // 2][:].rearrange("p t s -> p (t s)")[:, first : first + (j1 - j0) * P * PACK]
+            nc.vector.tensor_tensor(flat, flat, zero_or_one, ALU.mult)
 
         def quantise(group):
             nc.vector.quantize_mx(
@@ -245,19 +268,19 @@ def tile_moe_bdx_glu_relu_kernel(
 
         def second_product(kt, j0, j1):
             part = min(kt, 1)
-            k0 = kt * P - K_PARTS[part][0]
-            acc = psum.tile([P, j1 - j0, P], F32, name="acc2", tag="sums", bufs=4)
+            k0 = kt * P - WORD_PARTS[part][0]
+            acc = bank([P, j1 - j0, P], "acc2", "sums")
             for j in range(j0, j1):
                 e = j // 2
-                for which, w, ws in ((1, w3, w3s), (0, w1, w1s)):
+                for which, w, ws in ((DA3, w3, w3s), (DA1, w1, w1s)):
                     nc.tensor.matmul_mx(
                         out=acc[:, j - j0, :],
                         lhsT=w[part][:, e, 2 * k0 : 2 * (k0 + P)].bitcast(FP4X4),
-                        lhsT_scale=ws[part][:, e, k0 : k0 + P],
-                        rhs=unit(words, j, which).bitcast(FP8X4),
-                        rhs_scale=unit(scales, j, which),
-                        start=(which == 1),
-                        stop=(which == 0),
+                        lhsT_scale=ws[kt // 2][:, e, (kt % 2) * P : (kt % 2 + 1) * P],
+                        rhs=part_of(words, j, which).bitcast(FP8X4),
+                        rhs_scale=part_of(scales, j, which),
+                        start=(which == DA3),
+                        stop=(which == DA1),
                     )
             nc.scalar.copy(dx[kt][:, j0 * P : j1 * P], acc[:].rearrange("p j s -> p (j s)"))
 
@@ -271,46 +294,46 @@ def tile_moe_bdx_glu_relu_kernel(
                 mask_a3(j)
                 turn(j)
             for j in tiles:
-                product(j, 1)
-                product(j, 0)
-        for j in range(2 * POOL_EXPERTS, TILES):
+                product(j, DA3)
+                product(j, DA1)
+
+        for j in range(POOL_TILES, TILES):
             first_product(j)
             turn(j)
-            live[j] = half(a3_of[j // 2], j)
+            da1_factor[j] = half(a3_of[j // 2], j)
         for e in range(POOL_EXPERTS, E):
             rectify(e)
         for e in range(POOL_EXPERTS, E):
             make_mask(e)
-        pool_da3, pool_da1, late_da3, fifth_da1, tenth_da1, last_da1 = QUANT_GROUPS
-        quantise(pool_da3)
-        quantise(pool_da1)
-        for j in range(2 * POOL_EXPERTS, TILES):
-            product(j, 1)
-        for j in (8, 9):
-            product(j, 0)
-        quantise(late_da3)
-        mask_da1(fifth_da1)
-        product(10, 0)
-        quantise(fifth_da1)
-        product(11, 0)
-        mask_da1(tenth_da1)
-        mask_da1(last_da1)
-        quantise(tenth_da1)
-        quantise(last_da1)
+        quantise(POOL_DA3)
+        quantise(POOL_DA1)
+        for j in range(POOL_TILES, TILES):
+            product(j, DA3)
+        for j in range(POOL_TILES, TILES - 2):
+            product(j, DA1)
+        quantise(LATE_DA3)
+        mask_da1(FIFTH_EXPERT_DA1)
+        product(TILES - 2, DA1)
+        quantise(FIFTH_EXPERT_DA1)
+        product(TILES - 1, DA1)
+        mask_da1(NEXT_TO_LAST_DA1)
+        mask_da1(LAST_DA1)
+        quantise(NEXT_TO_LAST_DA1)
+        quantise(LAST_DA1)
+
         for kt in range(KT):
             for j0, j1 in (FIRST_BANK_GROUPS if kt == 0 else BANK_GROUPS):
                 second_product(kt, j0, j1)
 
         for kt in range(KT):
             cut = T // 2 if kt + 1 < KT else 2 * T // 3
-            halves = (slice(0, cut), slice(cut, T))
-            first = {}
-            for h, cols in enumerate(halves):
-                first[h] = ring.tile([P, cols.stop - cols.start], F32, name="first", tag="rows", bufs=8, align_bytes=64)
-                nc.vector.tensor_copy(first[h][:], dx[kt][:].indirect(pos1_sb[:, cols.start // 16 : cols.stop // 16]))
-            for h, cols in enumerate(halves):
-                total = ring.tile([P, cols.stop - cols.start], F32, name="total", tag="rows", bufs=8, align_bytes=64)
-                nc.vector.tensor_tensor(
-                    total[:], dx[kt][:].indirect(pos2_sb[:, cols.start // 16 : cols.stop // 16]), first[h][:], ALU.add
-                )
-                nc.sync.dma_start(out[kt * P : (kt + 1) * P, cols], total[:])
+            pieces = ((0, cut), (cut, T))
+            fetched = []
+            for t0, t1 in pieces:
+                first = row_tile([P, t1 - t0], "first")
+                nc.vector.tensor_copy(first[:], dx[kt][:].indirect(offsets(pos1_sb, t0, t1)))
+                fetched.append(first)
+            for (t0, t1), first in zip(pieces, fetched):
+                total = row_tile([P, t1 - t0], "total")
+                nc.vector.tensor_tensor(total[:], dx[kt][:].indirect(offsets(pos2_sb, t0, t1)), first[:], ALU.add)
+                nc.sync.dma_start(out[kt * P : (kt + 1) * P, t0:t1], total[:])

@@ -32,19 +32,19 @@ PAIR = 2 * C
 MOVED_ROWS = 3 * QUADRANT + PACK
 RUN = 2
 
-POOL_EXPERTS = 4
-POOL_TILES = 2 * POOL_EXPERTS
+POOL_EXPERTS = 3
+POOL_TILES = 8
 DA1, DA3 = 0, 1
-POOL_DA3 = (DA3, 0, POOL_TILES)
-POOL_DA1 = (DA1, 0, POOL_TILES)
-LATE_DA3 = (DA3, POOL_TILES, TILES)
-FIFTH_EXPERT_DA1 = (DA1, POOL_TILES, TILES - 2)
-NEXT_TO_LAST_DA1 = (DA1, TILES - 2, TILES - 1)
-LAST_DA1 = (DA1, TILES - 1, TILES)
-QUANT_GROUPS = (POOL_DA3, POOL_DA1, LATE_DA3, FIFTH_EXPERT_DA1, NEXT_TO_LAST_DA1, LAST_DA1)
+POOL_FIRST = ((DA1, 0, 6), (DA3, 4, 6))
+POOL_SECOND = ((DA3, 0, 4), (DA3, 6, 8), (DA1, 6, 8))
+LATE_DA3 = ((DA3, POOL_TILES, TILES),)
+FIFTH_EXPERT_DA1 = ((DA1, POOL_TILES, TILES - 2),)
+NEXT_TO_LAST_DA1 = ((DA1, TILES - 2, TILES - 1),)
+LAST_DA1 = ((DA1, TILES - 1, TILES),)
+QUANT_GROUPS = (POOL_FIRST, POOL_SECOND, LATE_DA3, FIFTH_EXPERT_DA1, NEXT_TO_LAST_DA1, LAST_DA1)
 BANK_GROUPS = ((0, 4), (4, 8), (8, 12))
 FIRST_BANK_GROUPS = ((0, 4), (4, 8), (8, 10), (10, 11), (11, 12))
-WORD_PARTS = ((0, P), (P, K))
+WORD_PARTS = ((0, K // 2), (K // 2, K))
 SCALE_PARTS = ((0, K // 2), (K // 2, K))
 
 
@@ -77,9 +77,9 @@ def tile_moe_bdx_glu_relu_kernel(
         w2 = [held([P, 2 * PASSES, 2 * H], U8, "w2_%d" % g) for g in range(PAIRS)]
         w1 = [held([P, E, 2 * (k1 - k0)], U8, "w1_%d" % k0) for k0, k1 in WORD_PARTS]
         w3 = [held([P, E, 2 * (k1 - k0)], U8, "w3_%d" % k0) for k0, k1 in WORD_PARTS]
-        w2s = [held([P, 2 * PASSES, H], U8, "w2s_%d" % g) for g in range(PAIRS)]
-        w1s = [held([P, E, k1 - k0], U8, "w1s_%d" % k0) for k0, k1 in SCALE_PARTS]
-        w3s = [held([P, E, k1 - k0], U8, "w3s_%d" % k0) for k0, k1 in SCALE_PARTS]
+        planes_even = held([P, 2 * PASSES, H], U8, "planes_even")
+        w1s = held([P, E, K], U8, "planes_odd")
+        w2s = [(planes_even, w1s)[g % 2][:, 0 : 2 * PASSES, :] for g in range(PAIRS)]
         dx = [held([P, S], F32, "dx%d" % kt) for kt in range(KT)]
         gate_rows = held([P, P], F32, "gate_rows")
         gate_col = held([P, TILES], F32, "gate_col")
@@ -87,13 +87,11 @@ def tile_moe_bdx_glu_relu_kernel(
 
         nc.gpsimd.memset(dys[:].bitcast(I32), 0)
         nc.gpsimd.memset(gate_rows[:], 0.0)
-        for plane in w2s:
+        for plane in (planes_even, w1s):
             nc.vector.memset(plane[:].rearrange("p a n -> p (a n)").bitcast(I32), 0)
         for plane in gs[1]:
             nc.vector.memset(plane[:].bitcast(I32), 0)
         make_identity(nc, ident[:])
-        for plane in w1s + w3s:
-            nc.gpsimd.memset(plane[:].rearrange("p a n -> p (a n)").bitcast(I32), 0)
 
         def load_scale_rows(plane, scale_rows):
             rows = scale_rows.rearrange("e s f n -> f (e s) n").bitcast(I32)
@@ -108,21 +106,20 @@ def tile_moe_bdx_glu_relu_kernel(
             for e in range(e0, e1):
                 views[e] = tile[:, :, (e - e0) * C : (e - e0 + 1) * C]
 
-        def load_w2(g):
-            load_scale_rows(w2s[g], w2_scales[2 * g : 2 * g + 2])
+        def load_w2_words(g):
             nc.sync.dma_start(
                 w2[g][:].bitcast(I32), w2_words[2 * g : 2 * g + 2].rearrange("e s p n -> p (e s) n").bitcast(I32)
             )
+
+        def load_w2(g):
+            load_scale_rows(w2s[g], w2_scales[2 * g : 2 * g + 2])
+            load_w2_words(g)
 
         def load_part_words(tiles, packed, part):
             k0, k1 = WORD_PARTS[part]
             nc.sync.dma_start(
                 tiles[part][:].bitcast(I32), packed[:, 0, :, 2 * k0 : 2 * k1].rearrange("e p n -> p e n").bitcast(I32)
             )
-
-        def load_part_scales(planes, scale_rows, part):
-            k0, k1 = SCALE_PARTS[part]
-            load_scale_rows(planes[part], scale_rows[:, :, :, k0:k1])
 
         def offsets(list_sb, first, end):
             return list_sb[:, first // PER_COLUMN : end // PER_COLUMN]
@@ -141,37 +138,26 @@ def tile_moe_bdx_glu_relu_kernel(
                 dys[QUADRANT * q : QUADRANT * q + PACK * PASSES, :].bitcast(I32),
                 dy_scales[:, PACK * q : PACK * (q + 1), :].bitcast(I32),
             )
-        load_saved(a1_of, a1, "a1", 0, 2)
+        load_saved(a1_of, a1, "a1", 0, 1)
         nc.sync.dma_start(dyw[:], dy_words.rearrange("o p t d -> p o (t d)").bitcast(I32))
         nc.sync.dma_start(gate_rows[0:TILES, :], gate[0].rearrange("(j s) -> j s", s=P))
-        load_w2(0)
+        load_saved(a1_of, a1, "a1", 1, 2)
+        load_scale_rows(w2s[0], w2_scales[0:2])
 
         nc.vector.tensor_copy(gs[0][0][:], dys[:].indirect(pair_offsets(0)))
         move_second_pass(0)
-        load_saved(a3_of, a3, "a3", 0, 2)
+        load_w2_words(0)
+        load_saved(a3_of, a3, "a3", 0, 1)
         for g in range(1, PAIRS):
             nc.vector.tensor_copy(gs[0][1][:, (g - 1) * PAIR : g * PAIR], dys[:].indirect(pair_offsets(g)))
         move_second_pass(1)
-
         load_saved(a1_of, a1, "a1", 2, 3)
-        nc.sync.dma_start(pos1_sb[:], pos1)
-        nc.sync.dma_start(pos2_sb[:], pos2)
+        load_saved(a3_of, a3, "a3", 1, 2)
+
         load_w2(1)
-        load_saved(a3_of, a3, "a3", 2, 3)
         load_saved(a1_of, a1, "a1", 3, 4)
+        load_saved(a3_of, a3, "a3", 2, 3)
         load_saved(a3_of, a3, "a3", 3, 4)
-        load_part_scales(w1s, w1_scales, 0)
-        load_w2(2)
-        load_saved(a1_of, a1, "a1", 4, 6)
-        load_saved(a3_of, a3, "a3", 4, 5)
-        load_part_scales(w3s, w3_scales, 0)
-        load_part_words(w1, w1_words, 0)
-        load_part_words(w3, w3_words, 0)
-        load_saved(a3_of, a3, "a3", 5, 6)
-        load_part_words(w1, w1_words, 1)
-        load_part_words(w3, w3_words, 1)
-        load_part_scales(w1s, w1_scales, 1)
-        load_part_scales(w3s, w3_scales, 1)
 
         for g in range(PAIRS):
             for o in range(PASSES):
@@ -225,24 +211,29 @@ def tile_moe_bdx_glu_relu_kernel(
             nc.scalar.activation(relu[e], a1_of[e], ACT.Relu)
 
         def make_mask(e):
-            mask[e] = ring.tile([P, PACK, C], BF16, name="mask", tag="mask", bufs=4, align_bytes=64)
+            if e == 0:
+                mask[e] = keep.tile([P, PACK, C], BF16, name="mask_0", tag="mask_0", align_bytes=64)
+            else:
+                mask[e] = ring.tile([P, PACK, C], BF16, name="mask", tag="mask", bufs=4, align_bytes=64)
             if e < POOL_EXPERTS:
                 nc.scalar.activation(mask[e][:], relu[e], ACT.Sign)
             else:
                 nc.scalar.activation(woven(mask[e][:].rearrange("p t s -> p (t s)")), in_runs(relu[e]), ACT.Sign)
 
-        def mask_a3(j):
-            da1_factor[j] = ring.tile([P, PACK, P], F32, name="masked_a3", tag="masked_a3", bufs=6, align_bytes=64)[:]
-            nc.gpsimd.tensor_tensor(da1_factor[j], half(a3_of[j // 2], j), half(mask[j // 2][:], j), ALU.mult)
+        def mask_a3(e):
+            masked = held([P, PACK, C], F32, "masked_a3_%d" % e)[:]
+            nc.gpsimd.tensor_tensor(masked, a3_of[e], mask[e][:], ALU.mult)
+            for j in (2 * e, 2 * e + 1):
+                da1_factor[j] = half(masked, j)
 
         place = {}
         for group in QUANT_GROUPS:
-            which, j0, j1 = group
-            da[group] = held([P, j1 - j0, P * PACK], BF16, "da%d_%d" % (which, j0))
-            words[group] = held([P, j1 - j0, P], U32, "da_words%d_%d" % (which, j0))
-            scales[group] = held([P, j1 - j0, P], U8, "da_scales%d_%d" % (which, j0))
-            for j in range(j0, j1):
-                place[j, which] = (group, j - j0)
+            members = [(j, which) for which, j0, j1 in group for j in range(j0, j1)]
+            da[group] = held([P, len(members), P * PACK], BF16, "da%d_%d" % members[0])
+            words[group] = held([P, len(members), P], U32, "da_words%d_%d" % members[0])
+            scales[group] = held([P, len(members), P], U8, "da_scales%d_%d" % members[0])
+            for n, member in enumerate(members):
+                place[member] = (group, n)
 
         def part_of(tiles, j, which):
             group, n = place[j, which]
@@ -252,9 +243,14 @@ def tile_moe_bdx_glu_relu_kernel(
             factor = half(relu[j // 2], j) if which == DA3 else da1_factor[j]
             nc.vector.tensor_tensor(woven(part_of(da, j, which)), in_runs(dh_cols[j][:]), in_runs(factor), ALU.mult)
 
-        def mask_da1(group):
-            which, j0, j1 = group
-            flat = da[group][:].rearrange("p j n -> p (j n)")
+        def products(e):
+            for which in (DA3, DA1):
+                for j in (2 * e, 2 * e + 1):
+                    product(j, which)
+
+        def mask_da1(j0, j1):
+            group, n = place[j0, DA1]
+            flat = da[group][:, n : n + j1 - j0, :].rearrange("p j n -> p (j n)")
             first = (j0 % 2) * P * PACK
             zero_or_one = mask[j0 // 2][:].rearrange("p t s -> p (t s)")[:, first : first + (j1 - j0) * P * PACK]
             nc.vector.tensor_tensor(flat, flat, zero_or_one, ALU.mult)
@@ -267,7 +263,7 @@ def tile_moe_bdx_glu_relu_kernel(
             )
 
         def second_product(kt, j0, j1):
-            part = min(kt, 1)
+            part = kt // 2
             k0 = kt * P - WORD_PARTS[part][0]
             acc = bank([P, j1 - j0, P], "acc2", "sums")
             for j in range(j0, j1):
@@ -276,7 +272,7 @@ def tile_moe_bdx_glu_relu_kernel(
                     nc.tensor.matmul_mx(
                         out=acc[:, j - j0, :],
                         lhsT=w[part][:, e, 2 * k0 : 2 * (k0 + P)].bitcast(FP4X4),
-                        lhsT_scale=ws[kt // 2][:, e, (kt % 2) * P : (kt % 2 + 1) * P],
+                        lhsT_scale=ws[:, e, kt * P : (kt + 1) * P],
                         rhs=part_of(words, j, which).bitcast(FP8X4),
                         rhs_scale=part_of(scales, j, which),
                         start=(which == DA3),
@@ -284,40 +280,72 @@ def tile_moe_bdx_glu_relu_kernel(
                     )
             nc.scalar.copy(dx[kt][:, j0 * P : j1 * P], acc[:].rearrange("p j s -> p (j s)"))
 
-        for e in range(POOL_EXPERTS):
-            tiles = (2 * e, 2 * e + 1)
+        for e in range(2):
             rectify(e)
             make_mask(e)
-            for j in tiles:
-                first_product(j)
-            for j in tiles:
-                mask_a3(j)
-                turn(j)
-            for j in tiles:
-                product(j, DA3)
-                product(j, DA1)
+            mask_a3(e)
+            if e == 0:
+                w3s = keep.tile([P, E, K], U8, name="w3s", tag="mask_0", align_bytes=64)
+                nc.gpsimd.memset(w3s[:].rearrange("p a n -> p (a n)").bitcast(I32), 0)
+        for j in range(4):
+            first_product(j)
+        load_saved(a1_of, a1, "a1", 4, 5)
+        load_w2(2)
+        load_saved(a1_of, a1, "a1", 5, 6)
+        nc.sync.dma_start(pos1_sb[:], pos1)
+        nc.sync.dma_start(pos2_sb[:], pos2)
+        load_saved(a3_of, a3, "a3", 4, 5)
+        for j in range(4):
+            turn(j)
+        rectify(2)
+        make_mask(2)
+        mask_a3(2)
+        for e in range(2):
+            products(e)
+        for j in (4, 5):
+            first_product(j)
+            turn(j)
+        rectify(3)
+        for j in (6, 7):
+            first_product(j)
+            turn(j)
+            da1_factor[j] = half(a3_of[3], j)
+        make_mask(3)
+        load_scale_rows(w1s, w1_scales)
+        load_part_words(w1, w1_words, 0)
+        load_scale_rows(w3s, w3_scales)
+        load_part_words(w3, w3_words, 0)
+        load_saved(a3_of, a3, "a3", 5, 6)
+        load_part_words(w1, w1_words, 1)
+        load_part_words(w3, w3_words, 1)
+        products(2)
+        product(6, DA3)
+        quantise(POOL_FIRST)
+        product(6, DA1)
+        product(7, DA1)
+        product(7, DA3)
+        mask_da1(6, 8)
 
         for j in range(POOL_TILES, TILES):
             first_product(j)
             turn(j)
             da1_factor[j] = half(a3_of[j // 2], j)
-        for e in range(POOL_EXPERTS, E):
+        for e in range(4, E):
             rectify(e)
-        for e in range(POOL_EXPERTS, E):
+        for e in range(4, E):
             make_mask(e)
-        quantise(POOL_DA3)
-        quantise(POOL_DA1)
+        quantise(POOL_SECOND)
         for j in range(POOL_TILES, TILES):
             product(j, DA3)
         for j in range(POOL_TILES, TILES - 2):
             product(j, DA1)
         quantise(LATE_DA3)
-        mask_da1(FIFTH_EXPERT_DA1)
+        mask_da1(8, 10)
         product(TILES - 2, DA1)
         quantise(FIFTH_EXPERT_DA1)
         product(TILES - 1, DA1)
-        mask_da1(NEXT_TO_LAST_DA1)
-        mask_da1(LAST_DA1)
+        mask_da1(10, 11)
+        mask_da1(11, 12)
         quantise(NEXT_TO_LAST_DA1)
         quantise(LAST_DA1)
 

@@ -30,18 +30,21 @@ KT = K // P
 PAIRS = E // 2
 PAIR = 2 * C
 MOVED_ROWS = 3 * QUADRANT + PACK
+WIDE = 1408
 RUN = 2
 
-POOL_EXPERTS = 3
+POOL_EXPERTS = 2
 POOL_TILES = 8
 DA1, DA3 = 0, 1
-POOL_FIRST = ((DA1, 0, 6), (DA3, 4, 6))
-POOL_SECOND = ((DA3, 0, 4), (DA3, 6, 8), (DA1, 6, 8))
-LATE_DA3 = ((DA3, POOL_TILES, TILES),)
-FIFTH_EXPERT_DA1 = ((DA1, POOL_TILES, TILES - 2),)
+POOL_FIRST = ((DA3, 0, 3), (DA1, 2, 3))
+POOL_REST = ((DA1, 0, 2), (DA1, 3, 4), (DA3, 3, 4))
+POOL_SECOND = ((DA1, 4, 8),)
+MIDDLE_DA3 = ((DA3, 4, 8),)
+LATE_DA3 = ((DA3, 8, 11), (DA1, 8, 9))
+FIFTH_EXPERT_DA1 = ((DA1, 9, 10), (DA3, 11, 12))
 NEXT_TO_LAST_DA1 = ((DA1, TILES - 2, TILES - 1),)
 LAST_DA1 = ((DA1, TILES - 1, TILES),)
-QUANT_GROUPS = (POOL_FIRST, POOL_SECOND, LATE_DA3, FIFTH_EXPERT_DA1, NEXT_TO_LAST_DA1, LAST_DA1)
+QUANT_GROUPS = (POOL_FIRST, POOL_REST, POOL_SECOND, MIDDLE_DA3, LATE_DA3, FIFTH_EXPERT_DA1, NEXT_TO_LAST_DA1, LAST_DA1)
 BANK_GROUPS = ((0, 4), (4, 8), (8, 12))
 FIRST_BANK_GROUPS = ((0, 4), (4, 8), (8, 10), (10, 11), (11, 12))
 WORD_PARTS = ((0, K // 2), (K // 2, K))
@@ -70,9 +73,9 @@ def tile_moe_bdx_glu_relu_kernel(
         offs_sb = keep.tile([P, S // PER_COLUMN], U16, name="offs_sb")
         pos1_sb = keep.tile([P, T // PER_COLUMN], U16, name="pos1_sb")
         pos2_sb = keep.tile([P, T // PER_COLUMN], U16, name="pos2_sb")
-        dyw = held([P, PASSES, T], I32, "dyw")
-        dys = held([P, T], U8, "dys")
-        gw = [[held([P, PAIR], U32, "gw%d_%d" % (o, g)) for g in range(PAIRS)] for o in range(PASSES)]
+        dyw = held([P, T + WIDE], I32, "dyw")
+        dys = held([P, WIDE], U8, "dys")
+        gw = [[held([P, cols], U32, "gw%d_%d" % (o, cols)) for cols in (PAIR, S - PAIR)] for o in range(PASSES)]
         gs = [[held([P, cols], U8, "gs%d_%d" % (o, cols)) for cols in (PAIR, S - PAIR)] for o in range(PASSES)]
         w2 = [held([P, 2 * PASSES, 2 * H], U8, "w2_%d" % g) for g in range(PAIRS)]
         w1 = [held([P, E, 2 * (k1 - k0)], U8, "w1_%d" % k0) for k0, k1 in WORD_PARTS]
@@ -91,6 +94,7 @@ def tile_moe_bdx_glu_relu_kernel(
             nc.vector.memset(plane[:].rearrange("p a n -> p (a n)").bitcast(I32), 0)
         for plane in gs[1]:
             nc.vector.memset(plane[:].bitcast(I32), 0)
+        nc.vector.memset(dyw[:, PASSES * T :], 0)
         make_identity(nc, ident[:])
 
         def load_scale_rows(plane, scale_rows):
@@ -124,9 +128,6 @@ def tile_moe_bdx_glu_relu_kernel(
         def offsets(list_sb, first, end):
             return list_sb[:, first // PER_COLUMN : end // PER_COLUMN]
 
-        def pair_offsets(g):
-            return offsets(offs_sb, g * PAIR, (g + 1) * PAIR)
-
         def move_second_pass(part):
             nc.sync.dma_start(
                 gs[1][part][0:MOVED_ROWS, :].bitcast(I32), gs[0][part][PACK : PACK + MOVED_ROWS, :].bitcast(I32)
@@ -135,33 +136,33 @@ def tile_moe_bdx_glu_relu_kernel(
         nc.sync.dma_start(offs_sb[:], offs)
         for q in range(P // QUADRANT):
             (nc.sync, nc.scalar)[q % 2].dma_start(
-                dys[QUADRANT * q : QUADRANT * q + PACK * PASSES, :].bitcast(I32),
+                dys[QUADRANT * q : QUADRANT * q + PACK * PASSES, 0:T].bitcast(I32),
                 dy_scales[:, PACK * q : PACK * (q + 1), :].bitcast(I32),
             )
         load_saved(a1_of, a1, "a1", 0, 1)
-        nc.sync.dma_start(dyw[:], dy_words.rearrange("o p t d -> p o (t d)").bitcast(I32))
+        nc.sync.dma_start(
+            dyw[:, 0 : PASSES * T].rearrange("p (o t) -> p o t", o=PASSES),
+            dy_words.rearrange("o p t d -> p o (t d)").bitcast(I32),
+        )
         nc.sync.dma_start(gate_rows[0:TILES, :], gate[0].rearrange("(j s) -> j s", s=P))
         load_saved(a1_of, a1, "a1", 1, 2)
         load_scale_rows(w2s[0], w2_scales[0:2])
 
-        nc.vector.tensor_copy(gs[0][0][:], dys[:].indirect(pair_offsets(0)))
+        nc.vector.tensor_copy(gs[0][0][:], dys[:, 0:T].indirect(offsets(offs_sb, 0, PAIR)))
         move_second_pass(0)
         load_w2_words(0)
-        load_saved(a3_of, a3, "a3", 0, 1)
-        for g in range(1, PAIRS):
-            nc.vector.tensor_copy(gs[0][1][:, (g - 1) * PAIR : g * PAIR], dys[:].indirect(pair_offsets(g)))
+        load_saved(a3_of, a3, "a3", 0, 2)
+        nc.vector.tensor_copy(gs[0][1][:], dys[:].indirect(offsets(offs_sb, PAIR, S)))
         move_second_pass(1)
-        load_saved(a1_of, a1, "a1", 2, 3)
-        load_saved(a3_of, a3, "a3", 1, 2)
-
         load_w2(1)
-        load_saved(a1_of, a1, "a1", 3, 4)
-        load_saved(a3_of, a3, "a3", 2, 3)
-        load_saved(a3_of, a3, "a3", 3, 4)
+        load_saved(a1_of, a1, "a1", 2, 4)
+        load_saved(a3_of, a3, "a3", 2, 4)
 
-        for g in range(PAIRS):
+        for part, (first, end, window) in enumerate(((0, PAIR, T), (PAIR, S, WIDE))):
             for o in range(PASSES):
-                nc.vector.tensor_copy(gw[o][g][:], dyw[:, o, :].bitcast(U32).indirect(pair_offsets(g)))
+                nc.vector.tensor_copy(
+                    gw[o][part][:], dyw[:, o * T : o * T + window].bitcast(U32).indirect(offsets(offs_sb, first, end))
+                )
 
         gate_ps = bank([P, PACK, P], "gate_ps", "turned")
         nc.tensor.transpose(gate_ps[:, 0, :], gate_rows[:], ident[:])
@@ -169,19 +170,19 @@ def tile_moe_bdx_glu_relu_kernel(
 
         dh_rows, dh_cols, relu, mask, da1_factor, da, words, scales = {}, {}, {}, {}, {}, {}, {}, {}
 
-        def gathered_plane(o, j):
+        def gathered(tiles, o, j):
             if j < PAIR // P:
-                return gs[o][0][:, j * P : (j + 1) * P]
-            return gs[o][1][:, j * P - PAIR : (j + 1) * P - PAIR]
+                return tiles[o][0][:, j * P : (j + 1) * P]
+            return tiles[o][1][:, j * P - PAIR : (j + 1) * P - PAIR]
 
         def first_product(j):
-            g, in_pair, second_expert = j // 4, j % 4, j // 2 % 2
+            g, second_expert = j // 4, j // 2 % 2
             acc = bank([P, H], "acc1", "sums")
             for o in range(PASSES):
                 nc.tensor.matmul_mx(
                     out=acc[:],
-                    lhsT=gw[o][g][:, in_pair * P : (in_pair + 1) * P].bitcast(FP8X4),
-                    lhsT_scale=gathered_plane(o, j),
+                    lhsT=gathered(gw, o, j).bitcast(FP8X4),
+                    lhsT_scale=gathered(gs, o, j),
                     rhs=w2[g][:, second_expert * PASSES + o, :].bitcast(FP4X4),
                     rhs_scale=w2s[g][:, second_expert * PASSES + o, :],
                     start=(o == 0),
@@ -211,7 +212,7 @@ def tile_moe_bdx_glu_relu_kernel(
             nc.scalar.activation(relu[e], a1_of[e], ACT.Relu)
 
         def make_mask(e):
-            if e == 0:
+            if e == POOL_EXPERTS - 1:
                 mask[e] = keep.tile([P, PACK, C], BF16, name="mask_0", tag="mask_0", align_bytes=64)
             else:
                 mask[e] = ring.tile([P, PACK, C], BF16, name="mask", tag="mask", bufs=4, align_bytes=64)
@@ -240,7 +241,10 @@ def tile_moe_bdx_glu_relu_kernel(
             return tiles[group][:, n, :]
 
         def product(j, which):
-            factor = half(relu[j // 2], j) if which == DA3 else da1_factor[j]
+            if which == DA3:
+                factor = half(relu[j // 2], j)
+            else:
+                factor = da1_factor[j] if j in da1_factor else half(a3_of[j // 2], j)
             nc.vector.tensor_tensor(woven(part_of(da, j, which)), in_runs(dh_cols[j][:]), in_runs(factor), ALU.mult)
 
         def products(e):
@@ -266,51 +270,52 @@ def tile_moe_bdx_glu_relu_kernel(
             part = kt // 2
             k0 = kt * P - WORD_PARTS[part][0]
             acc = bank([P, j1 - j0, P], "acc2", "sums")
-            for j in range(j0, j1):
+            last_first = kt == 1 and j1 == TILES
+            for j in (range(j1 - 1, j0 - 1, -1) if last_first else range(j0, j1)):
                 e = j // 2
-                for which, w, ws in ((DA3, w3, w3s), (DA1, w1, w1s)):
+                both = ((DA3, w3, w3s), (DA1, w1, w1s))
+                for n, (which, w, ws) in enumerate(both[::-1] if last_first else both):
                     nc.tensor.matmul_mx(
                         out=acc[:, j - j0, :],
                         lhsT=w[part][:, e, 2 * k0 : 2 * (k0 + P)].bitcast(FP4X4),
                         lhsT_scale=ws[:, e, kt * P : (kt + 1) * P],
                         rhs=part_of(words, j, which).bitcast(FP8X4),
                         rhs_scale=part_of(scales, j, which),
-                        start=(which == DA3),
-                        stop=(which == DA1),
+                        start=(n == 0),
+                        stop=(n == 1),
                     )
             nc.scalar.copy(dx[kt][:, j0 * P : j1 * P], acc[:].rearrange("p j s -> p (j s)"))
 
-        for e in range(2):
+        for e in range(POOL_EXPERTS):
             rectify(e)
             make_mask(e)
             mask_a3(e)
-            if e == 0:
-                w3s = keep.tile([P, E, K], U8, name="w3s", tag="mask_0", align_bytes=64)
-                nc.gpsimd.memset(w3s[:].rearrange("p a n -> p (a n)").bitcast(I32), 0)
+        w3s = keep.tile([P, E, K], U8, name="w3s", tag="mask_0", align_bytes=64)
+        nc.gpsimd.memset(w3s[:].rearrange("p a n -> p (a n)").bitcast(I32), 0)
         for j in range(4):
             first_product(j)
-        load_saved(a1_of, a1, "a1", 4, 5)
         load_w2(2)
-        load_saved(a1_of, a1, "a1", 5, 6)
+        load_saved(a1_of, a1, "a1", 4, 6)
         nc.sync.dma_start(pos1_sb[:], pos1)
         nc.sync.dma_start(pos2_sb[:], pos2)
         load_saved(a3_of, a3, "a3", 4, 5)
         for j in range(4):
             turn(j)
-        rectify(2)
-        make_mask(2)
-        mask_a3(2)
-        for e in range(2):
+        for e in range(POOL_EXPERTS):
             products(e)
-        for j in (4, 5):
-            first_product(j)
-            turn(j)
-        rectify(3)
-        for j in (6, 7):
-            first_product(j)
-            turn(j)
-            da1_factor[j] = half(a3_of[3], j)
-        make_mask(3)
+        quantise(POOL_FIRST)
+        quantise(POOL_REST)
+
+        def prepare(g):
+            for e in (2 * g, 2 * g + 1):
+                for j in (2 * e, 2 * e + 1):
+                    first_product(j)
+                    turn(j)
+                rectify(e)
+            for e in (2 * g, 2 * g + 1):
+                make_mask(e)
+
+        prepare(1)
         load_scale_rows(w1s, w1_scales)
         load_part_words(w1, w1_words, 0)
         load_scale_rows(w3s, w3_scales)
@@ -319,49 +324,54 @@ def tile_moe_bdx_glu_relu_kernel(
         load_part_words(w1, w1_words, 1)
         load_part_words(w3, w3_words, 1)
         products(2)
-        product(6, DA3)
-        quantise(POOL_FIRST)
         product(6, DA1)
+        mask_da1(4, 6)
         product(7, DA1)
-        product(7, DA3)
+        product(6, DA3)
         mask_da1(6, 8)
-
-        for j in range(POOL_TILES, TILES):
-            first_product(j)
-            turn(j)
-            da1_factor[j] = half(a3_of[j // 2], j)
-        for e in range(4, E):
-            rectify(e)
-        for e in range(4, E):
-            make_mask(e)
+        product(7, DA3)
         quantise(POOL_SECOND)
+        quantise(MIDDLE_DA3)
+        prepare(2)
         for j in range(POOL_TILES, TILES):
             product(j, DA3)
         for j in range(POOL_TILES, TILES - 2):
             product(j, DA1)
+        mask_da1(8, 9)
+        mask_da1(9, 10)
         quantise(LATE_DA3)
-        mask_da1(8, 10)
-        product(TILES - 2, DA1)
         quantise(FIFTH_EXPERT_DA1)
+        product(TILES - 2, DA1)
         product(TILES - 1, DA1)
         mask_da1(10, 11)
         mask_da1(11, 12)
         quantise(NEXT_TO_LAST_DA1)
         quantise(LAST_DA1)
 
-        for kt in range(KT):
-            for j0, j1 in (FIRST_BANK_GROUPS if kt == 0 else BANK_GROUPS):
+        for kt in range(2):
+            for j0, j1 in BANK_GROUPS[:2]:
+                second_product(kt, j0, j1)
+        for j0, j1 in FIRST_BANK_GROUPS[2:]:
+            second_product(0, j0, j1)
+        second_product(1, *BANK_GROUPS[2])
+        for kt in range(2, KT):
+            for j0, j1 in BANK_GROUPS:
                 second_product(kt, j0, j1)
 
-        for kt in range(KT):
-            cut = T // 2 if kt + 1 < KT else 2 * T // 3
-            pieces = ((0, cut), (cut, T))
-            fetched = []
-            for t0, t1 in pieces:
-                first = row_tile([P, t1 - t0], "first")
-                nc.vector.tensor_copy(first[:], dx[kt][:].indirect(offsets(pos1_sb, t0, t1)))
-                fetched.append(first)
-            for (t0, t1), first in zip(pieces, fetched):
-                total = row_tile([P, t1 - t0], "total")
-                nc.vector.tensor_tensor(total[:], dx[kt][:].indirect(offsets(pos2_sb, t0, t1)), first[:], ALU.add)
-                nc.sync.dma_start(out[kt * P : (kt + 1) * P, t0:t1], total[:])
+        fetched = {}
+
+        def fetch(kt):
+            fetched[kt] = row_tile([P, T], "first")
+            nc.vector.tensor_copy(fetched[kt][:], dx[kt][:].indirect(pos1_sb[:]))
+
+        def add_and_store(kt, t0, t1):
+            total = row_tile([P, t1 - t0], "total")
+            nc.vector.tensor_tensor(total[:], dx[kt][:].indirect(offsets(pos2_sb, t0, t1)), fetched[kt][:, t0:t1], ALU.add)
+            nc.sync.dma_start(out[kt * P : (kt + 1) * P, t0:t1], total[:])
+
+        fetch(0)
+        for kt in range(KT - 1):
+            fetch(kt + 1)
+            add_and_store(kt, 0, T)
+        add_and_store(KT - 1, 0, 2 * T // 3)
+        add_and_store(KT - 1, 2 * T // 3, T)

@@ -34,21 +34,21 @@ WIDE = 1408
 RUN = 2
 
 POOL_EXPERTS = 2
-POOL_TILES = 8
 DA1, DA3 = 0, 1
-POOL_FIRST = ((DA3, 0, 3), (DA1, 2, 3))
-POOL_REST = ((DA1, 0, 2), (DA1, 3, 4), (DA3, 3, 4))
-POOL_SECOND = ((DA1, 4, 8),)
-MIDDLE_DA3 = ((DA3, 4, 8),)
-LATE_DA3 = ((DA3, 8, 11), (DA1, 8, 9))
-FIFTH_EXPERT_DA1 = ((DA1, 9, 10), (DA3, 11, 12))
-NEXT_TO_LAST_DA1 = ((DA1, TILES - 2, TILES - 1),)
-LAST_DA1 = ((DA1, TILES - 1, TILES),)
-QUANT_GROUPS = (POOL_FIRST, POOL_REST, POOL_SECOND, MIDDLE_DA3, LATE_DA3, FIFTH_EXPERT_DA1, NEXT_TO_LAST_DA1, LAST_DA1)
+FIRST_PAIR_A = ((DA3, 0, 3), (DA1, 2, 3))
+FIRST_PAIR_B = ((DA1, 0, 2), (DA1, 3, 4), (DA3, 3, 4))
+SECOND_PAIR_DA1 = ((DA1, 4, 8),)
+SECOND_PAIR_DA3 = ((DA3, 4, 8),)
+LAST_PAIR_A = ((DA3, 8, 11), (DA1, 8, 9))
+LAST_PAIR_B = ((DA1, 9, 10), (DA3, 11, 12))
+NEXT_TO_LAST_DA1 = ((DA1, 10, 11),)
+LAST_DA1 = ((DA1, 11, 12),)
+QUANT_GROUPS = (
+    FIRST_PAIR_A, FIRST_PAIR_B, SECOND_PAIR_DA1, SECOND_PAIR_DA3, LAST_PAIR_A, LAST_PAIR_B, NEXT_TO_LAST_DA1, LAST_DA1
+)
 BANK_GROUPS = ((0, 4), (4, 8), (8, 12))
 FIRST_BANK_GROUPS = ((0, 4), (4, 8), (8, 10), (10, 11), (11, 12))
 WORD_PARTS = ((0, K // 2), (K // 2, K))
-SCALE_PARTS = ((0, K // 2), (K // 2, K))
 
 
 def tile_moe_bdx_glu_relu_kernel(
@@ -80,22 +80,23 @@ def tile_moe_bdx_glu_relu_kernel(
         w2 = [held([P, 2 * PASSES, 2 * H], U8, "w2_%d" % g) for g in range(PAIRS)]
         w1 = [held([P, E, 2 * (k1 - k0)], U8, "w1_%d" % k0) for k0, k1 in WORD_PARTS]
         w3 = [held([P, E, 2 * (k1 - k0)], U8, "w3_%d" % k0) for k0, k1 in WORD_PARTS]
-        planes_even = held([P, 2 * PASSES, H], U8, "planes_even")
-        w1s = held([P, E, K], U8, "planes_odd")
-        w2s = [(planes_even, w1s)[g % 2][:, 0 : 2 * PASSES, :] for g in range(PAIRS)]
+        planes = [held([P, 2 * PASSES * H], U8, "planes_%d" % n) for n in range(2)]
+        w2s = [planes[g % 2][:].rearrange("p (a n) -> p a n", n=H) for g in range(PAIRS)]
+        late_w3s, late_w1s = (plane[:, 0 : E * K // 2].rearrange("p (e n) -> p e n", e=E) for plane in planes)
         dx = [held([P, S], F32, "dx%d" % kt) for kt in range(KT)]
         gate_rows = held([P, P], F32, "gate_rows")
         gate_col = held([P, TILES], F32, "gate_col")
         ident = held([P, P], F32, "ident")
 
-        nc.gpsimd.memset(dys[:].bitcast(I32), 0)
+        nc.gpsimd.memset(dys[:, 0:T].bitcast(I32), 0)
         nc.gpsimd.memset(gate_rows[:], 0.0)
-        for plane in (planes_even, w1s):
-            nc.vector.memset(plane[:].rearrange("p a n -> p (a n)").bitcast(I32), 0)
+        for plane in planes:
+            nc.vector.memset(plane[:].bitcast(I32), 0)
         for plane in gs[1]:
             nc.vector.memset(plane[:].bitcast(I32), 0)
         nc.vector.memset(dyw[:, PASSES * T :], 0)
         make_identity(nc, ident[:])
+        nc.gpsimd.memset(dys[:, T:WIDE].bitcast(I32), 0)
 
         def load_scale_rows(plane, scale_rows):
             rows = scale_rows.rearrange("e s f n -> f (e s) n").bitcast(I32)
@@ -124,6 +125,10 @@ def tile_moe_bdx_glu_relu_kernel(
             nc.sync.dma_start(
                 tiles[part][:].bitcast(I32), packed[:, 0, :, 2 * k0 : 2 * k1].rearrange("e p n -> p e n").bitcast(I32)
             )
+
+        def load_part_scales(parts, scale_rows, part):
+            k0, k1 = WORD_PARTS[part]
+            load_scale_rows(parts[part], scale_rows[:, :, :, k0:k1])
 
         def offsets(list_sb, first, end):
             return list_sb[:, first // PER_COLUMN : end // PER_COLUMN]
@@ -188,9 +193,12 @@ def tile_moe_bdx_glu_relu_kernel(
                     start=(o == 0),
                     stop=(o == PASSES - 1),
                 )
-            dh_rows[j] = row_tile([P, PACK, P], "dh_rows")
+            if j // 2 == 3:
+                dh_rows[j] = half(a1_of[j // 2 - 1], j)
+            else:
+                dh_rows[j] = row_tile([P, PACK, P], "dh_rows")[:]
             nc.scalar.activation(
-                dh_rows[j][:], acc[:].rearrange("s (m t) -> s t m", t=PACK), ACT.Copy, scale=gate_col[:, j : j + 1]
+                dh_rows[j], acc[:].rearrange("s (m t) -> s t m", t=PACK), ACT.Copy, scale=gate_col[:, j : j + 1]
             )
 
         def turn(j):
@@ -213,9 +221,9 @@ def tile_moe_bdx_glu_relu_kernel(
 
         def make_mask(e):
             if e == POOL_EXPERTS - 1:
-                mask[e] = keep.tile([P, PACK, C], BF16, name="mask_0", tag="mask_0", align_bytes=64)
+                mask[e] = keep.tile([P, PACK, C], BF16, name="second_mask", tag="second_mask", align_bytes=64)
             else:
-                mask[e] = ring.tile([P, PACK, C], BF16, name="mask", tag="mask", bufs=4, align_bytes=64)
+                mask[e] = ring.tile([P, PACK, C], BF16, name="mask", tag="mask", bufs=3, align_bytes=64)
             if e < POOL_EXPERTS:
                 nc.scalar.activation(mask[e][:], relu[e], ACT.Sign)
             else:
@@ -231,7 +239,8 @@ def tile_moe_bdx_glu_relu_kernel(
         for group in QUANT_GROUPS:
             members = [(j, which) for which, j0, j1 in group for j in range(j0, j1)]
             da[group] = held([P, len(members), P * PACK], BF16, "da%d_%d" % members[0])
-            words[group] = held([P, len(members), P], U32, "da_words%d_%d" % members[0])
+            if group != SECOND_PAIR_DA3:
+                words[group] = held([P, len(members), P], U32, "da_words%d_%d" % members[0])
             scales[group] = held([P, len(members), P], U8, "da_scales%d_%d" % members[0])
             for n, member in enumerate(members):
                 place[member] = (group, n)
@@ -278,7 +287,7 @@ def tile_moe_bdx_glu_relu_kernel(
                     nc.tensor.matmul_mx(
                         out=acc[:, j - j0, :],
                         lhsT=w[part][:, e, 2 * k0 : 2 * (k0 + P)].bitcast(FP4X4),
-                        lhsT_scale=ws[:, e, kt * P : (kt + 1) * P],
+                        lhsT_scale=ws[part][:, e, k0 : k0 + P],
                         rhs=part_of(words, j, which).bitcast(FP8X4),
                         rhs_scale=part_of(scales, j, which),
                         start=(n == 0),
@@ -290,21 +299,23 @@ def tile_moe_bdx_glu_relu_kernel(
             rectify(e)
             make_mask(e)
             mask_a3(e)
-        w3s = keep.tile([P, E, K], U8, name="w3s", tag="mask_0", align_bytes=64)
-        nc.gpsimd.memset(w3s[:].rearrange("p a n -> p (a n)").bitcast(I32), 0)
+        early_planes = keep.tile([P, 2, E, K // 2], U8, name="early_planes", tag="second_mask", align_bytes=64)
+        nc.gpsimd.memset(early_planes[:].rearrange("p a e n -> p (a e n)").bitcast(I32), 0)
+        w1s, w3s = (early_planes[:, 0], late_w1s), (early_planes[:, 1], late_w3s)
         for j in range(4):
             first_product(j)
         load_w2(2)
         load_saved(a1_of, a1, "a1", 4, 6)
         nc.sync.dma_start(pos1_sb[:], pos1)
         nc.sync.dma_start(pos2_sb[:], pos2)
+        load_part_scales(w1s, w1_scales, 0)
         load_saved(a3_of, a3, "a3", 4, 5)
         for j in range(4):
             turn(j)
         for e in range(POOL_EXPERTS):
             products(e)
-        quantise(POOL_FIRST)
-        quantise(POOL_REST)
+        quantise(FIRST_PAIR_A)
+        quantise(FIRST_PAIR_B)
 
         def prepare(g):
             for e in (2 * g, 2 * g + 1):
@@ -312,35 +323,42 @@ def tile_moe_bdx_glu_relu_kernel(
                     first_product(j)
                     turn(j)
                 rectify(e)
-            for e in (2 * g, 2 * g + 1):
-                make_mask(e)
 
         prepare(1)
-        load_scale_rows(w1s, w1_scales)
+        for j in (6, 7):
+            tile_mask = keep.tile([P, PACK, P], BF16, name="tile_mask", tag="mask_%d" % j, align_bytes=64)
+            nc.scalar.activation(tile_mask[:], half(relu[3], j), ACT.Sign)
+            da1_factor[j] = held([P, PACK, P], F32, "masked_%d" % j)[:]
+            nc.gpsimd.tensor_tensor(da1_factor[j], half(a3_of[3], j), tile_mask[:], ALU.mult)
+        make_mask(2)
+        load_part_scales(w3s, w3_scales, 0)
         load_part_words(w1, w1_words, 0)
-        load_scale_rows(w3s, w3_scales)
         load_part_words(w3, w3_words, 0)
         load_saved(a3_of, a3, "a3", 5, 6)
+        load_part_scales(w1s, w1_scales, 1)
         load_part_words(w1, w1_words, 1)
-        load_part_words(w3, w3_words, 1)
         products(2)
+        product(6, DA3)
+        product(7, DA3)
         product(6, DA1)
         mask_da1(4, 6)
         product(7, DA1)
-        product(6, DA3)
-        mask_da1(6, 8)
-        product(7, DA3)
-        quantise(POOL_SECOND)
-        quantise(MIDDLE_DA3)
+        words[SECOND_PAIR_DA3] = keep.tile([P, 4, P], U32, name="middle_words", tag="mask_7", align_bytes=64)
+        quantise(SECOND_PAIR_DA3)
+        quantise(SECOND_PAIR_DA1)
         prepare(2)
-        for j in range(POOL_TILES, TILES):
+        load_part_scales(w3s, w3_scales, 1)
+        load_part_words(w3, w3_words, 1)
+        make_mask(4)
+        make_mask(5)
+        for j in range(2 * PAIR // P, TILES):
             product(j, DA3)
-        for j in range(POOL_TILES, TILES - 2):
+        for j in range(2 * PAIR // P, TILES - 2):
             product(j, DA1)
         mask_da1(8, 9)
         mask_da1(9, 10)
-        quantise(LATE_DA3)
-        quantise(FIFTH_EXPERT_DA1)
+        quantise(LAST_PAIR_A)
+        quantise(LAST_PAIR_B)
         product(TILES - 2, DA1)
         product(TILES - 1, DA1)
         mask_da1(10, 11)
@@ -366,7 +384,8 @@ def tile_moe_bdx_glu_relu_kernel(
 
         def add_and_store(kt, t0, t1):
             total = row_tile([P, t1 - t0], "total")
-            nc.vector.tensor_tensor(total[:], dx[kt][:].indirect(offsets(pos2_sb, t0, t1)), fetched[kt][:, t0:t1], ALU.add)
+            second = dx[kt][:].indirect(offsets(pos2_sb, t0, t1))
+            nc.vector.tensor_tensor(total[:], second, fetched[kt][:, t0:t1], ALU.add)
             nc.sync.dma_start(out[kt * P : (kt + 1) * P, t0:t1], total[:])
 
         fetch(0)

@@ -37,14 +37,16 @@ POOL_EXPERTS = 2
 DA1, DA3 = 0, 1
 FIRST_PAIR_A = ((DA3, 0, 3), (DA1, 2, 3))
 FIRST_PAIR_B = ((DA1, 0, 2), (DA1, 3, 4), (DA3, 3, 4))
-SECOND_PAIR_DA1 = ((DA1, 4, 8),)
+THIRD_DA1 = ((DA1, 4, 6),)
+FOURTH_DA1 = ((DA1, 6, 8),)
 SECOND_PAIR_DA3 = ((DA3, 4, 8),)
 LAST_PAIR_A = ((DA3, 8, 11), (DA1, 8, 9))
 LAST_PAIR_B = ((DA1, 9, 10), (DA3, 11, 12))
 NEXT_TO_LAST_DA1 = ((DA1, 10, 11),)
 LAST_DA1 = ((DA1, 11, 12),)
 QUANT_GROUPS = (
-    FIRST_PAIR_A, FIRST_PAIR_B, SECOND_PAIR_DA1, SECOND_PAIR_DA3, LAST_PAIR_A, LAST_PAIR_B, NEXT_TO_LAST_DA1, LAST_DA1
+    FIRST_PAIR_A, FIRST_PAIR_B, THIRD_DA1, FOURTH_DA1, SECOND_PAIR_DA3, LAST_PAIR_A, LAST_PAIR_B, NEXT_TO_LAST_DA1,
+    LAST_DA1,
 )
 BANK_GROUPS = ((0, 4), (4, 8), (8, 12))
 FIRST_BANK_GROUPS = ((0, 4), (4, 8), (8, 10), (10, 11), (11, 12))
@@ -82,21 +84,24 @@ def tile_moe_bdx_glu_relu_kernel(
         w3 = [held([P, E, 2 * (k1 - k0)], U8, "w3_%d" % k0) for k0, k1 in WORD_PARTS]
         planes = [held([P, 2 * PASSES * H], U8, "planes_%d" % n) for n in range(2)]
         w2s = [planes[g % 2][:].rearrange("p (a n) -> p a n", n=H) for g in range(PAIRS)]
-        late_w3s, late_w1s = (plane[:, 0 : E * K // 2].rearrange("p (e n) -> p e n", e=E) for plane in planes)
+        w1s = [held([P, E, k1 - k0], U8, "w1s_%d" % k0) for k0, k1 in WORD_PARTS]
+        w3s = [held([P, E, k1 - k0], U8, "w3s_%d" % k0) for k0, k1 in WORD_PARTS]
         dx = [held([P, S], F32, "dx%d" % kt) for kt in range(KT)]
         gate_rows = held([P, P], F32, "gate_rows")
         gate_col = held([P, TILES], F32, "gate_col")
         ident = held([P, P], F32, "ident")
 
         nc.gpsimd.memset(dys[:, 0:T].bitcast(I32), 0)
+        nc.gpsimd.memset(planes[0][:].bitcast(I32), 0)
         nc.gpsimd.memset(gate_rows[:], 0.0)
-        for plane in planes:
-            nc.vector.memset(plane[:].bitcast(I32), 0)
-        for plane in gs[1]:
-            nc.vector.memset(plane[:].bitcast(I32), 0)
-        nc.vector.memset(dyw[:, PASSES * T :], 0)
-        make_identity(nc, ident[:])
         nc.gpsimd.memset(dys[:, T:WIDE].bitcast(I32), 0)
+        nc.gpsimd.memset(gs[1][0][:].bitcast(I32), 0)
+        make_identity(nc, ident[:])
+        nc.gpsimd.memset(gs[1][1][:].bitcast(I32), 0)
+        nc.gpsimd.memset(planes[1][:].bitcast(I32), 0)
+        nc.gpsimd.memset(dyw[:, PASSES * T :], 0)
+        for plane in (w1s[0], w3s[0], w1s[1], w3s[1]):
+            nc.gpsimd.memset(plane[:].rearrange("p e n -> p (e n)").bitcast(I32), 0)
 
         def load_scale_rows(plane, scale_rows):
             rows = scale_rows.rearrange("e s f n -> f (e s) n").bitcast(I32)
@@ -156,12 +161,12 @@ def tile_moe_bdx_glu_relu_kernel(
         nc.vector.tensor_copy(gs[0][0][:], dys[:, 0:T].indirect(offsets(offs_sb, 0, PAIR)))
         move_second_pass(0)
         load_w2_words(0)
-        load_saved(a3_of, a3, "a3", 0, 2)
+        load_saved(a3_of, a3, "a3", 0, 1)
         nc.vector.tensor_copy(gs[0][1][:], dys[:].indirect(offsets(offs_sb, PAIR, S)))
         move_second_pass(1)
         load_w2(1)
+        load_saved(a3_of, a3, "a3", 1, 2)
         load_saved(a1_of, a1, "a1", 2, 4)
-        load_saved(a3_of, a3, "a3", 2, 4)
 
         for part, (first, end, window) in enumerate(((0, PAIR, T), (PAIR, S, WIDE))):
             for o in range(PASSES):
@@ -193,8 +198,8 @@ def tile_moe_bdx_glu_relu_kernel(
                     start=(o == 0),
                     stop=(o == PASSES - 1),
                 )
-            if j // 2 == 3:
-                dh_rows[j] = half(a1_of[j // 2 - 1], j)
+            if j >= TILES - 2:
+                dh_rows[j] = keep.tile([P, PACK, P], F32, name="last_rows", tag="rows%d" % j, align_bytes=64)[:]
             else:
                 dh_rows[j] = row_tile([P, PACK, P], "dh_rows")[:]
             nc.scalar.activation(
@@ -216,14 +221,16 @@ def tile_moe_bdx_glu_relu_kernel(
             return flat.rearrange("p (c i t) -> p c t i", i=RUN, t=PACK)
 
         def rectify(e):
-            relu[e] = ring.tile([P, PACK, C], F32, name="relu", tag="relu", bufs=4, align_bytes=64)[:]
+            relu[e] = ring.tile([P, PACK, C], F32, name="relu", tag="relu", bufs=2, align_bytes=64)[:]
             nc.scalar.activation(relu[e], a1_of[e], ACT.Relu)
 
         def make_mask(e):
             if e == POOL_EXPERTS - 1:
                 mask[e] = keep.tile([P, PACK, C], BF16, name="second_mask", tag="second_mask", align_bytes=64)
+            elif e >= E - 2:
+                mask[e] = keep.tile([P, PACK, C], BF16, name="last_mask", tag="rows%d" % (e + E), align_bytes=64)
             else:
-                mask[e] = ring.tile([P, PACK, C], BF16, name="mask", tag="mask", bufs=3, align_bytes=64)
+                mask[e] = held([P, PACK, C], BF16, "first_mask")
             if e < POOL_EXPERTS:
                 nc.scalar.activation(mask[e][:], relu[e], ACT.Sign)
             else:
@@ -238,8 +245,9 @@ def tile_moe_bdx_glu_relu_kernel(
         place = {}
         for group in QUANT_GROUPS:
             members = [(j, which) for which, j0, j1 in group for j in range(j0, j1)]
-            da[group] = held([P, len(members), P * PACK], BF16, "da%d_%d" % members[0])
-            if group != SECOND_PAIR_DA3:
+            if group != FOURTH_DA1:
+                da[group] = held([P, len(members), P * PACK], BF16, "da%d_%d" % members[0])
+            if group not in (SECOND_PAIR_DA3, FOURTH_DA1):
                 words[group] = held([P, len(members), P], U32, "da_words%d_%d" % members[0])
             scales[group] = held([P, len(members), P], U8, "da_scales%d_%d" % members[0])
             for n, member in enumerate(members):
@@ -275,6 +283,36 @@ def tile_moe_bdx_glu_relu_kernel(
                 in_=da[group][:].rearrange("p j n -> p (j n)"),
             )
 
+        def by_slot(view):
+            return view.rearrange("p t s -> p s t")
+
+        def words_of(flat):
+            return flat.rearrange("p (s t) -> p s t", t=PACK)
+
+        masked_dh = {}
+
+        def tile_cols(flat, j):
+            return words_of(flat[:, (j % 2) * P * PACK : (j % 2 + 1) * P * PACK])
+
+        def rectify_woven(e):
+            relu[e] = held([P, PACK * C], F32, "woven_relu%d" % e)
+            nc.scalar.activation(woven(relu[e][:]), in_runs(a1_of[e]), ACT.Relu)
+
+        def mask_dh(j):
+            nc.vector.scalar_tensor_tensor(
+                tile_cols(masked_dh[j // 2], j), tile_cols(relu[j // 2], j), 0.0, by_slot(dh_cols[j][:]),
+                ALU.is_gt, ALU.mult,
+            )
+
+        def woven_da3(j):
+            nc.vector.tensor_tensor(
+                words_of(part_of(da, j, DA3)), by_slot(dh_cols[j][:]), tile_cols(relu[j // 2], j), ALU.mult
+            )
+
+        def pool_da1(e, group):
+            flat = da[group][:].rearrange("p j n -> p (j n)")
+            nc.gpsimd.tensor_tensor(words_of(flat), words_of(masked_dh[e][:]), by_slot(a3_of[e]), ALU.mult)
+
         def second_product(kt, j0, j1):
             part = kt // 2
             k0 = kt * P - WORD_PARTS[part][0]
@@ -299,17 +337,13 @@ def tile_moe_bdx_glu_relu_kernel(
             rectify(e)
             make_mask(e)
             mask_a3(e)
-        early_planes = keep.tile([P, 2, E, K // 2], U8, name="early_planes", tag="second_mask", align_bytes=64)
-        nc.gpsimd.memset(early_planes[:].rearrange("p a e n -> p (a e n)").bitcast(I32), 0)
-        w1s, w3s = (early_planes[:, 0], late_w1s), (early_planes[:, 1], late_w3s)
         for j in range(4):
             first_product(j)
         load_w2(2)
+        load_saved(a3_of, a3, "a3", 2, 3)
         load_saved(a1_of, a1, "a1", 4, 6)
-        nc.sync.dma_start(pos1_sb[:], pos1)
-        nc.sync.dma_start(pos2_sb[:], pos2)
         load_part_scales(w1s, w1_scales, 0)
-        load_saved(a3_of, a3, "a3", 4, 5)
+        load_saved(a3_of, a3, "a3", 3, 5)
         for j in range(4):
             turn(j)
         for e in range(POOL_EXPERTS):
@@ -318,34 +352,36 @@ def tile_moe_bdx_glu_relu_kernel(
         quantise(FIRST_PAIR_B)
 
         def prepare(g):
+            for j in range(4 * g, 4 * g + 4):
+                first_product(j)
             for e in (2 * g, 2 * g + 1):
-                for j in (2 * e, 2 * e + 1):
-                    first_product(j)
-                    turn(j)
-                rectify(e)
+                (rectify_woven if g == 1 else rectify)(e)
+            for j in range(4 * g, 4 * g + 4):
+                turn(j)
 
         prepare(1)
-        for j in (6, 7):
-            tile_mask = keep.tile([P, PACK, P], BF16, name="tile_mask", tag="mask_%d" % j, align_bytes=64)
-            nc.scalar.activation(tile_mask[:], half(relu[3], j), ACT.Sign)
-            da1_factor[j] = held([P, PACK, P], F32, "masked_%d" % j)[:]
-            nc.gpsimd.tensor_tensor(da1_factor[j], half(a3_of[3], j), tile_mask[:], ALU.mult)
-        make_mask(2)
         load_part_scales(w3s, w3_scales, 0)
         load_part_words(w1, w1_words, 0)
         load_part_words(w3, w3_words, 0)
         load_saved(a3_of, a3, "a3", 5, 6)
+        nc.sync.dma_start(pos1_sb[:], pos1)
+        nc.sync.dma_start(pos2_sb[:], pos2)
         load_part_scales(w1s, w1_scales, 1)
         load_part_words(w1, w1_words, 1)
-        products(2)
-        product(6, DA3)
-        product(7, DA3)
-        product(6, DA1)
-        mask_da1(4, 6)
-        product(7, DA1)
-        words[SECOND_PAIR_DA3] = keep.tile([P, 4, P], U32, name="middle_words", tag="mask_7", align_bytes=64)
+        for e in (2, 3):
+            masked_dh[e] = held([P, PACK * C], F32, "masked_dh%d" % e)
+        mask_dh(4)
+        mask_dh(5)
+        pool_da1(2, THIRD_DA1)
+        for j in range(4, 8):
+            woven_da3(j)
+        mask_dh(6)
+        mask_dh(7)
+        words[SECOND_PAIR_DA3] = keep.tile([P, 4, P], U32, name="middle_words", tag="masked_dh2", align_bytes=64)
         quantise(SECOND_PAIR_DA3)
-        quantise(SECOND_PAIR_DA1)
+        quantise(THIRD_DA1)
+        da[FOURTH_DA1] = keep.tile([P, 2, P * PACK], BF16, name="fourth_da1", tag="da4_0", align_bytes=64)
+        pool_da1(3, FOURTH_DA1)
         prepare(2)
         load_part_scales(w3s, w3_scales, 1)
         load_part_words(w3, w3_words, 1)
@@ -357,6 +393,8 @@ def tile_moe_bdx_glu_relu_kernel(
             product(j, DA1)
         mask_da1(8, 9)
         mask_da1(9, 10)
+        words[FOURTH_DA1] = keep.tile([P, 2, P], U32, name="fourth_words", tag="a3_3", align_bytes=64)
+        quantise(FOURTH_DA1)
         quantise(LAST_PAIR_A)
         quantise(LAST_PAIR_B)
         product(TILES - 2, DA1)
@@ -366,12 +404,8 @@ def tile_moe_bdx_glu_relu_kernel(
         quantise(NEXT_TO_LAST_DA1)
         quantise(LAST_DA1)
 
-        for kt in range(2):
-            for j0, j1 in BANK_GROUPS[:2]:
-                second_product(kt, j0, j1)
-        for j0, j1 in FIRST_BANK_GROUPS[2:]:
-            second_product(0, j0, j1)
-        second_product(1, *BANK_GROUPS[2])
+        for kt, j0, j1 in ((0, 0, 4), (1, 0, 4), (0, 4, 8), (1, 4, 8), (0, 8, 10), (0, 10, 11), (0, 11, 12), (1, 8, 12)):
+            second_product(kt, j0, j1)
         for kt in range(2, KT):
             for j0, j1 in BANK_GROUPS:
                 second_product(kt, j0, j1)

@@ -29,28 +29,10 @@ TILES = S // P
 KT = K // P
 PAIRS = E // 2
 PAIR = 2 * C
-MOVED_ROWS = 3 * QUADRANT + PACK
-WIDE = 1408
+WORD_WINDOW = 1408
+BYTE_WINDOW = 2048
 RUN = 2
-
-POOL_EXPERTS = 2
-DA1, DA3 = 0, 1
-FIRST_PAIR_A = ((DA3, 0, 3), (DA1, 2, 3))
-FIRST_PAIR_B = ((DA1, 0, 2), (DA1, 3, 4), (DA3, 3, 4))
-THIRD_DA1 = ((DA1, 4, 6),)
-FOURTH_DA1 = ((DA1, 6, 8),)
-SECOND_PAIR_DA3 = ((DA3, 4, 8),)
-LAST_PAIR_A = ((DA3, 8, 11), (DA1, 8, 9))
-LAST_PAIR_B = ((DA1, 9, 10), (DA3, 11, 12))
-NEXT_TO_LAST_DA1 = ((DA1, 10, 11),)
-LAST_DA1 = ((DA1, 11, 12),)
-QUANT_GROUPS = (
-    FIRST_PAIR_A, FIRST_PAIR_B, THIRD_DA1, FOURTH_DA1, SECOND_PAIR_DA3, LAST_PAIR_A, LAST_PAIR_B, NEXT_TO_LAST_DA1,
-    LAST_DA1,
-)
-BANK_GROUPS = ((0, 4), (4, 8), (8, 12))
-FIRST_BANK_GROUPS = ((0, 4), (4, 8), (8, 10), (10, 11), (11, 12))
-WORD_PARTS = ((0, K // 2), (K // 2, K))
+PIECE = T // 2
 
 
 def tile_moe_bdx_glu_relu_kernel(
@@ -60,88 +42,69 @@ def tile_moe_bdx_glu_relu_kernel(
     nc = tc.nc
     with ExitStack() as ctx:
         keep = ctx.enter_context(tc.tile_pool(name="keep", bufs=1))
-        ring = ctx.enter_context(tc.tile_pool(name="ring", bufs=3))
-        psum = ctx.enter_context(tc.psum_pool(name="psum", bufs=2))
+        ring = ctx.enter_context(tc.tile_pool(name="ring", bufs=8))
+        psum = ctx.enter_context(tc.psum_pool(name="psum", bufs=4))
 
-        def held(shape, dtype, name):
-            return keep.tile(shape, dtype, name=name, align_bytes=64)
+        def held(shape, dtype, name, tag=None):
+            return keep.tile(shape, dtype, name=name, tag=tag or name, align_bytes=64)
 
         def bank(shape, name, tag):
-            return psum.tile(shape, F32, name=name, tag=tag, bufs=4)
+            return psum.tile(shape, F32, name=name, tag=tag)
 
         def row_tile(shape, name):
-            return ring.tile(shape, F32, name=name, tag="rows", bufs=8, align_bytes=64)
+            return ring.tile(shape, F32, name=name, tag="rows", align_bytes=64)
 
         offs_sb = keep.tile([P, S // PER_COLUMN], U16, name="offs_sb")
         pos1_sb = keep.tile([P, T // PER_COLUMN], U16, name="pos1_sb")
         pos2_sb = keep.tile([P, T // PER_COLUMN], U16, name="pos2_sb")
-        dyw = held([P, T + WIDE], I32, "dyw")
-        dys = held([P, WIDE], U8, "dys")
+        dyw = held([P, T + WORD_WINDOW], I32, "dyw")
+        dys = held([P, BYTE_WINDOW], U8, "dys")
         gw = [[held([P, cols], U32, "gw%d_%d" % (o, cols)) for cols in (PAIR, S - PAIR)] for o in range(PASSES)]
-        gs = [[held([P, cols], U8, "gs%d_%d" % (o, cols)) for cols in (PAIR, S - PAIR)] for o in range(PASSES)]
+        gs = [held([P, S], U8, "gs%d" % o) for o in range(PASSES)]
         w2 = [held([P, 2 * PASSES, 2 * H], U8, "w2_%d" % g) for g in range(PAIRS)]
-        w1 = [held([P, E, 2 * (k1 - k0)], U8, "w1_%d" % k0) for k0, k1 in WORD_PARTS]
-        w3 = [held([P, E, 2 * (k1 - k0)], U8, "w3_%d" % k0) for k0, k1 in WORD_PARTS]
-        planes = [held([P, 2 * PASSES * H], U8, "planes_%d" % n) for n in range(2)]
-        w2s = [planes[g % 2][:].rearrange("p (a n) -> p a n", n=H) for g in range(PAIRS)]
-        w1s = [held([P, E, k1 - k0], U8, "w1s_%d" % k0) for k0, k1 in WORD_PARTS]
-        w3s = [held([P, E, k1 - k0], U8, "w3s_%d" % k0) for k0, k1 in WORD_PARTS]
+        w1 = [held([P, 2, 2 * K], U8, "w1_%d" % g) for g in range(PAIRS)]
+        w3 = [held([P, 2, 2 * K], U8, "w3_%d" % g) for g in range(PAIRS)]
+        w2s = held([P, E * PASSES, H], U8, "w2s")
+        w1s = held([P, E, K], U8, "w1s")
+        w3s = held([P, E, K], U8, "w3s")
         dx = [held([P, S], F32, "dx%d" % kt) for kt in range(KT)]
         gate_rows = held([P, P], F32, "gate_rows")
         gate_col = held([P, TILES], F32, "gate_col")
         ident = held([P, P], F32, "ident")
 
+        def flat(view):
+            return view.rearrange("p a n -> p (a n)")
+
         nc.gpsimd.memset(dys[:, 0:T].bitcast(I32), 0)
-        nc.gpsimd.memset(planes[0][:].bitcast(I32), 0)
+        nc.gpsimd.memset(dys[:, T:].bitcast(I32), 0)
         nc.gpsimd.memset(gate_rows[:], 0.0)
-        nc.gpsimd.memset(dys[:, T:WIDE].bitcast(I32), 0)
-        nc.gpsimd.memset(gs[1][0][:].bitcast(I32), 0)
+        nc.gpsimd.memset(flat(w2s[:]).bitcast(I32), 0)
         make_identity(nc, ident[:])
-        nc.gpsimd.memset(gs[1][1][:].bitcast(I32), 0)
-        nc.gpsimd.memset(planes[1][:].bitcast(I32), 0)
+        nc.gpsimd.memset(gs[1][:].bitcast(I32), 0)
         nc.gpsimd.memset(dyw[:, PASSES * T :], 0)
-        for plane in (w1s[0], w3s[0], w1s[1], w3s[1]):
-            nc.gpsimd.memset(plane[:].rearrange("p e n -> p (e n)").bitcast(I32), 0)
+        for plane in (w3s, w1s):
+            nc.gpsimd.memset(flat(plane[:]).bitcast(I32), 0)
 
         def load_scale_rows(plane, scale_rows):
             rows = scale_rows.rearrange("e s f n -> f (e s) n").bitcast(I32)
             for r in range(PACK):
                 nc.sync.dma_start(plane[r:P:QUADRANT].bitcast(I32), rows[r : PACK * PACK : PACK])
 
+        def load_words(tiles, packed, g):
+            nc.sync.dma_start(
+                tiles[g][:].bitcast(I32), packed[2 * g : 2 * g + 2].rearrange("e s p n -> p (e s) n").bitcast(I32)
+            )
+
         a1_of, a3_of = {}, {}
 
-        def load_saved(views, saved, name, e0, e1):
-            tile = held([P, PACK, (e1 - e0) * C], F32, "%s_%d" % (name, e0))
-            nc.sync.dma_start(tile[:], saved.rearrange("(p t) s -> p t s", t=PACK)[:, :, e0 * C : e1 * C])
-            for e in range(e0, e1):
-                views[e] = tile[:, :, (e - e0) * C : (e - e0 + 1) * C]
-
-        def load_w2_words(g):
-            nc.sync.dma_start(
-                w2[g][:].bitcast(I32), w2_words[2 * g : 2 * g + 2].rearrange("e s p n -> p (e s) n").bitcast(I32)
-            )
-
-        def load_w2(g):
-            load_scale_rows(w2s[g], w2_scales[2 * g : 2 * g + 2])
-            load_w2_words(g)
-
-        def load_part_words(tiles, packed, part):
-            k0, k1 = WORD_PARTS[part]
-            nc.sync.dma_start(
-                tiles[part][:].bitcast(I32), packed[:, 0, :, 2 * k0 : 2 * k1].rearrange("e p n -> p e n").bitcast(I32)
-            )
-
-        def load_part_scales(parts, scale_rows, part):
-            k0, k1 = WORD_PARTS[part]
-            load_scale_rows(parts[part], scale_rows[:, :, :, k0:k1])
+        def load_saved(views, saved, name, g):
+            tile = held([P, PACK, PAIR], F32, "%s_%d" % (name, g))
+            nc.sync.dma_start(tile[:], saved.rearrange("(p t) s -> p t s", t=PACK)[:, :, g * PAIR : (g + 1) * PAIR])
+            for n in range(2):
+                views[2 * g + n] = tile[:, :, n * C : (n + 1) * C]
 
         def offsets(list_sb, first, end):
             return list_sb[:, first // PER_COLUMN : end // PER_COLUMN]
-
-        def move_second_pass(part):
-            nc.sync.dma_start(
-                gs[1][part][0:MOVED_ROWS, :].bitcast(I32), gs[0][part][PACK : PACK + MOVED_ROWS, :].bitcast(I32)
-            )
 
         nc.sync.dma_start(offs_sb[:], offs)
         for q in range(P // QUADRANT):
@@ -149,67 +112,70 @@ def tile_moe_bdx_glu_relu_kernel(
                 dys[QUADRANT * q : QUADRANT * q + PACK * PASSES, 0:T].bitcast(I32),
                 dy_scales[:, PACK * q : PACK * (q + 1), :].bitcast(I32),
             )
-        load_saved(a1_of, a1, "a1", 0, 1)
         nc.sync.dma_start(
             dyw[:, 0 : PASSES * T].rearrange("p (o t) -> p o t", o=PASSES),
             dy_words.rearrange("o p t d -> p o (t d)").bitcast(I32),
         )
         nc.sync.dma_start(gate_rows[0:TILES, :], gate[0].rearrange("(j s) -> j s", s=P))
-        load_saved(a1_of, a1, "a1", 1, 2)
-        load_scale_rows(w2s[0], w2_scales[0:2])
+        load_saved(a1_of, a1, "a1", 0)
+        load_scale_rows(w2s, w2_scales)
+        load_words(w2, w2_words, 0)
 
-        nc.vector.tensor_copy(gs[0][0][:], dys[:, 0:T].indirect(offsets(offs_sb, 0, PAIR)))
-        move_second_pass(0)
-        load_w2_words(0)
-        load_saved(a3_of, a3, "a3", 0, 1)
-        nc.vector.tensor_copy(gs[0][1][:], dys[:].indirect(offsets(offs_sb, PAIR, S)))
-        move_second_pass(1)
-        load_w2(1)
-        load_saved(a3_of, a3, "a3", 1, 2)
-        load_saved(a1_of, a1, "a1", 2, 4)
-
-        for part, (first, end, window) in enumerate(((0, PAIR, T), (PAIR, S, WIDE))):
+        nc.vector.tensor_copy(gs[0][:], dys[:].indirect(offs_sb[:]))
+        for r in range(PACK):
+            nc.sync.dma_start(gs[1][r:P:QUADRANT].bitcast(I32), gs[0][PACK + r : P : QUADRANT].bitcast(I32))
+        for part, (first, end, window) in enumerate(((0, PAIR, T), (PAIR, S, WORD_WINDOW))):
             for o in range(PASSES):
                 nc.vector.tensor_copy(
                     gw[o][part][:], dyw[:, o * T : o * T + window].bitcast(U32).indirect(offsets(offs_sb, first, end))
                 )
 
+        load_saved(a3_of, a3, "a3", 0)
+        load_words(w2, w2_words, 1)
+        load_saved(a1_of, a1, "a1", 1)
+        load_saved(a3_of, a3, "a3", 1)
+        load_words(w2, w2_words, 2)
+        load_saved(a1_of, a1, "a1", 2)
+        load_scale_rows(w3s, w3_scales)
+        load_words(w3, w3_words, 0)
+        load_scale_rows(w1s, w1_scales)
+        load_words(w1, w1_words, 0)
+        load_saved(a3_of, a3, "a3", 2)
+        for g in range(1, PAIRS):
+            load_words(w3, w3_words, g)
+            load_words(w1, w1_words, g)
+        nc.sync.dma_start(pos1_sb[:], pos1)
+        nc.sync.dma_start(pos2_sb[:], pos2)
+
         gate_ps = bank([P, PACK, P], "gate_ps", "turned")
         nc.tensor.transpose(gate_ps[:, 0, :], gate_rows[:], ident[:])
         nc.scalar.copy(gate_col[:], gate_ps[:, 0, 0:TILES])
 
-        dh_rows, dh_cols, relu, mask, da1_factor, da, words, scales = {}, {}, {}, {}, {}, {}, {}, {}
+        dh_cols, relu = {}, {}
 
-        def gathered(tiles, o, j):
-            if j < PAIR // P:
-                return tiles[o][0][:, j * P : (j + 1) * P]
-            return tiles[o][1][:, j * P - PAIR : (j + 1) * P - PAIR]
-
-        def first_product(j):
-            g, second_expert = j // 4, j // 2 % 2
-            acc = bank([P, H], "acc1", "sums")
-            for o in range(PASSES):
-                nc.tensor.matmul_mx(
-                    out=acc[:],
-                    lhsT=gathered(gw, o, j).bitcast(FP8X4),
-                    lhsT_scale=gathered(gs, o, j),
-                    rhs=w2[g][:, second_expert * PASSES + o, :].bitcast(FP4X4),
-                    rhs_scale=w2s[g][:, second_expert * PASSES + o, :],
-                    start=(o == 0),
-                    stop=(o == PASSES - 1),
+        def make_dh(g):
+            rows = {}
+            for j in range(4 * g, 4 * g + 4):
+                part, first = (0, j * P) if g == 0 else (1, j * P - PAIR)
+                acc = bank([P, H], "acc1", "sums")
+                for o in range(PASSES):
+                    nc.tensor.matmul_mx(
+                        out=acc[:],
+                        lhsT=gw[o][part][:, first : first + P].bitcast(FP8X4),
+                        lhsT_scale=gs[o][:, j * P : (j + 1) * P],
+                        rhs=w2[g][:, (j // 2 % 2) * PASSES + o, :].bitcast(FP4X4),
+                        rhs_scale=w2s[:, (j // 2) * PASSES + o, :],
+                        start=(o == 0),
+                        stop=(o == PASSES - 1),
+                    )
+                rows[j] = row_tile([P, PACK, P], "dh_rows")
+                nc.scalar.activation(
+                    rows[j][:], acc[:].rearrange("s (m t) -> s t m", t=PACK), ACT.Copy, scale=gate_col[:, j : j + 1]
                 )
-            if j >= TILES - 2:
-                dh_rows[j] = keep.tile([P, PACK, P], F32, name="last_rows", tag="rows%d" % j, align_bytes=64)[:]
-            else:
-                dh_rows[j] = row_tile([P, PACK, P], "dh_rows")[:]
-            nc.scalar.activation(
-                dh_rows[j], acc[:].rearrange("s (m t) -> s t m", t=PACK), ACT.Copy, scale=gate_col[:, j : j + 1]
-            )
-
-        def turn(j):
-            dh_cols[j] = bank([P, PACK, P], "dh_cols", "turned")
-            for t in range(PACK):
-                nc.tensor.transpose(dh_cols[j][:, t, :], dh_rows[j][:, t, :], ident[:])
+            for j in range(4 * g, 4 * g + 4):
+                dh_cols[j] = bank([P, PACK, P], "dh_cols", "turned")
+                for t in range(PACK):
+                    nc.tensor.transpose(dh_cols[j][:, t, :], rows[j][:, t, :], ident[:])
 
         def half(expert_view, j):
             return expert_view[:, :, (j % 2) * P : (j % 2 + 1) * P]
@@ -217,214 +183,151 @@ def tile_moe_bdx_glu_relu_kernel(
         def in_runs(view):
             return view.rearrange("p t (c i) -> p c t i", i=RUN)
 
-        def woven(flat):
-            return flat.rearrange("p (c i t) -> p c t i", i=RUN, t=PACK)
-
-        def rectify(e):
-            relu[e] = ring.tile([P, PACK, C], F32, name="relu", tag="relu", bufs=2, align_bytes=64)[:]
-            nc.scalar.activation(relu[e], a1_of[e], ACT.Relu)
-
-        def make_mask(e):
-            if e == POOL_EXPERTS - 1:
-                mask[e] = keep.tile([P, PACK, C], BF16, name="second_mask", tag="second_mask", align_bytes=64)
-            elif e >= E - 2:
-                mask[e] = keep.tile([P, PACK, C], BF16, name="last_mask", tag="rows%d" % (e + E), align_bytes=64)
-            else:
-                mask[e] = held([P, PACK, C], BF16, "first_mask")
-            if e < POOL_EXPERTS:
-                nc.scalar.activation(mask[e][:], relu[e], ACT.Sign)
-            else:
-                nc.scalar.activation(woven(mask[e][:].rearrange("p t s -> p (t s)")), in_runs(relu[e]), ACT.Sign)
-
-        def mask_a3(e):
-            masked = held([P, PACK, C], F32, "masked_a3_%d" % e)[:]
-            nc.gpsimd.tensor_tensor(masked, a3_of[e], mask[e][:], ALU.mult)
-            for j in (2 * e, 2 * e + 1):
-                da1_factor[j] = half(masked, j)
-
-        place = {}
-        for group in QUANT_GROUPS:
-            members = [(j, which) for which, j0, j1 in group for j in range(j0, j1)]
-            if group != FOURTH_DA1:
-                da[group] = held([P, len(members), P * PACK], BF16, "da%d_%d" % members[0])
-            if group not in (SECOND_PAIR_DA3, FOURTH_DA1):
-                words[group] = held([P, len(members), P], U32, "da_words%d_%d" % members[0])
-            scales[group] = held([P, len(members), P], U8, "da_scales%d_%d" % members[0])
-            for n, member in enumerate(members):
-                place[member] = (group, n)
-
-        def part_of(tiles, j, which):
-            group, n = place[j, which]
-            return tiles[group][:, n, :]
-
-        def product(j, which):
-            if which == DA3:
-                factor = half(relu[j // 2], j)
-            else:
-                factor = da1_factor[j] if j in da1_factor else half(a3_of[j // 2], j)
-            nc.vector.tensor_tensor(woven(part_of(da, j, which)), in_runs(dh_cols[j][:]), in_runs(factor), ALU.mult)
-
-        def products(e):
-            for which in (DA3, DA1):
-                for j in (2 * e, 2 * e + 1):
-                    product(j, which)
-
-        def mask_da1(j0, j1):
-            group, n = place[j0, DA1]
-            flat = da[group][:, n : n + j1 - j0, :].rearrange("p j n -> p (j n)")
-            first = (j0 % 2) * P * PACK
-            zero_or_one = mask[j0 // 2][:].rearrange("p t s -> p (t s)")[:, first : first + (j1 - j0) * P * PACK]
-            nc.vector.tensor_tensor(flat, flat, zero_or_one, ALU.mult)
-
-        def quantise(group):
-            nc.vector.quantize_mx(
-                out=words[group][:].rearrange("p j n -> p (j n)").bitcast(FP8X4),
-                scales=scales[group][:].rearrange("p j n -> p (j n)"),
-                in_=da[group][:].rearrange("p j n -> p (j n)"),
-            )
+        def woven(view):
+            return view.rearrange("p (c i t) -> p c t i", i=RUN, t=PACK)
 
         def by_slot(view):
             return view.rearrange("p t s -> p s t")
 
-        def words_of(flat):
-            return flat.rearrange("p (s t) -> p s t", t=PACK)
+        def words_of(view):
+            return view.rearrange("p (s t) -> p s t", t=PACK)
 
+        def product(dst, j, factor):
+            nc.vector.tensor_tensor(woven(dst), in_runs(dh_cols[j][:]), in_runs(half(factor, j)), ALU.mult)
+
+        def quantise(words, scales, values):
+            nc.vector.quantize_mx(out=flat(words).bitcast(FP8X4), scales=flat(scales), in_=flat(values))
+
+        da, words, scales = {}, {}, {}
+
+        def second_product(acc, kt, g, n0, n1):
+            e = 2 * g + n0 // 2
+            for first, w, ws in ((0, w3, w3s), (4, w1, w1s)):
+                nc.tensor.matmul_mx(
+                    out=acc,
+                    lhsT=w[g][:, n0 // 2, 2 * kt * P : 2 * (kt + 1) * P].bitcast(FP4X4),
+                    lhsT_scale=ws[:, e, kt * P : (kt + 1) * P],
+                    rhs=flat(words[g, first, n0][:, 0 : n1 - n0, :]).bitcast(FP8X4),
+                    rhs_scale=flat(scales[g, first, n0][:, 0 : n1 - n0, :]),
+                    start=(first == 0),
+                    stop=(first == 4),
+                )
+
+        def name_parts(g, first, n0, n1, word_tile, scale_tile):
+            for n in range(n0, n1):
+                words[g, first, n] = word_tile[:, n - n0 :, :]
+                scales[g, first, n] = scale_tile[:, n - n0 :, :]
+
+        def pair_product(g):
+            for kt in range(KT):
+                acc = bank([P, PAIR], "acc2", "sums")
+                for n in range(2):
+                    second_product(acc[:, n * C : (n + 1) * C], kt, g, 2 * n, 2 * n + 2)
+                nc.scalar.copy(dx[kt][:, g * PAIR : (g + 1) * PAIR], acc[:])
+
+        masked_a3 = {}
+        for e in range(2):
+            relu[e] = held([P, PACK, C], F32, "relu%d" % e)
+            nc.scalar.activation(relu[e][:], a1_of[e], ACT.Relu)
+            mask = held([P, PACK, C], BF16, "mask%d" % e)
+            nc.scalar.activation(mask[:], relu[e][:], ACT.Sign)
+            masked_a3[e] = held([P, PACK, C], F32, "masked%d" % e)
+            nc.gpsimd.tensor_tensor(masked_a3[e][:], a3_of[e], mask[:], ALU.mult)
+        make_dh(0)
+        da3_0 = held([P, 4, P * PACK], BF16, "da3_0")
+        da1_0 = held([P, 4, P * PACK], BF16, "da1_0")
+        for j in range(4):
+            product(da3_0[:, j, :], j, relu[j // 2][:])
+        for j in range(4):
+            product(da1_0[:, j, :], j, masked_a3[j // 2][:])
+        for first, values, tag in ((0, da3_0, "mask1"), (4, da1_0, None)):
+            word_tile = held([P, 4, P], U32, "words0_%d" % first)
+            scale_tile = held([P, 4, P], U8, "scales0_%d" % first, tag)
+            quantise(word_tile[:], scale_tile[:], values[:])
+            name_parts(0, first, 0, 4, word_tile, scale_tile)
+
+        make_dh(1)
+        da[1] = held([P, 8, P * PACK], BF16, "da_1", "a1_0")
         masked_dh = {}
-
-        def tile_cols(flat, j):
-            return words_of(flat[:, (j % 2) * P * PACK : (j % 2 + 1) * P * PACK])
-
-        def rectify_woven(e):
-            relu[e] = held([P, PACK * C], F32, "woven_relu%d" % e)
-            nc.scalar.activation(woven(relu[e][:]), in_runs(a1_of[e]), ACT.Relu)
-
-        def mask_dh(j):
-            nc.vector.scalar_tensor_tensor(
-                tile_cols(masked_dh[j // 2], j), tile_cols(relu[j // 2], j), 0.0, by_slot(dh_cols[j][:]),
-                ALU.is_gt, ALU.mult,
-            )
-
-        def woven_da3(j):
-            nc.vector.tensor_tensor(
-                words_of(part_of(da, j, DA3)), by_slot(dh_cols[j][:]), tile_cols(relu[j // 2], j), ALU.mult
-            )
-
-        def pool_da1(e, group):
-            flat = da[group][:].rearrange("p j n -> p (j n)")
-            nc.gpsimd.tensor_tensor(words_of(flat), words_of(masked_dh[e][:]), by_slot(a3_of[e]), ALU.mult)
-
-        def second_product(kt, j0, j1):
-            part = kt // 2
-            k0 = kt * P - WORD_PARTS[part][0]
-            acc = bank([P, j1 - j0, P], "acc2", "sums")
-            last_first = kt == 1 and j1 == TILES
-            for j in (range(j1 - 1, j0 - 1, -1) if last_first else range(j0, j1)):
-                e = j // 2
-                both = ((DA3, w3, w3s), (DA1, w1, w1s))
-                for n, (which, w, ws) in enumerate(both[::-1] if last_first else both):
-                    nc.tensor.matmul_mx(
-                        out=acc[:, j - j0, :],
-                        lhsT=w[part][:, e, 2 * k0 : 2 * (k0 + P)].bitcast(FP4X4),
-                        lhsT_scale=ws[part][:, e, k0 : k0 + P],
-                        rhs=part_of(words, j, which).bitcast(FP8X4),
-                        rhs_scale=part_of(scales, j, which),
-                        start=(n == 0),
-                        stop=(n == 1),
-                    )
-            nc.scalar.copy(dx[kt][:, j0 * P : j1 * P], acc[:].rearrange("p j s -> p (j s)"))
-
-        for e in range(POOL_EXPERTS):
-            rectify(e)
-            make_mask(e)
-            mask_a3(e)
-        for j in range(4):
-            first_product(j)
-        load_w2(2)
-        load_saved(a3_of, a3, "a3", 2, 3)
-        load_saved(a1_of, a1, "a1", 4, 6)
-        load_part_scales(w1s, w1_scales, 0)
-        load_saved(a3_of, a3, "a3", 3, 5)
-        for j in range(4):
-            turn(j)
-        for e in range(POOL_EXPERTS):
-            products(e)
-        quantise(FIRST_PAIR_A)
-        quantise(FIRST_PAIR_B)
-
-        def prepare(g):
-            for j in range(4 * g, 4 * g + 4):
-                first_product(j)
-            for e in (2 * g, 2 * g + 1):
-                (rectify_woven if g == 1 else rectify)(e)
-            for j in range(4 * g, 4 * g + 4):
-                turn(j)
-
-        prepare(1)
-        load_part_scales(w3s, w3_scales, 0)
-        load_part_words(w1, w1_words, 0)
-        load_part_words(w3, w3_words, 0)
-        load_saved(a3_of, a3, "a3", 5, 6)
-        nc.sync.dma_start(pos1_sb[:], pos1)
-        nc.sync.dma_start(pos2_sb[:], pos2)
-        load_part_scales(w1s, w1_scales, 1)
-        load_part_words(w1, w1_words, 1)
         for e in (2, 3):
-            masked_dh[e] = held([P, PACK * C], F32, "masked_dh%d" % e)
-        mask_dh(4)
-        mask_dh(5)
-        pool_da1(2, THIRD_DA1)
+            relu[e] = held([P, 2, P * PACK], F32, "relu%d" % e)
+            nc.scalar.activation(woven(flat(relu[e][:])), in_runs(a1_of[e]), ACT.Relu)
+            masked_dh[e] = held([P, 2, P * PACK], F32, "masked_dh%d" % e, "masked%d" % (e - 2))
+            for j in (2 * e, 2 * e + 1):
+                nc.vector.scalar_tensor_tensor(
+                    words_of(masked_dh[e][:, j % 2, :]), words_of(relu[e][:, j % 2, :]), 0.0, by_slot(dh_cols[j][:]),
+                    ALU.is_gt, ALU.mult,
+                )
+            nc.gpsimd.tensor_tensor(
+                words_of(flat(da[1][:, 2 * e : 2 * e + 2, :])), words_of(flat(masked_dh[e][:])), by_slot(a3_of[e]),
+                ALU.mult,
+            )
         for j in range(4, 8):
-            woven_da3(j)
-        mask_dh(6)
-        mask_dh(7)
-        words[SECOND_PAIR_DA3] = keep.tile([P, 4, P], U32, name="middle_words", tag="masked_dh2", align_bytes=64)
-        quantise(SECOND_PAIR_DA3)
-        quantise(THIRD_DA1)
-        da[FOURTH_DA1] = keep.tile([P, 2, P * PACK], BF16, name="fourth_da1", tag="da4_0", align_bytes=64)
-        pool_da1(3, FOURTH_DA1)
-        prepare(2)
-        load_part_scales(w3s, w3_scales, 1)
-        load_part_words(w3, w3_words, 1)
-        make_mask(4)
-        make_mask(5)
-        for j in range(2 * PAIR // P, TILES):
-            product(j, DA3)
-        for j in range(2 * PAIR // P, TILES - 2):
-            product(j, DA1)
-        mask_da1(8, 9)
-        mask_da1(9, 10)
-        words[FOURTH_DA1] = keep.tile([P, 2, P], U32, name="fourth_words", tag="a3_3", align_bytes=64)
-        quantise(FOURTH_DA1)
-        quantise(LAST_PAIR_A)
-        quantise(LAST_PAIR_B)
-        product(TILES - 2, DA1)
-        product(TILES - 1, DA1)
-        mask_da1(10, 11)
-        mask_da1(11, 12)
-        quantise(NEXT_TO_LAST_DA1)
-        quantise(LAST_DA1)
+            nc.vector.tensor_tensor(
+                words_of(da[1][:, j - 4, :]), by_slot(dh_cols[j][:]), words_of(relu[j // 2][:, j % 2, :]), ALU.mult
+            )
 
-        for kt, j0, j1 in ((0, 0, 4), (1, 0, 4), (0, 4, 8), (1, 4, 8), (0, 8, 10), (0, 10, 11), (0, 11, 12), (1, 8, 12)):
-            second_product(kt, j0, j1)
-        for kt in range(2, KT):
-            for j0, j1 in BANK_GROUPS:
-                second_product(kt, j0, j1)
+        make_dh(2)
+        last_mask = {}
+        for e in (4, 5):
+            relu[e] = held([P, PACK, C], F32, "relu%d" % e, "relu%d" % (e - 4))
+            nc.scalar.activation(relu[e][:], a1_of[e], ACT.Relu)
+        for e in (4, 5):
+            last_mask[e] = held([P, 2, P * PACK], BF16, "mask%d" % e)
+            nc.scalar.activation(woven(flat(last_mask[e][:])), in_runs(relu[e][:]), ACT.Sign)
+        pair_product(0)
+        da3_2 = held([P, 4, P * PACK], BF16, "da3_2", "da3_0")
+        da1_2 = held([P, 4, P * PACK], BF16, "da1_2", "da1_0")
+        for j in range(8, 12):
+            product(da3_2[:, j - 8, :], j, relu[j // 2][:])
 
-        fetched = {}
+        word_tile = held([P, 8, P], U32, "words1")
+        scale_tile = held([P, 8, P], U8, "scales1", "relu1")
+        quantise(word_tile[:], scale_tile[:], da[1][:])
+        name_parts(1, 0, 0, 4, word_tile, scale_tile)
+        name_parts(1, 4, 0, 4, word_tile[:, 4:, :], scale_tile[:, 4:, :])
+        pair_product(1)
 
-        def fetch(kt):
-            fetched[kt] = row_tile([P, T], "first")
-            nc.vector.tensor_copy(fetched[kt][:], dx[kt][:].indirect(pos1_sb[:]))
+        def quantise_last(first, values, n0, n1):
+            word_tile = held([P, n1 - n0, P], U32, "words2_%d_%d" % (first, n0))
+            scale_tile = held([P, n1 - n0, P], U8, "scales2_%d_%d" % (first, n0))
+            quantise(word_tile[:], scale_tile[:], values[:, n0:n1, :])
+            name_parts(2, first, n0, n1, word_tile, scale_tile)
 
-        def add_and_store(kt, t0, t1):
-            total = row_tile([P, t1 - t0], "total")
-            second = dx[kt][:].indirect(offsets(pos2_sb, t0, t1))
-            nc.vector.tensor_tensor(total[:], second, fetched[kt][:, t0:t1], ALU.add)
-            nc.sync.dma_start(out[kt * P : (kt + 1) * P, t0:t1], total[:])
+        def lay_mask(n0, n1):
+            values = flat(da1_2[:, n0:n1, :])
+            zero_or_one = flat(last_mask[4 + n0 // 2][:, n0 % 2 : n0 % 2 + n1 - n0, :])
+            nc.vector.tensor_tensor(values, values, zero_or_one, ALU.mult)
 
-        fetch(0)
-        for kt in range(KT - 1):
-            fetch(kt + 1)
-            add_and_store(kt, 0, T)
-        add_and_store(KT - 1, 0, 2 * T // 3)
-        add_and_store(KT - 1, 2 * T // 3, T)
+        quantise_last(0, da3_2, 0, 4)
+        product(da1_2[:, 0, :], 8, a3_of[4])
+        product(da1_2[:, 1, :], 9, a3_of[4])
+        product(da1_2[:, 2, :], 10, a3_of[5])
+        lay_mask(0, 2)
+        product(da1_2[:, 3, :], 11, a3_of[5])
+        quantise_last(4, da1_2, 0, 2)
+        lay_mask(2, 3)
+        lay_mask(3, 4)
+        quantise_last(4, da1_2, 2, 3)
+        quantise_last(4, da1_2, 3, 4)
+
+        for kt in range(KT):
+            acc = bank([P, C], "acc4", "sums")
+            second_product(acc[:], kt, 2, 0, 2)
+            nc.scalar.copy(dx[kt][:, S - PAIR : S - C], acc[:])
+        last = [bank([P, 2, P], "acc5", "turned") for kt in range(KT)]
+        for n in (2, 3):
+            for kt in range(KT):
+                second_product(last[kt][:, n - 2, :], kt, 2, n, n + 1)
+        nc.scalar.copy(dx[0][:, S - C :], flat(last[0][:]))
+        for kt in range(1, KT):
+            nc.vector.tensor_copy(dx[kt][:, S - C :], flat(last[kt][:]))
+
+        for kt in range(KT):
+            for t0 in range(0, T, PIECE):
+                first = row_tile([P, PIECE], "first")
+                nc.scalar.activation(first[:], dx[kt][:].indirect(offsets(pos1_sb, t0, t0 + PIECE)), ACT.Copy)
+                total = row_tile([P, PIECE], "total")
+                second = dx[kt][:].indirect(offsets(pos2_sb, t0, t0 + PIECE))
+                nc.vector.tensor_tensor(total[:], second, first[:], ALU.add)
+                nc.sync.dma_start(out[kt * P : (kt + 1) * P, t0 : t0 + PIECE], total[:])

@@ -62,8 +62,6 @@ def tile_moe_bdx_glu_relu_kernel(
         gw = [[held([P, cols], U32, "gw%d_%d" % (o, cols)) for cols in (PAIR, S - PAIR)] for o in range(PASSES)]
         gs = [held([P, S], U8, "gs%d" % o) for o in range(PASSES)]
         w2 = [held([P, 2 * PASSES, 2 * H], U8, "w2_%d" % g) for g in range(PAIRS)]
-        w1 = [held([P, 2, 2 * K], U8, "w1_%d" % g) for g in range(PAIRS)]
-        w3 = [held([P, 2, 2 * K], U8, "w3_%d" % g) for g in range(PAIRS)]
         w2s = held([P, E * PASSES, H], U8, "w2s")
         w1s = held([P, E, K], U8, "w1s")
         w3s = held([P, E, K], U8, "w3s")
@@ -95,13 +93,26 @@ def tile_moe_bdx_glu_relu_kernel(
                 tiles[g][:].bitcast(I32), packed[2 * g : 2 * g + 2].rearrange("e s p n -> p (e s) n").bitcast(I32)
             )
 
+        w1, w3 = {}, {}
+
+        def load_second_words(e0, e1, kt0, kt1):
+            for views, packed, name in ((w3, w3_words, "w3"), (w1, w1_words, "w1")):
+                if e0 == 0:
+                    load_scale_rows(*{"w3": (w3s, w3_scales), "w1": (w1s, w1_scales)}[name])
+                tile = held([P, e1 - e0, 2 * P * (kt1 - kt0)], U8, "%s_%d_%d" % (name, e0, kt0))
+                rows = packed[e0:e1, 0, :, 2 * P * kt0 : 2 * P * kt1].rearrange("e p n -> p e n")
+                nc.sync.dma_start(tile[:].bitcast(I32), rows.bitcast(I32))
+                for e in range(e0, e1):
+                    for kt in range(kt0, kt1):
+                        views[e, kt] = tile[:, e - e0, 2 * P * (kt - kt0) : 2 * P * (kt - kt0 + 1)]
+
         a1_of, a3_of = {}, {}
 
-        def load_saved(views, saved, name, g):
-            tile = held([P, PACK, PAIR], F32, "%s_%d" % (name, g))
-            nc.sync.dma_start(tile[:], saved.rearrange("(p t) s -> p t s", t=PACK)[:, :, g * PAIR : (g + 1) * PAIR])
-            for n in range(2):
-                views[2 * g + n] = tile[:, :, n * C : (n + 1) * C]
+        def load_saved(views, saved, name, e0, e1):
+            tile = held([P, PACK, (e1 - e0) * C], F32, "%s_%d" % (name, e0))
+            nc.sync.dma_start(tile[:], saved.rearrange("(p t) s -> p t s", t=PACK)[:, :, e0 * C : e1 * C])
+            for e in range(e0, e1):
+                views[e] = tile[:, :, (e - e0) * C : (e - e0 + 1) * C]
 
         def offsets(list_sb, first, end):
             return list_sb[:, first // PER_COLUMN : end // PER_COLUMN]
@@ -117,7 +128,7 @@ def tile_moe_bdx_glu_relu_kernel(
             dy_words.rearrange("o p t d -> p o (t d)").bitcast(I32),
         )
         nc.sync.dma_start(gate_rows[0:TILES, :], gate[0].rearrange("(j s) -> j s", s=P))
-        load_saved(a1_of, a1, "a1", 0)
+        load_saved(a1_of, a1, "a1", 0, 2)
         load_scale_rows(w2s, w2_scales)
         load_words(w2, w2_words, 0)
 
@@ -130,22 +141,20 @@ def tile_moe_bdx_glu_relu_kernel(
                     gw[o][part][:], dyw[:, o * T : o * T + window].bitcast(U32).indirect(offsets(offs_sb, first, end))
                 )
 
-        load_saved(a3_of, a3, "a3", 0)
+        load_saved(a3_of, a3, "a3", 0, 2)
         load_words(w2, w2_words, 1)
-        load_saved(a1_of, a1, "a1", 1)
-        load_saved(a3_of, a3, "a3", 1)
-        load_words(w2, w2_words, 2)
-        load_saved(a1_of, a1, "a1", 2)
-        load_scale_rows(w3s, w3_scales)
-        load_words(w3, w3_words, 0)
-        load_scale_rows(w1s, w1_scales)
-        load_words(w1, w1_words, 0)
-        load_saved(a3_of, a3, "a3", 2)
-        for g in range(1, PAIRS):
-            load_words(w3, w3_words, g)
-            load_words(w1, w1_words, g)
+        load_saved(a1_of, a1, "a1", 2, 4)
         nc.sync.dma_start(pos1_sb[:], pos1)
+        load_saved(a3_of, a3, "a3", 2, 4)
         nc.sync.dma_start(pos2_sb[:], pos2)
+        load_words(w2, w2_words, 2)
+        load_saved(a1_of, a1, "a1", 4, 6)
+        load_second_words(0, 2, 0, KT)
+        load_saved(a3_of, a3, "a3", 4, 5)
+        load_saved(a3_of, a3, "a3", 5, 6)
+        load_second_words(2, 4, 0, KT // 2)
+        load_second_words(4, 6, 0, KT // 2)
+        load_second_words(2, 6, KT // 2, KT)
 
         gate_ps = bank([P, PACK, P], "gate_ps", "turned")
         nc.tensor.transpose(gate_ps[:, 0, :], gate_rows[:], ident[:])
@@ -205,7 +214,7 @@ def tile_moe_bdx_glu_relu_kernel(
             for first, w, ws in ((0, w3, w3s), (4, w1, w1s)):
                 nc.tensor.matmul_mx(
                     out=acc,
-                    lhsT=w[g][:, n0 // 2, 2 * kt * P : 2 * (kt + 1) * P].bitcast(FP4X4),
+                    lhsT=w[e, kt].bitcast(FP4X4),
                     lhsT_scale=ws[:, e, kt * P : (kt + 1) * P],
                     rhs=flat(words[g, first, n0][:, 0 : n1 - n0, :]).bitcast(FP8X4),
                     rhs_scale=flat(scales[g, first, n0][:, 0 : n1 - n0, :]),
@@ -218,12 +227,11 @@ def tile_moe_bdx_glu_relu_kernel(
                 words[g, first, n] = word_tile[:, n - n0 :, :]
                 scales[g, first, n] = scale_tile[:, n - n0 :, :]
 
-        def pair_product(g):
-            for kt in range(KT):
-                acc = bank([P, PAIR], "acc2", "sums")
-                for n in range(2):
-                    second_product(acc[:, n * C : (n + 1) * C], kt, g, 2 * n, 2 * n + 2)
-                nc.scalar.copy(dx[kt][:, g * PAIR : (g + 1) * PAIR], acc[:])
+        def pair_product(g, kt, tag, empty):
+            acc = bank([P, 4, P], "acc2", tag)
+            for n0, n1 in ((0, 2), (2, 3), (3, 4)) if g == PAIRS - 1 else ((0, 2), (2, 4)):
+                second_product(flat(acc[:, n0:n1, :]), kt, g, n0, n1)
+            empty(dx[kt][:, g * PAIR : (g + 1) * PAIR], flat(acc[:]))
 
         masked_a3 = {}
         for e in range(2):
@@ -275,7 +283,8 @@ def tile_moe_bdx_glu_relu_kernel(
         for e in (4, 5):
             last_mask[e] = held([P, 2, P * PACK], BF16, "mask%d" % e)
             nc.scalar.activation(woven(flat(last_mask[e][:])), in_runs(relu[e][:]), ACT.Sign)
-        pair_product(0)
+        for kt in range(KT):
+            pair_product(0, kt, "sums", nc.scalar.copy)
         da3_2 = held([P, 4, P * PACK], BF16, "da3_2", "da3_0")
         da1_2 = held([P, 4, P * PACK], BF16, "da1_2", "da1_0")
         for j in range(8, 12):
@@ -286,7 +295,8 @@ def tile_moe_bdx_glu_relu_kernel(
         quantise(word_tile[:], scale_tile[:], da[1][:])
         name_parts(1, 0, 0, 4, word_tile, scale_tile)
         name_parts(1, 4, 0, 4, word_tile[:, 4:, :], scale_tile[:, 4:, :])
-        pair_product(1)
+        for kt in range(KT // 2):
+            pair_product(1, kt, "sums", nc.scalar.copy)
 
         def quantise_last(first, values, n0, n1):
             word_tile = held([P, n1 - n0, P], U32, "words2_%d_%d" % (first, n0))
@@ -311,23 +321,38 @@ def tile_moe_bdx_glu_relu_kernel(
         quantise_last(4, da1_2, 2, 3)
         quantise_last(4, da1_2, 3, 4)
 
-        for kt in range(KT):
-            acc = bank([P, C], "acc4", "sums")
-            second_product(acc[:], kt, 2, 0, 2)
-            nc.scalar.copy(dx[kt][:, S - PAIR : S - C], acc[:])
-        last = [bank([P, 2, P], "acc5", "turned") for kt in range(KT)]
-        for n in (2, 3):
-            for kt in range(KT):
-                second_product(last[kt][:, n - 2, :], kt, 2, n, n + 1)
-        nc.scalar.copy(dx[0][:, S - C :], flat(last[0][:]))
-        for kt in range(1, KT):
-            nc.vector.tensor_copy(dx[kt][:, S - C :], flat(last[kt][:]))
+        def last_product(kt, n0, n1, tag, empty):
+            acc = bank([P, n1 - n0, P], "acc_last", tag)
+            for m0, m1 in ((0, 2), (2, 3), (3, 4)):
+                if n0 <= m0 < n1:
+                    second_product(flat(acc[:, m0 - n0 : m1 - n0, :]), kt, 2, m0, m1)
+            empty(dx[kt][:, S - PAIR + n0 * P : S - PAIR + n1 * P], flat(acc[:]))
 
-        for kt in range(KT):
-            for t0 in range(0, T, PIECE):
-                first = row_tile([P, PIECE], "first")
-                nc.scalar.activation(first[:], dx[kt][:].indirect(offsets(pos1_sb, t0, t0 + PIECE)), ACT.Copy)
-                total = row_tile([P, PIECE], "total")
-                second = dx[kt][:].indirect(offsets(pos2_sb, t0, t0 + PIECE))
-                nc.vector.tensor_tensor(total[:], second, first[:], ALU.add)
-                nc.sync.dma_start(out[kt * P : (kt + 1) * P, t0 : t0 + PIECE], total[:])
+        last_product(0, 0, 2, "turned", nc.scalar.copy)
+        last_product(1, 0, 2, "turned", nc.vector.tensor_copy)
+        last_product(0, 2, 3, "turned", nc.scalar.copy)
+        last_product(0, 3, 4, "turned", nc.scalar.copy)
+        last_product(1, 2, 4, "sums", nc.scalar.copy)
+
+        def fetch(kt, t0, t1):
+            first = row_tile([P, t1 - t0], "first")
+            window = dx[kt][:].indirect(offsets(pos1_sb, t0, t1))
+            if kt == 0:
+                nc.vector.tensor_copy(first[:], window)
+            else:
+                nc.scalar.activation(first[:], window, ACT.Copy)
+            return first
+
+        def add_and_store(kt, t0, t1, first):
+            total = row_tile([P, t1 - t0], "total")
+            second = dx[kt][:].indirect(offsets(pos2_sb, t0, t1))
+            nc.vector.tensor_tensor(total[:], second, first, ALU.add)
+            nc.sync.dma_start(out[kt * P : (kt + 1) * P, t0:t1], total[:])
+
+        for kt, cuts in enumerate(((0, T // 2, T), (0, T), (0, T), (0, T // 3, 2 * T // 3, T))):
+            if kt >= KT // 2:
+                for g in range(1, PAIRS):
+                    pair_product(g, kt, "sums", nc.scalar.copy)
+            pieces = [(t0, t1, fetch(kt, t0, t1)) for t0, t1 in zip(cuts, cuts[1:])]
+            for t0, t1, first in pieces:
+                add_and_store(kt, t0, t1, first[:])

@@ -62,7 +62,7 @@ def tile_moe_bdx_glu_relu_kernel(
         gw = [[held([P, cols], U32, "gw%d_%d" % (o, cols)) for cols in (PAIR, S - PAIR)] for o in range(PASSES)]
         gs = [held([P, S], U8, "gs%d" % o) for o in range(PASSES)]
         w2 = [held([P, 2 * PASSES, 2 * H], U8, "w2_%d" % g) for g in range(PAIRS)]
-        w2s = held([P, E * PASSES, H], U8, "w2s")
+        w2s = [held([P, 2 * PASSES, H], U8, "w2s_%d" % g) for g in range(PAIRS)]
         w1s = held([P, E, K], U8, "w1s")
         w3s = held([P, E, K], U8, "w3s")
         dx = [held([P, S], F32, "dx%d" % kt) for kt in range(KT)]
@@ -76,11 +76,11 @@ def tile_moe_bdx_glu_relu_kernel(
         nc.gpsimd.memset(dys[:, 0:T].bitcast(I32), 0)
         nc.gpsimd.memset(dys[:, T:].bitcast(I32), 0)
         nc.gpsimd.memset(gate_rows[:], 0.0)
-        nc.gpsimd.memset(flat(w2s[:]).bitcast(I32), 0)
+        nc.gpsimd.memset(flat(w2s[0][:]).bitcast(I32), 0)
         make_identity(nc, ident[:])
         nc.gpsimd.memset(gs[1][:].bitcast(I32), 0)
         nc.gpsimd.memset(dyw[:, PASSES * T :], 0)
-        for plane in (w3s, w1s):
+        for plane in (w2s[1], w2s[2], w3s, w1s):
             nc.gpsimd.memset(flat(plane[:]).bitcast(I32), 0)
 
         def load_scale_rows(plane, scale_rows):
@@ -129,7 +129,7 @@ def tile_moe_bdx_glu_relu_kernel(
         )
         nc.sync.dma_start(gate_rows[0:TILES, :], gate[0].rearrange("(j s) -> j s", s=P))
         load_saved(a1_of, a1, "a1", 0, 2)
-        load_scale_rows(w2s, w2_scales)
+        load_scale_rows(w2s[0], w2_scales[0:2])
         load_words(w2, w2_words, 0)
 
         nc.vector.tensor_copy(gs[0][:], dys[:].indirect(offs_sb[:]))
@@ -142,19 +142,19 @@ def tile_moe_bdx_glu_relu_kernel(
                 )
 
         load_saved(a3_of, a3, "a3", 0, 2)
+        load_scale_rows(w2s[1], w2_scales[2:4])
         load_words(w2, w2_words, 1)
         load_saved(a1_of, a1, "a1", 2, 4)
         nc.sync.dma_start(pos1_sb[:], pos1)
         load_saved(a3_of, a3, "a3", 2, 4)
-        nc.sync.dma_start(pos2_sb[:], pos2)
+        load_scale_rows(w2s[2], w2_scales[4:6])
         load_words(w2, w2_words, 2)
+        nc.sync.dma_start(pos2_sb[:], pos2)
         load_saved(a1_of, a1, "a1", 4, 6)
         load_second_words(0, 2, 0, KT)
-        load_saved(a3_of, a3, "a3", 4, 5)
-        load_saved(a3_of, a3, "a3", 5, 6)
-        load_second_words(2, 4, 0, KT // 2)
-        load_second_words(4, 6, 0, KT // 2)
-        load_second_words(2, 6, KT // 2, KT)
+        load_saved(a3_of, a3, "a3", 4, 6)
+        load_second_words(2, 4, 0, KT)
+        load_second_words(4, 6, 0, KT)
 
         gate_ps = bank([P, PACK, P], "gate_ps", "turned")
         nc.tensor.transpose(gate_ps[:, 0, :], gate_rows[:], ident[:])
@@ -173,7 +173,7 @@ def tile_moe_bdx_glu_relu_kernel(
                         lhsT=gw[o][part][:, first : first + P].bitcast(FP8X4),
                         lhsT_scale=gs[o][:, j * P : (j + 1) * P],
                         rhs=w2[g][:, (j // 2 % 2) * PASSES + o, :].bitcast(FP4X4),
-                        rhs_scale=w2s[:, (j // 2) * PASSES + o, :],
+                        rhs_scale=w2s[g][:, (j // 2 % 2) * PASSES + o, :],
                         start=(o == 0),
                         stop=(o == PASSES - 1),
                     )
@@ -207,7 +207,7 @@ def tile_moe_bdx_glu_relu_kernel(
         def quantise(words, scales, values):
             nc.vector.quantize_mx(out=flat(words).bitcast(FP8X4), scales=flat(scales), in_=flat(values))
 
-        da, words, scales = {}, {}, {}
+        words, scales = {}, {}
 
         def second_product(acc, kt, g, n0, n1):
             e = 2 * g + n0 // 2
@@ -233,69 +233,89 @@ def tile_moe_bdx_glu_relu_kernel(
                 second_product(flat(acc[:, n0:n1, :]), kt, g, n0, n1)
             empty(dx[kt][:, g * PAIR : (g + 1) * PAIR], flat(acc[:]))
 
-        masked_a3 = {}
-        for e in range(2):
-            relu[e] = held([P, PACK, C], F32, "relu%d" % e)
-            nc.scalar.activation(relu[e][:], a1_of[e], ACT.Relu)
-            mask = held([P, PACK, C], BF16, "mask%d" % e)
-            nc.scalar.activation(mask[:], relu[e][:], ACT.Sign)
-            masked_a3[e] = held([P, PACK, C], F32, "masked%d" % e)
-            nc.gpsimd.tensor_tensor(masked_a3[e][:], a3_of[e], mask[:], ALU.mult)
-        make_dh(0)
-        da3_0 = held([P, 4, P * PACK], BF16, "da3_0")
-        da1_0 = held([P, 4, P * PACK], BF16, "da1_0")
-        for j in range(4):
-            product(da3_0[:, j, :], j, relu[j // 2][:])
-        for j in range(4):
-            product(da1_0[:, j, :], j, masked_a3[j // 2][:])
-        for first, values, tag in ((0, da3_0, "mask1"), (4, da1_0, None)):
-            word_tile = held([P, 4, P], U32, "words0_%d" % first)
-            scale_tile = held([P, 4, P], U8, "scales0_%d" % first, tag)
-            quantise(word_tile[:], scale_tile[:], values[:])
-            name_parts(0, first, 0, 4, word_tile, scale_tile)
-
-        make_dh(1)
-        da[1] = held([P, 8, P * PACK], BF16, "da_1", "a1_0")
         masked_dh = {}
-        for e in (2, 3):
+
+        def rectify_woven(e):
             relu[e] = held([P, 2, P * PACK], F32, "relu%d" % e)
             nc.scalar.activation(woven(flat(relu[e][:])), in_runs(a1_of[e]), ACT.Relu)
-            masked_dh[e] = held([P, 2, P * PACK], F32, "masked_dh%d" % e, "masked%d" % (e - 2))
+
+        def mask_dh(e):
+            masked_dh[e] = held([P, 2, P * PACK], F32, "masked_dh%d" % e)
             for j in (2 * e, 2 * e + 1):
                 nc.vector.scalar_tensor_tensor(
                     words_of(masked_dh[e][:, j % 2, :]), words_of(relu[e][:, j % 2, :]), 0.0, by_slot(dh_cols[j][:]),
                     ALU.is_gt, ALU.mult,
                 )
-            nc.gpsimd.tensor_tensor(
-                words_of(flat(da[1][:, 2 * e : 2 * e + 2, :])), words_of(flat(masked_dh[e][:])), by_slot(a3_of[e]),
-                ALU.mult,
-            )
-        for j in range(4, 8):
-            nc.vector.tensor_tensor(
-                words_of(da[1][:, j - 4, :]), by_slot(dh_cols[j][:]), words_of(relu[j // 2][:, j % 2, :]), ALU.mult
-            )
 
-        make_dh(2)
+        def pool_da1(dst, e):
+            nc.gpsimd.tensor_tensor(words_of(flat(dst)), words_of(flat(masked_dh[e][:])), by_slot(a3_of[e]), ALU.mult)
+
+        def woven_da3(dst, e):
+            for n in range(2):
+                nc.vector.tensor_tensor(
+                    words_of(dst[:, n, :]), by_slot(dh_cols[2 * e + n][:]), words_of(relu[e][:, n, :]), ALU.mult
+                )
+
+        for e in range(2):
+            rectify_woven(e)
+        make_dh(0)
+        da_0 = held([P, 8, P * PACK], BF16, "da_0", "a1_0")
+        for e in range(2):
+            mask_dh(e)
+            pool_da1(da_0[:, 4 + 2 * e : 6 + 2 * e, :], e)
+        for e in range(2):
+            woven_da3(da_0[:, 2 * e : 2 * e + 2, :], e)
+
+        def quantise_parts(values, name, parts, scale_tag=None):
+            word_tile = held([P, values.shape[1], P], U32, "words_" + name)
+            scale_tile = held([P, values.shape[1], P], U8, "scales_" + name, scale_tag)
+            quantise(word_tile[:], scale_tile[:], values[:])
+            at = 0
+            for g, first, n0, n1 in parts:
+                name_parts(g, first, n0, n1, word_tile[:, at:, :], scale_tile[:, at:, :])
+                at = at + n1 - n0
+
         last_mask = {}
-        for e in (4, 5):
-            relu[e] = held([P, PACK, C], F32, "relu%d" % e, "relu%d" % (e - 4))
+
+        def rectify(e, tag):
+            relu[e] = held([P, PACK, C], F32, "relu%d" % e, tag)
             nc.scalar.activation(relu[e][:], a1_of[e], ACT.Relu)
-        for e in (4, 5):
+
+        def make_mask(e):
             last_mask[e] = held([P, 2, P * PACK], BF16, "mask%d" % e)
             nc.scalar.activation(woven(flat(last_mask[e][:])), in_runs(relu[e][:]), ACT.Sign)
+
+        make_dh(1)
+        rectify_woven(2)
+        rectify(3, None)
+        make_mask(3)
+        wide = held([P, 8, P * PACK], BF16, "wide")
+        mask_dh(2)
+        woven_da3(wide[:, 0:2, :], 2)
+        for j in (6, 7):
+            product(wide[:, j - 4, :], j, relu[3][:])
+        for j in (6, 7):
+            product(wide[:, j - 2, :], j, a3_of[3])
+        nc.vector.tensor_tensor(flat(wide[:, 4:6, :]), flat(wide[:, 4:6, :]), flat(last_mask[3][:]), ALU.mult)
+        quantise_parts(da_0, "first", ((0, 0, 0, 4), (0, 4, 0, 4)), "relu3")
+        late = held([P, 4, P * PACK], BF16, "late", "a1_0")
+        pool_da1(late[:, 0:2, :], 2)
+
+        make_dh(2)
+        for e in (4, 5):
+            rectify(e, "relu%d" % (e - 4))
+        for e in (4, 5):
+            make_mask(e)
         for kt in range(KT):
             pair_product(0, kt, "sums", nc.scalar.copy)
-        da3_2 = held([P, 4, P * PACK], BF16, "da3_2", "da3_0")
-        da1_2 = held([P, 4, P * PACK], BF16, "da1_2", "da1_0")
-        for j in range(8, 12):
-            product(da3_2[:, j - 8, :], j, relu[j // 2][:])
-
-        word_tile = held([P, 8, P], U32, "words1")
-        scale_tile = held([P, 8, P], U8, "scales1", "relu1")
-        quantise(word_tile[:], scale_tile[:], da[1][:])
-        name_parts(1, 0, 0, 4, word_tile, scale_tile)
-        name_parts(1, 4, 0, 4, word_tile[:, 4:, :], scale_tile[:, 4:, :])
-        for kt in range(KT // 2):
+        da1_2 = held([P, 4, P * PACK], BF16, "da1_2")
+        for j in (8, 9):
+            product(wide[:, j - 2, :], j, relu[4][:])
+        for j in (10, 11):
+            product(late[:, j - 8, :], j, relu[5][:])
+        quantise_parts(wide, "wide", ((1, 0, 0, 4), (1, 4, 2, 4), (2, 0, 0, 2)), "relu1")
+        quantise_parts(late, "late", ((1, 4, 0, 2), (2, 0, 2, 4)))
+        for kt in range(KT):
             pair_product(1, kt, "sums", nc.scalar.copy)
 
         def quantise_last(first, values, n0, n1):
@@ -309,7 +329,6 @@ def tile_moe_bdx_glu_relu_kernel(
             zero_or_one = flat(last_mask[4 + n0 // 2][:, n0 % 2 : n0 % 2 + n1 - n0, :])
             nc.vector.tensor_tensor(values, values, zero_or_one, ALU.mult)
 
-        quantise_last(0, da3_2, 0, 4)
         product(da1_2[:, 0, :], 8, a3_of[4])
         product(da1_2[:, 1, :], 9, a3_of[4])
         product(da1_2[:, 2, :], 10, a3_of[5])
@@ -332,12 +351,11 @@ def tile_moe_bdx_glu_relu_kernel(
         last_product(1, 0, 2, "turned", nc.vector.tensor_copy)
         last_product(0, 2, 3, "turned", nc.scalar.copy)
         last_product(0, 3, 4, "turned", nc.scalar.copy)
-        last_product(1, 2, 4, "sums", nc.scalar.copy)
 
         def fetch(kt, t0, t1):
             first = row_tile([P, t1 - t0], "first")
             window = dx[kt][:].indirect(offsets(pos1_sb, t0, t1))
-            if kt == 0:
+            if (kt, t0) == (0, 0):
                 nc.vector.tensor_copy(first[:], window)
             else:
                 nc.scalar.activation(first[:], window, ACT.Copy)
@@ -349,10 +367,10 @@ def tile_moe_bdx_glu_relu_kernel(
             nc.vector.tensor_tensor(total[:], second, first, ALU.add)
             nc.sync.dma_start(out[kt * P : (kt + 1) * P, t0:t1], total[:])
 
-        for kt, cuts in enumerate(((0, T // 2, T), (0, T), (0, T), (0, T // 3, 2 * T // 3, T))):
-            if kt >= KT // 2:
-                for g in range(1, PAIRS):
-                    pair_product(g, kt, "sums", nc.scalar.copy)
+        for kt in range(KT):
+            if kt > 0:
+                last_product(kt, 2 if kt == 1 else 0, 4, "sums", nc.scalar.copy)
+            cuts = (0, 2 * T // 3, T) if kt in (0, KT - 1) else (0, T)
             pieces = [(t0, t1, fetch(kt, t0, t1)) for t0, t1 in zip(cuts, cuts[1:])]
-            for t0, t1, first in pieces:
+            for t0, t1, first in pieces[::-1] if kt == 0 else pieces:
                 add_and_store(kt, t0, t1, first[:])

@@ -152,8 +152,9 @@ def tile_moe_bdx_glu_relu_kernel(
         nc.sync.dma_start(pos2_sb[:], pos2)
         load_saved(a1_of, a1, "a1", 4, 6)
         load_second_words(0, 2, 0, KT)
-        load_saved(a3_of, a3, "a3", 4, 6)
+        load_saved(a3_of, a3, "a3", 4, 5)
         load_second_words(2, 4, 0, KT)
+        load_saved(a3_of, a3, "a3", 5, 6)
         load_second_words(4, 6, 0, KT)
 
         gate_ps = bank([P, PACK, P], "gate_ps", "turned")
@@ -209,34 +210,35 @@ def tile_moe_bdx_glu_relu_kernel(
 
         words, scales = {}, {}
 
-        def second_product(acc, kt, g, n0, n1):
-            e = 2 * g + n0 // 2
-            for first, w, ws in ((0, w3, w3s), (4, w1, w1s)):
-                nc.tensor.matmul_mx(
-                    out=acc,
-                    lhsT=w[e, kt].bitcast(FP4X4),
-                    lhsT_scale=ws[:, e, kt * P : (kt + 1) * P],
-                    rhs=flat(words[g, first, n0][:, 0 : n1 - n0, :]).bitcast(FP8X4),
-                    rhs_scale=flat(scales[g, first, n0][:, 0 : n1 - n0, :]),
-                    start=(first == 0),
-                    stop=(first == 4),
-                )
+        def second_pass(acc, kt, e, first):
+            g, n0 = e // 2, 2 * (e % 2)
+            w, ws = (w3, w3s) if first == 0 else (w1, w1s)
+            nc.tensor.matmul_mx(
+                out=acc,
+                lhsT=w[e, kt].bitcast(FP4X4),
+                lhsT_scale=ws[:, e, kt * P : (kt + 1) * P],
+                rhs=flat(words[g, first, n0][:, 0:2, :]).bitcast(FP8X4),
+                rhs_scale=flat(scales[g, first, n0][:, 0:2, :]),
+                start=(first == 0),
+                stop=(first == 4),
+            )
 
         def name_parts(g, first, n0, n1, word_tile, scale_tile):
             for n in range(n0, n1):
                 words[g, first, n] = word_tile[:, n - n0 :, :]
                 scales[g, first, n] = scale_tile[:, n - n0 :, :]
 
-        def pair_product(g, kt, tag, empty):
-            acc = bank([P, 4, P], "acc2", tag)
-            for n0, n1 in ((0, 2), (2, 3), (3, 4)) if g == PAIRS - 1 else ((0, 2), (2, 4)):
-                second_product(flat(acc[:, n0:n1, :]), kt, g, n0, n1)
-            empty(dx[kt][:, g * PAIR : (g + 1) * PAIR], flat(acc[:]))
+        def second_product(kt, e0, e1, tag, empty):
+            acc = bank([P, e1 - e0, C], "acc2", tag)
+            for e in range(e0, e1):
+                for first in (0, 4):
+                    second_pass(acc[:, e - e0, :], kt, e, first)
+            empty(dx[kt][:, e0 * C : e1 * C], flat(acc[:]))
 
         masked_dh = {}
 
-        def rectify_woven(e):
-            relu[e] = held([P, 2, P * PACK], F32, "relu%d" % e)
+        def rectify_woven(e, tag=None):
+            relu[e] = held([P, 2, P * PACK], F32, "relu%d" % e, tag)
             nc.scalar.activation(woven(flat(relu[e][:])), in_runs(a1_of[e]), ACT.Relu)
 
         def mask_dh(e):
@@ -285,72 +287,58 @@ def tile_moe_bdx_glu_relu_kernel(
             last_mask[e] = held([P, 2, P * PACK], BF16, "mask%d" % e)
             nc.scalar.activation(woven(flat(last_mask[e][:])), in_runs(relu[e][:]), ACT.Sign)
 
+        def lay_mask(values, e, n0, n1):
+            zero_or_one = flat(last_mask[e][:, n0:n1, :])
+            nc.vector.tensor_tensor(flat(values), flat(values), zero_or_one, ALU.mult)
+
         make_dh(1)
-        rectify_woven(2)
-        rectify(3, None)
-        make_mask(3)
-        wide = held([P, 8, P * PACK], BF16, "wide")
-        mask_dh(2)
-        woven_da3(wide[:, 0:2, :], 2)
-        for j in (6, 7):
-            product(wide[:, j - 4, :], j, relu[3][:])
-        for j in (6, 7):
-            product(wide[:, j - 2, :], j, a3_of[3])
-        nc.vector.tensor_tensor(flat(wide[:, 4:6, :]), flat(wide[:, 4:6, :]), flat(last_mask[3][:]), ALU.mult)
-        quantise_parts(da_0, "first", ((0, 0, 0, 4), (0, 4, 0, 4)), "relu3")
-        late = held([P, 4, P * PACK], BF16, "late", "a1_0")
-        pool_da1(late[:, 0:2, :], 2)
+        for e in (2, 3):
+            rectify(e, None)
+        for e in (2, 3):
+            make_mask(e)
+        da_1 = held([P, 8, P * PACK], BF16, "da_1")
+        for j in range(4, 8):
+            product(da_1[:, j - 4, :], j, relu[j // 2][:])
+        for j in range(4, 8):
+            product(da_1[:, j, :], j, a3_of[j // 2])
+        for e in (2, 3):
+            lay_mask(da_1[:, 2 * e : 2 * e + 2, :], e, 0, 2)
+        quantise_parts(da_0, "first", ((0, 0, 0, 4), (0, 4, 0, 4)), "a3_2")
+        quantise_parts(da_1, "second", ((1, 0, 0, 4), (1, 4, 0, 4)))
 
         make_dh(2)
-        for e in (4, 5):
-            rectify(e, "relu%d" % (e - 4))
-        for e in (4, 5):
-            make_mask(e)
-        for kt in range(KT):
-            pair_product(0, kt, "sums", nc.scalar.copy)
-        da1_2 = held([P, 4, P * PACK], BF16, "da1_2")
-        for j in (8, 9):
-            product(wide[:, j - 2, :], j, relu[4][:])
+        rectify_woven(4, "relu0")
+        rectify(5, "relu1")
+        make_mask(5)
+        for g in range(2):
+            for kt in range(KT):
+                second_product(kt, 2 * g, 2 * g + 2, "sums", nc.scalar.copy)
+        da3_2 = held([P, 4, P * PACK], BF16, "da3_2")
+        da1_4 = held([P, 2, P * PACK], BF16, "da1_4")
+        da1_5 = held([P, 2, P * PACK], BF16, "da1_5")
+        mask_dh(4)
+        for n in range(2):
+            nc.gpsimd.tensor_tensor(
+                words_of(da1_4[:, n, :]), words_of(masked_dh[4][:, n, :]), by_slot(half(a3_of[4], n)), ALU.mult
+            )
+        woven_da3(da3_2[:, 0:2, :], 4)
         for j in (10, 11):
-            product(late[:, j - 8, :], j, relu[5][:])
-        quantise_parts(wide, "wide", ((1, 0, 0, 4), (1, 4, 2, 4), (2, 0, 0, 2)), "relu1")
-        quantise_parts(late, "late", ((1, 4, 0, 2), (2, 0, 2, 4)))
-        for kt in range(KT):
-            pair_product(1, kt, "sums", nc.scalar.copy)
+            product(da3_2[:, j - 8, :], j, relu[5][:])
+        for j in (10, 11):
+            product(da1_5[:, j - 10, :], j, a3_of[5])
+        for n in range(2):
+            lay_mask(da1_5[:, n : n + 1, :], 5, n, n + 1)
+        quantise_parts(da3_2, "last_da3", ((2, 0, 0, 4),), "a3_5")
+        quantise_parts(da1_4, "fifth_da1", ((2, 4, 0, 2),), "mask5")
+        quantise_parts(da1_5, "last_da1", ((2, 4, 2, 4),))
 
-        def quantise_last(first, values, n0, n1):
-            word_tile = held([P, n1 - n0, P], U32, "words2_%d_%d" % (first, n0))
-            scale_tile = held([P, n1 - n0, P], U8, "scales2_%d_%d" % (first, n0))
-            quantise(word_tile[:], scale_tile[:], values[:, n0:n1, :])
-            name_parts(2, first, n0, n1, word_tile, scale_tile)
-
-        def lay_mask(n0, n1):
-            values = flat(da1_2[:, n0:n1, :])
-            zero_or_one = flat(last_mask[4 + n0 // 2][:, n0 % 2 : n0 % 2 + n1 - n0, :])
-            nc.vector.tensor_tensor(values, values, zero_or_one, ALU.mult)
-
-        product(da1_2[:, 0, :], 8, a3_of[4])
-        product(da1_2[:, 1, :], 9, a3_of[4])
-        product(da1_2[:, 2, :], 10, a3_of[5])
-        lay_mask(0, 2)
-        product(da1_2[:, 3, :], 11, a3_of[5])
-        quantise_last(4, da1_2, 0, 2)
-        lay_mask(2, 3)
-        lay_mask(3, 4)
-        quantise_last(4, da1_2, 2, 3)
-        quantise_last(4, da1_2, 3, 4)
-
-        def last_product(kt, n0, n1, tag, empty):
-            acc = bank([P, n1 - n0, P], "acc_last", tag)
-            for m0, m1 in ((0, 2), (2, 3), (3, 4)):
-                if n0 <= m0 < n1:
-                    second_product(flat(acc[:, m0 - n0 : m1 - n0, :]), kt, 2, m0, m1)
-            empty(dx[kt][:, S - PAIR + n0 * P : S - PAIR + n1 * P], flat(acc[:]))
-
-        last_product(0, 0, 2, "turned", nc.scalar.copy)
-        last_product(1, 0, 2, "turned", nc.vector.tensor_copy)
-        last_product(0, 2, 3, "turned", nc.scalar.copy)
-        last_product(0, 3, 4, "turned", nc.scalar.copy)
+        last = {e: bank([P, C], "acc_last", "turned") for e in (4, 5)}
+        for e in (4, 5):
+            second_pass(last[e][:], 0, e, 0)
+        for e in (4, 5):
+            second_pass(last[e][:], 0, e, 4)
+            nc.scalar.copy(dx[0][:, e * C : (e + 1) * C], last[e][:])
+        second_product(1, 4, 5, "turned", nc.vector.tensor_copy)
 
         def fetch(kt, t0, t1):
             first = row_tile([P, t1 - t0], "first")
@@ -369,7 +357,7 @@ def tile_moe_bdx_glu_relu_kernel(
 
         for kt in range(KT):
             if kt > 0:
-                last_product(kt, 2 if kt == 1 else 0, 4, "sums", nc.scalar.copy)
+                second_product(kt, 5 if kt == 1 else 4, E, "sums", nc.scalar.copy)
             cuts = (0, 2 * T // 3, T) if kt in (0, KT - 1) else (0, T)
             pieces = [(t0, t1, fetch(kt, t0, t1)) for t0, t1 in zip(cuts, cuts[1:])]
             for t0, t1, first in pieces[::-1] if kt == 0 else pieces:

@@ -57,9 +57,8 @@ def tile_moe_bdx_glu_relu_kernel(
         offs_sb = keep.tile([P, S // PER_COLUMN], U16, name="offs_sb")
         pos1_sb = keep.tile([P, T // PER_COLUMN], U16, name="pos1_sb")
         pos2_sb = keep.tile([P, T // PER_COLUMN], U16, name="pos2_sb")
-        dyw = held([P, T + WORD_WINDOW], I32, "dyw")
+        dyw = held([P, PASSES * T], I32, "dyw")
         dys = held([P, BYTE_WINDOW], U8, "dys")
-        gw = [[held([P, cols], U32, "gw%d_%d" % (o, cols)) for cols in (PAIR, S - PAIR)] for o in range(PASSES)]
         gs = [held([P, S], U8, "gs%d" % o) for o in range(PASSES)]
         w2 = [held([P, 2 * PASSES, 2 * H], U8, "w2_%d" % g) for g in range(PAIRS)]
         w2s = [held([P, 2 * PASSES, H], U8, "w2s_%d" % g) for g in range(PAIRS)]
@@ -79,7 +78,6 @@ def tile_moe_bdx_glu_relu_kernel(
         nc.gpsimd.memset(flat(w2s[0][:]).bitcast(I32), 0)
         make_identity(nc, ident[:])
         nc.gpsimd.memset(gs[1][:].bitcast(I32), 0)
-        nc.gpsimd.memset(dyw[:, PASSES * T :], 0)
         for plane in (w2s[1], w2s[2], w3s, w1s):
             nc.gpsimd.memset(flat(plane[:]).bitcast(I32), 0)
 
@@ -124,7 +122,7 @@ def tile_moe_bdx_glu_relu_kernel(
                 dy_scales[:, PACK * q : PACK * (q + 1), :].bitcast(I32),
             )
         nc.sync.dma_start(
-            dyw[:, 0 : PASSES * T].rearrange("p (o t) -> p o t", o=PASSES),
+            dyw[:].rearrange("p (o t) -> p o t", o=PASSES),
             dy_words.rearrange("o p t d -> p o (t d)").bitcast(I32),
         )
         nc.sync.dma_start(gate_rows[0:TILES, :], gate[0].rearrange("(j s) -> j s", s=P))
@@ -135,11 +133,13 @@ def tile_moe_bdx_glu_relu_kernel(
         nc.vector.tensor_copy(gs[0][:], dys[:].indirect(offs_sb[:]))
         for r in range(PACK):
             nc.sync.dma_start(gs[1][r:P:QUADRANT].bitcast(I32), gs[0][PACK + r : P : QUADRANT].bitcast(I32))
-        for part, (first, end, window) in enumerate(((0, PAIR, T), (PAIR, S, WORD_WINDOW))):
-            for o in range(PASSES):
-                nc.vector.tensor_copy(
-                    gw[o][part][:], dyw[:, o * T : o * T + window].bitcast(U32).indirect(offsets(offs_sb, first, end))
-                )
+        gw = {}
+        for o, g0, g1 in ((0, 0, 1), (1, 0, 1), (0, 1, 3), (1, 1, 2), (1, 2, 3)):
+            tile = held([P, (g1 - g0) * PAIR], U32, "gw%d_%d" % (o, g0))
+            window = dyw[:, o * T : o * T + (T if g1 - g0 == 1 else WORD_WINDOW)].bitcast(U32)
+            nc.vector.tensor_copy(tile[:], window.indirect(offsets(offs_sb, g0 * PAIR, g1 * PAIR)))
+            for j in range(4 * g0, 4 * g1):
+                gw[o, j] = tile[:, (j - 4 * g0) * P : (j - 4 * g0 + 1) * P]
 
         load_saved(a3_of, a3, "a3", 0, 2)
         load_scale_rows(w2s[1], w2_scales[2:4])
@@ -163,15 +163,19 @@ def tile_moe_bdx_glu_relu_kernel(
 
         dh_cols, relu = {}, {}
 
+        def turn(j, rows):
+            dh_cols[j] = bank([P, PACK, P], "dh_cols", "turned")
+            for t in range(PACK):
+                nc.tensor.transpose(dh_cols[j][:, t, :], rows[:, t, :], ident[:])
+
         def make_dh(g):
             rows = {}
             for j in range(4 * g, 4 * g + 4):
-                part, first = (0, j * P) if g == 0 else (1, j * P - PAIR)
                 acc = bank([P, H], "acc1", "sums")
                 for o in range(PASSES):
                     nc.tensor.matmul_mx(
                         out=acc[:],
-                        lhsT=gw[o][part][:, first : first + P].bitcast(FP8X4),
+                        lhsT=gw[o, j].bitcast(FP8X4),
                         lhsT_scale=gs[o][:, j * P : (j + 1) * P],
                         rhs=w2[g][:, (j // 2 % 2) * PASSES + o, :].bitcast(FP4X4),
                         rhs_scale=w2s[g][:, (j // 2 % 2) * PASSES + o, :],
@@ -182,10 +186,11 @@ def tile_moe_bdx_glu_relu_kernel(
                 nc.scalar.activation(
                     rows[j][:], acc[:].rearrange("s (m t) -> s t m", t=PACK), ACT.Copy, scale=gate_col[:, j : j + 1]
                 )
-            for j in range(4 * g, 4 * g + 4):
-                dh_cols[j] = bank([P, PACK, P], "dh_cols", "turned")
-                for t in range(PACK):
-                    nc.tensor.transpose(dh_cols[j][:, t, :], rows[j][:, t, :], ident[:])
+                if g == 0:
+                    turn(j, rows[j])
+            if g > 0:
+                for j in range(4 * g, 4 * g + 4):
+                    turn(j, rows[j])
 
         def half(expert_view, j):
             return expert_view[:, :, (j % 2) * P : (j % 2 + 1) * P]
@@ -210,15 +215,15 @@ def tile_moe_bdx_glu_relu_kernel(
 
         words, scales = {}, {}
 
-        def second_pass(acc, kt, e, first):
+        def second_pass(acc, kt, e, first, t0=0, t1=2):
             g, n0 = e // 2, 2 * (e % 2)
             w, ws = (w3, w3s) if first == 0 else (w1, w1s)
             nc.tensor.matmul_mx(
                 out=acc,
                 lhsT=w[e, kt].bitcast(FP4X4),
                 lhsT_scale=ws[:, e, kt * P : (kt + 1) * P],
-                rhs=flat(words[g, first, n0][:, 0:2, :]).bitcast(FP8X4),
-                rhs_scale=flat(scales[g, first, n0][:, 0:2, :]),
+                rhs=flat(words[g, first, n0][:, t0:t1, :]).bitcast(FP8X4),
+                rhs_scale=flat(scales[g, first, n0][:, t0:t1, :]),
                 start=(first == 0),
                 stop=(first == 4),
             )
@@ -235,110 +240,72 @@ def tile_moe_bdx_glu_relu_kernel(
                     second_pass(acc[:, e - e0, :], kt, e, first)
             empty(dx[kt][:, e0 * C : e1 * C], flat(acc[:]))
 
-        masked_dh = {}
+        def prepare(g):
+            even = held([P, 2, P * PACK], F32, "relu%d" % (2 * g), "woven_relu")
+            nc.scalar.activation(woven(flat(even[:])), in_runs(a1_of[2 * g]), ACT.Relu)
+            odd = held([P, PACK, C], F32, "relu%d" % (2 * g + 1), "relu")
+            nc.scalar.activation(odd[:], a1_of[2 * g + 1], ACT.Relu)
+            mask = held([P, 2, P * PACK], BF16, "mask%d" % g, "mask")
+            nc.scalar.activation(woven(flat(mask[:])), in_runs(odd[:]), ACT.Sign)
+            return even, odd, mask
 
-        def rectify_woven(e, tag=None):
-            relu[e] = held([P, 2, P * PACK], F32, "relu%d" % e, tag)
-            nc.scalar.activation(woven(flat(relu[e][:])), in_runs(a1_of[e]), ACT.Relu)
-
-        def mask_dh(e):
-            masked_dh[e] = held([P, 2, P * PACK], F32, "masked_dh%d" % e)
-            for j in (2 * e, 2 * e + 1):
+        def make_da(g, even, odd, mask):
+            j0 = 4 * g
+            da = held([P, 8, P * PACK], BF16, "da%d" % g, "a1_%d" % (2 * g))
+            for n in range(2):
+                masked = held([P, P * PACK], F32, "masked_dh%d" % (j0 + n), "masked_dh%d" % n)
                 nc.vector.scalar_tensor_tensor(
-                    words_of(masked_dh[e][:, j % 2, :]), words_of(relu[e][:, j % 2, :]), 0.0, by_slot(dh_cols[j][:]),
-                    ALU.is_gt, ALU.mult,
+                    words_of(masked[:]), words_of(even[:, n, :]), 0.0, by_slot(dh_cols[j0 + n][:]), ALU.is_gt, ALU.mult
                 )
-
-        def pool_da1(dst, e):
-            nc.gpsimd.tensor_tensor(words_of(flat(dst)), words_of(flat(masked_dh[e][:])), by_slot(a3_of[e]), ALU.mult)
-
-        def woven_da3(dst, e):
+                nc.gpsimd.tensor_tensor(
+                    words_of(da[:, 4 + n, :]), words_of(masked[:]), by_slot(half(a3_of[2 * g], n)), ALU.mult
+                )
             for n in range(2):
                 nc.vector.tensor_tensor(
-                    words_of(dst[:, n, :]), by_slot(dh_cols[2 * e + n][:]), words_of(relu[e][:, n, :]), ALU.mult
+                    words_of(da[:, n, :]), by_slot(dh_cols[j0 + n][:]), words_of(even[:, n, :]), ALU.mult
                 )
+            for n in (2, 3):
+                product(da[:, n, :], j0 + n, odd[:])
+            for n in (2, 3):
+                product(da[:, 4 + n, :], j0 + n, a3_of[2 * g + 1])
+            word_tile = held([P, 8, P], U32, "words%d" % g)
+            scale_tile = held([P, 8, P], U8, "scales%d" % g, "a3_%d" % (2 * g + g // 2))
+            name_parts(g, 0, 0, 4, word_tile, scale_tile)
+            name_parts(g, 4, 0, 4, word_tile[:, 4:, :], scale_tile[:, 4:, :])
 
-        for e in range(2):
-            rectify_woven(e)
+            def quantise_range(n0, n1):
+                quantise(word_tile[:, n0:n1, :], scale_tile[:, n0:n1, :], da[:, n0:n1, :])
+
+            if g == PAIRS - 1:
+                quantise_range(0, 4)
+                quantise_range(4, 6)
+            for n in (2, 3):
+                nc.vector.tensor_tensor(da[:, 4 + n, :], da[:, 4 + n, :], mask[:, n - 2, :], ALU.mult)
+            for n0, n1 in ((6, 7), (7, 8)) if g == PAIRS - 1 else ((0, 4), (4, 8)):
+                quantise_range(n0, n1)
+
+        factors = prepare(0)
         make_dh(0)
-        da_0 = held([P, 8, P * PACK], BF16, "da_0", "a1_0")
-        for e in range(2):
-            mask_dh(e)
-            pool_da1(da_0[:, 4 + 2 * e : 6 + 2 * e, :], e)
-        for e in range(2):
-            woven_da3(da_0[:, 2 * e : 2 * e + 2, :], e)
+        make_da(0, *factors)
+        for g in range(1, PAIRS):
+            make_dh(g)
+            factors = prepare(g)
+            if g == PAIRS - 1:
+                for kt in range(KT):
+                    second_product(kt, 0, 2, "sums", nc.scalar.copy)
+            make_da(g, *factors)
+        for kt in range(KT):
+            second_product(kt, 2, 4, "sums", nc.scalar.copy)
 
-        def quantise_parts(values, name, parts, scale_tag=None):
-            word_tile = held([P, values.shape[1], P], U32, "words_" + name)
-            scale_tile = held([P, values.shape[1], P], U8, "scales_" + name, scale_tag)
-            quantise(word_tile[:], scale_tile[:], values[:])
-            at = 0
-            for g, first, n0, n1 in parts:
-                name_parts(g, first, n0, n1, word_tile[:, at:, :], scale_tile[:, at:, :])
-                at = at + n1 - n0
-
-        last_mask = {}
-
-        def rectify(e, tag):
-            relu[e] = held([P, PACK, C], F32, "relu%d" % e, tag)
-            nc.scalar.activation(relu[e][:], a1_of[e], ACT.Relu)
-
-        def make_mask(e):
-            last_mask[e] = held([P, 2, P * PACK], BF16, "mask%d" % e)
-            nc.scalar.activation(woven(flat(last_mask[e][:])), in_runs(relu[e][:]), ACT.Sign)
-
-        def lay_mask(values, e, n0, n1):
-            zero_or_one = flat(last_mask[e][:, n0:n1, :])
-            nc.vector.tensor_tensor(flat(values), flat(values), zero_or_one, ALU.mult)
-
-        make_dh(1)
-        for e in (2, 3):
-            rectify(e, None)
-        for e in (2, 3):
-            make_mask(e)
-        da_1 = held([P, 8, P * PACK], BF16, "da_1")
-        for j in range(4, 8):
-            product(da_1[:, j - 4, :], j, relu[j // 2][:])
-        for j in range(4, 8):
-            product(da_1[:, j, :], j, a3_of[j // 2])
-        for e in (2, 3):
-            lay_mask(da_1[:, 2 * e : 2 * e + 2, :], e, 0, 2)
-        quantise_parts(da_0, "first", ((0, 0, 0, 4), (0, 4, 0, 4)), "a3_2")
-        quantise_parts(da_1, "second", ((1, 0, 0, 4), (1, 4, 0, 4)))
-
-        make_dh(2)
-        rectify_woven(4, "relu0")
-        rectify(5, "relu1")
-        make_mask(5)
-        for g in range(2):
-            for kt in range(KT):
-                second_product(kt, 2 * g, 2 * g + 2, "sums", nc.scalar.copy)
-        da3_2 = held([P, 4, P * PACK], BF16, "da3_2")
-        da1_4 = held([P, 2, P * PACK], BF16, "da1_4")
-        da1_5 = held([P, 2, P * PACK], BF16, "da1_5")
-        mask_dh(4)
-        for n in range(2):
-            nc.gpsimd.tensor_tensor(
-                words_of(da1_4[:, n, :]), words_of(masked_dh[4][:, n, :]), by_slot(half(a3_of[4], n)), ALU.mult
-            )
-        woven_da3(da3_2[:, 0:2, :], 4)
-        for j in (10, 11):
-            product(da3_2[:, j - 8, :], j, relu[5][:])
-        for j in (10, 11):
-            product(da1_5[:, j - 10, :], j, a3_of[5])
-        for n in range(2):
-            lay_mask(da1_5[:, n : n + 1, :], 5, n, n + 1)
-        quantise_parts(da3_2, "last_da3", ((2, 0, 0, 4),), "a3_5")
-        quantise_parts(da1_4, "fifth_da1", ((2, 4, 0, 2),), "mask5")
-        quantise_parts(da1_5, "last_da1", ((2, 4, 2, 4),))
-
-        last = {e: bank([P, C], "acc_last", "turned") for e in (4, 5)}
-        for e in (4, 5):
-            second_pass(last[e][:], 0, e, 0)
-        for e in (4, 5):
-            second_pass(last[e][:], 0, e, 4)
-            nc.scalar.copy(dx[0][:, e * C : (e + 1) * C], last[e][:])
+        steps = ((4, 0, 2), (5, 0, 1), (5, 1, 2))
+        last = [bank([P, (t1 - t0) * P], "acc_last", "turned") for e, t0, t1 in steps]
+        for acc, (e, t0, t1) in zip(last, steps):
+            second_pass(acc[:], 0, e, 0, t0, t1)
+        for acc, (e, t0, t1) in zip(last, steps):
+            second_pass(acc[:], 0, e, 4, t0, t1)
+            nc.scalar.copy(dx[0][:, e * C + t0 * P : e * C + t1 * P], acc[:])
         second_product(1, 4, 5, "turned", nc.vector.tensor_copy)
+        second_product(2, 4, 5, "sums", nc.vector.tensor_copy)
 
         def fetch(kt, t0, t1):
             first = row_tile([P, t1 - t0], "first")
@@ -357,7 +324,7 @@ def tile_moe_bdx_glu_relu_kernel(
 
         for kt in range(KT):
             if kt > 0:
-                second_product(kt, 5 if kt == 1 else 4, E, "sums", nc.scalar.copy)
+                second_product(kt, 5 if kt < KT - 1 else 4, E, "sums", nc.scalar.copy)
             cuts = (0, 2 * T // 3, T) if kt in (0, KT - 1) else (0, T)
             pieces = [(t0, t1, fetch(kt, t0, t1)) for t0, t1 in zip(cuts, cuts[1:])]
             for t0, t1, first in pieces[::-1] if kt == 0 else pieces:

@@ -61,7 +61,7 @@ def tile_moe_bdx_glu_relu_kernel(
         dys = held([P, BYTE_WINDOW], U8, "dys")
         gs = [held([P, S], U8, "gs%d" % o) for o in range(PASSES)]
         w2 = [held([P, 2 * PASSES, 2 * H], U8, "w2_%d" % g) for g in range(PAIRS)]
-        w2s = [held([P, 2 * PASSES, H], U8, "w2s_%d" % g) for g in range(PAIRS)]
+        w2s = [held([P, n * PASSES, H], U8, "w2s_%d" % n) for n in (2, E - 2)]
         w1s = held([P, E, K], U8, "w1s")
         w3s = held([P, E, K], U8, "w3s")
         dx = [held([P, S], F32, "dx%d" % kt) for kt in range(KT)]
@@ -78,7 +78,7 @@ def tile_moe_bdx_glu_relu_kernel(
         nc.gpsimd.memset(flat(w2s[0][:]).bitcast(I32), 0)
         make_identity(nc, ident[:])
         nc.gpsimd.memset(gs[1][:].bitcast(I32), 0)
-        for plane in (w2s[1], w2s[2], w3s, w1s):
+        for plane in (w2s[1], w3s, w1s):
             nc.gpsimd.memset(flat(plane[:]).bitcast(I32), 0)
 
         def load_scale_rows(plane, scale_rows):
@@ -142,20 +142,19 @@ def tile_moe_bdx_glu_relu_kernel(
                 gw[o, j] = tile[:, (j - 4 * g0) * P : (j - 4 * g0 + 1) * P]
 
         load_saved(a3_of, a3, "a3", 0, 2)
-        load_scale_rows(w2s[1], w2_scales[2:4])
+        load_scale_rows(w2s[1], w2_scales[2:E])
         load_words(w2, w2_words, 1)
         load_saved(a1_of, a1, "a1", 2, 4)
-        nc.sync.dma_start(pos1_sb[:], pos1)
         load_saved(a3_of, a3, "a3", 2, 4)
-        load_scale_rows(w2s[2], w2_scales[4:6])
         load_words(w2, w2_words, 2)
-        nc.sync.dma_start(pos2_sb[:], pos2)
         load_saved(a1_of, a1, "a1", 4, 6)
         load_second_words(0, 2, 0, KT)
         load_saved(a3_of, a3, "a3", 4, 5)
         load_second_words(2, 4, 0, KT)
         load_saved(a3_of, a3, "a3", 5, 6)
         load_second_words(4, 6, 0, KT)
+        nc.sync.dma_start(pos1_sb[:], pos1)
+        nc.sync.dma_start(pos2_sb[:], pos2)
 
         gate_ps = bank([P, PACK, P], "gate_ps", "turned")
         nc.tensor.transpose(gate_ps[:, 0, :], gate_rows[:], ident[:])
@@ -178,7 +177,7 @@ def tile_moe_bdx_glu_relu_kernel(
                         lhsT=gw[o, j].bitcast(FP8X4),
                         lhsT_scale=gs[o][:, j * P : (j + 1) * P],
                         rhs=w2[g][:, (j // 2 % 2) * PASSES + o, :].bitcast(FP4X4),
-                        rhs_scale=w2s[g][:, (j // 2 % 2) * PASSES + o, :],
+                        rhs_scale=w2s[min(g, 1)][:, (j // 2 - 2 * min(g, 1)) * PASSES + o, :],
                         start=(o == 0),
                         stop=(o == PASSES - 1),
                     )
@@ -319,13 +318,17 @@ def tile_moe_bdx_glu_relu_kernel(
         def add_and_store(kt, t0, t1, first):
             total = row_tile([P, t1 - t0], "total")
             second = dx[kt][:].indirect(offsets(pos2_sb, t0, t1))
+            if (kt, t1) == (KT - 1, T):
+                fetched = row_tile([P, t1 - t0], "second")
+                nc.scalar.activation(fetched[:], second, ACT.Copy)
+                second = fetched[:]
             nc.vector.tensor_tensor(total[:], second, first, ALU.add)
             nc.sync.dma_start(out[kt * P : (kt + 1) * P, t0:t1], total[:])
 
         for kt in range(KT):
             if kt > 0:
                 second_product(kt, 5 if kt < KT - 1 else 4, E, "sums", nc.scalar.copy)
-            cuts = (0, 2 * T // 3, T) if kt in (0, KT - 1) else (0, T)
+            cuts = {0: (0, 11 * T // 12, T), KT - 1: (0, 2 * T // 3, T)}.get(kt, (0, T))
             pieces = [(t0, t1, fetch(kt, t0, t1)) for t0, t1 in zip(cuts, cuts[1:])]
             for t0, t1, first in pieces[::-1] if kt == 0 else pieces:
                 add_and_store(kt, t0, t1, first[:])

from contextlib import ExitStack

import concourse.mybir as mybir
from concourse.masks import make_identity

K, T, E, C, H, N = 512, 768, 6, 256, 512, 1024
S = E * C
FLOPS = 2 * S * (N * H + 2 * H * K)
BYTES = (N * T + N * T // 32 + 2 * 4 * H * S + E * (N * H + 2 * H * K) // 2 + E * (N * H + 2 * H * K) // 32
         + 4 * S + 2 * 128 * (S + 2 * T) // 16 + 4 * K * T)

F32 = mybir.dt.float32
BF16 = mybir.dt.bfloat16
I32 = mybir.dt.int32
U32 = mybir.dt.uint32
U16 = mybir.dt.uint16
U8 = mybir.dt.uint8
FP8X4 = mybir.dt.float8_e4m3fn_x4
FP4X4 = mybir.dt.float4_e2m1fn_x4
ALU = mybir.AluOpType
ACT = mybir.ActivationFunctionType

P = 128
PACK = 4
PER_COLUMN = 16
QUADRANT = 32
PASSES = N // (P * PACK)
TILES = S // P
KT = K // P
PAIRS = E // 2
PAIR = 2 * C
WORD_WINDOW = 1408
BYTE_WINDOW = 2048
RUN = 2
PIECE = T // 2


def tile_moe_bdx_glu_relu_kernel(
    tc, dy_words, dy_scales, a1, a3, w2_words, w2_scales, w1_words, w1_scales, w3_words, w3_scales,
    gate, offs, pos1, pos2, out,
):
    nc = tc.nc
    with ExitStack() as ctx:
        keep = ctx.enter_context(tc.tile_pool(name="keep", bufs=1))
        ring = ctx.enter_context(tc.tile_pool(name="ring", bufs=8))
        psum = ctx.enter_context(tc.psum_pool(name="psum", bufs=4))

        def held(shape, dtype, name, tag=None):
            return keep.tile(shape, dtype, name=name, tag=tag or name, align_bytes=64)

        def bank(shape, name, tag):
            return psum.tile(shape, F32, name=name, tag=tag)

        def row_tile(shape, name):
            return ring.tile(shape, F32, name=name, tag="rows", align_bytes=64)

        offs_sb = keep.tile([P, S // PER_COLUMN], U16, name="offs_sb")
        pos1_sb = keep.tile([P, T // PER_COLUMN], U16, name="pos1_sb")
        pos2_sb = keep.tile([P, T // PER_COLUMN], U16, name="pos2_sb")
        dyw = held([P, PASSES * T], I32, "dyw")
        dys = held([P, BYTE_WINDOW], U8, "dys")
        gs = [held([P, S], U8, "gs%d" % o) for o in range(PASSES)]
        w2 = [held([P, 2 * PASSES, 2 * H], U8, "w2_%d" % g) for g in range(PAIRS)]
        w2s = [held([P, n * PASSES, H], U8, "w2s_%d" % n) for n in (2, E - 2)]
        w1s = held([P, E, K], U8, "w1s")
        w3s = held([P, E, K], U8, "w3s")
        dx = [held([P, S], F32, "dx%d" % kt) for kt in range(KT)]
        gate_rows = held([P, P], F32, "gate_rows")
        gate_col = held([P, TILES], F32, "gate_col")
        ident = held([P, P], F32, "ident")

        def flat(view):
            return view.rearrange("p a n -> p (a n)")

        nc.gpsimd.memset(dys[:, 0:T].bitcast(I32), 0)
        nc.gpsimd.memset(dys[:, T:].bitcast(I32), 0)
        nc.gpsimd.memset(gate_rows[:], 0.0)
        nc.gpsimd.memset(flat(w2s[0][:]).bitcast(I32), 0)
        make_identity(nc, ident[:])
        nc.gpsimd.memset(gs[1][:].bitcast(I32), 0)
        for plane in (w2s[1], w3s, w1s):
            nc.gpsimd.memset(flat(plane[:]).bitcast(I32), 0)

        def load_scale_rows(plane, scale_rows):
            rows = scale_rows.rearrange("e s f n -> f (e s) n").bitcast(I32)
            for r in range(PACK):
                nc.sync.dma_start(plane[r:P:QUADRANT].bitcast(I32), rows[r : PACK * PACK : PACK])

        def load_words(tiles, packed, g):
            nc.sync.dma_start(
                tiles[g][:].bitcast(I32), packed[2 * g : 2 * g + 2].rearrange("e s p n -> p (e s) n").bitcast(I32)
            )

        w1, w3 = {}, {}

        def load_second_words(e0, e1, kt0, kt1):
            for views, packed, name in ((w3, w3_words, "w3"), (w1, w1_words, "w1")):
                if e0 == 0:
                    load_scale_rows(*{"w3": (w3s, w3_scales), "w1": (w1s, w1_scales)}[name])
                tile = held([P, e1 - e0, 2 * P * (kt1 - kt0)], U8, "%s_%d_%d" % (name, e0, kt0))
                rows = packed[e0:e1, 0, :, 2 * P * kt0 : 2 * P * kt1].rearrange("e p n -> p e n")
                nc.sync.dma_start(tile[:].bitcast(I32), rows.bitcast(I32))
                for e in range(e0, e1):
                    for kt in range(kt0, kt1):
                        views[e, kt] = tile[:, e - e0, 2 * P * (kt - kt0) : 2 * P * (kt - kt0 + 1)]

        a1_of, a3_of = {}, {}

        def load_saved(views, saved, name, e0, e1):
            tile = held([P, PACK, (e1 - e0) * C], F32, "%s_%d" % (name, e0))
            nc.sync.dma_start(tile[:], saved.rearrange("(p t) s -> p t s", t=PACK)[:, :, e0 * C : e1 * C])
            for e in range(e0, e1):
                views[e] = tile[:, :, (e - e0) * C : (e - e0 + 1) * C]

        def offsets(list_sb, first, end):
            return list_sb[:, first // PER_COLUMN : end // PER_COLUMN]

        nc.sync.dma_start(offs_sb[:], offs)
        for q in range(P // QUADRANT):
            (nc.sync, nc.scalar)[q % 2].dma_start(
                dys[QUADRANT * q : QUADRANT * q + PACK * PASSES, 0:T].bitcast(I32),
                dy_scales[:, PACK * q : PACK * (q + 1), :].bitcast(I32),
            )
        nc.sync.dma_start(
            dyw[:].rearrange("p (o t) -> p o t", o=PASSES),
            dy_words.rearrange("o p t d -> p o (t d)").bitcast(I32),
        )
        nc.sync.dma_start(gate_rows[0:TILES, :], gate[0].rearrange("(j s) -> j s", s=P))
        load_saved(a1_of, a1, "a1", 0, 2)
        load_scale_rows(w2s[0], w2_scales[0:2])
        load_words(w2, w2_words, 0)

        nc.vector.tensor_copy(gs[0][:], dys[:].indirect(offs_sb[:]))
        for r in range(PACK):
            nc.sync.dma_start(gs[1][r:P:QUADRANT].bitcast(I32), gs[0][PACK + r : P : QUADRANT].bitcast(I32))
        gw = {}
        for o, g0, g1 in ((0, 0, 1), (1, 0, 1), (0, 1, 3), (1, 1, 2), (1, 2, 3)):
            tile = held([P, (g1 - g0) * PAIR], U32, "gw%d_%d" % (o, g0))
            window = dyw[:, o * T : o * T + (T if g1 - g0 == 1 else WORD_WINDOW)].bitcast(U32)
            nc.vector.tensor_copy(tile[:], window.indirect(offsets(offs_sb, g0 * PAIR, g1 * PAIR)))
            for j in range(4 * g0, 4 * g1):
                gw[o, j] = tile[:, (j - 4 * g0) * P : (j - 4 * g0 + 1) * P]

        load_saved(a3_of, a3, "a3", 0, 2)
        load_scale_rows(w2s[1], w2_scales[2:E])
        load_words(w2, w2_words, 1)
        load_saved(a1_of, a1, "a1", 2, 4)
        load_saved(a3_of, a3, "a3", 2, 4)
        load_words(w2, w2_words, 2)
        load_saved(a1_of, a1, "a1", 4, 6)
        load_second_words(0, 2, 0, KT)
        load_saved(a3_of, a3, "a3", 4, 5)
        load_second_words(2, 4, 0, KT)
        load_saved(a3_of, a3, "a3", 5, 6)
        load_second_words(4, 6, 0, KT)
        nc.sync.dma_start(pos1_sb[:], pos1)
        nc.sync.dma_start(pos2_sb[:], pos2)

        gate_ps = bank([P, PACK, P], "gate_ps", "turned")
        nc.tensor.transpose(gate_ps[:, 0, :], gate_rows[:], ident[:])
        nc.scalar.copy(gate_col[:], gate_ps[:, 0, 0:TILES])

        dh_cols, relu = {}, {}

        def turn(j, rows):
            dh_cols[j] = bank([P, PACK, P], "dh_cols", "turned")
            for t in range(PACK):
                nc.tensor.transpose(dh_cols[j][:, t, :], rows[:, t, :], ident[:])

        def make_dh(g):
            rows = {}
            for j in range(4 * g, 4 * g + 4):
                acc = bank([P, H], "acc1", "sums")
                for o in range(PASSES):
                    nc.tensor.matmul_mx(
                        out=acc[:],
                        lhsT=gw[o, j].bitcast(FP8X4),
                        lhsT_scale=gs[o][:, j * P : (j + 1) * P],
                        rhs=w2[g][:, (j // 2 % 2) * PASSES + o, :].bitcast(FP4X4),
                        rhs_scale=w2s[min(g, 1)][:, (j // 2 - 2 * min(g, 1)) * PASSES + o, :],
                        start=(o == 0),
                        stop=(o == PASSES - 1),
                    )
                rows[j] = row_tile([P, PACK, P], "dh_rows")
                nc.scalar.activation(
                    rows[j][:], acc[:].rearrange("s (m t) -> s t m", t=PACK), ACT.Copy, scale=gate_col[:, j : j + 1]
                )
                if g == 0:
                    turn(j, rows[j])
            if g > 0:
                for j in range(4 * g, 4 * g + 4):
                    turn(j, rows[j])

        def half(expert_view, j):
            return expert_view[:, :, (j % 2) * P : (j % 2 + 1) * P]

        def in_runs(view):
            return view.rearrange("p t (c i) -> p c t i", i=RUN)

        def woven(view):
            return view.rearrange("p (c i t) -> p c t i", i=RUN, t=PACK)

        def by_slot(view):
            return view.rearrange("p t s -> p s t")

        def words_of(view):
            return view.rearrange("p (s t) -> p s t", t=PACK)

        def product(dst, j, factor):
            nc.vector.tensor_tensor(woven(dst), in_runs(dh_cols[j][:]), in_runs(half(factor, j)), ALU.mult)

        def quantise(words, scales, values):
            nc.vector.quantize_mx(out=flat(words).bitcast(FP8X4), scales=flat(scales), in_=flat(values))

        words, scales = {}, {}

        def second_pass(acc, kt, e, first, t0=0, t1=2):
            g, n0 = e // 2, 2 * (e % 2)
            w, ws = (w3, w3s) if first == 0 else (w1, w1s)
            nc.tensor.matmul_mx(
                out=acc,
                lhsT=w[e, kt].bitcast(FP4X4),
                lhsT_scale=ws[:, e, kt * P : (kt + 1) * P],
                rhs=flat(words[g, first, n0][:, t0:t1, :]).bitcast(FP8X4),
                rhs_scale=flat(scales[g, first, n0][:, t0:t1, :]),
                start=(first == 0),
                stop=(first == 4),
            )

        def name_parts(g, first, n0, n1, word_tile, scale_tile):
            for n in range(n0, n1):
                words[g, first, n] = word_tile[:, n - n0 :, :]
                scales[g, first, n] = scale_tile[:, n - n0 :, :]

        def second_product(kt, e0, e1, tag, empty):
            acc = bank([P, e1 - e0, C], "acc2", tag)
            for e in range(e0, e1):
                for first in (0, 4):
                    second_pass(acc[:, e - e0, :], kt, e, first)
            empty(dx[kt][:, e0 * C : e1 * C], flat(acc[:]))

        def prepare(g):
            even = held([P, 2, P * PACK], F32, "relu%d" % (2 * g), "woven_relu")
            nc.scalar.activation(woven(flat(even[:])), in_runs(a1_of[2 * g]), ACT.Relu)
            odd = held([P, PACK, C], F32, "relu%d" % (2 * g + 1), "relu")
            nc.scalar.activation(odd[:], a1_of[2 * g + 1], ACT.Relu)
            mask = held([P, 2, P * PACK], BF16, "mask%d" % g, "mask")
            nc.scalar.activation(woven(flat(mask[:])), in_runs(odd[:]), ACT.Sign)
            return even, odd, mask

        def make_da(g, even, odd, mask):
            j0 = 4 * g
            da = held([P, 8, P * PACK], BF16, "da%d" % g, "a1_%d" % (2 * g))
            for n in range(2):
                masked = held([P, P * PACK], F32, "masked_dh%d" % (j0 + n), "masked_dh%d" % n)
                nc.vector.scalar_tensor_tensor(
                    words_of(masked[:]), words_of(even[:, n, :]), 0.0, by_slot(dh_cols[j0 + n][:]), ALU.is_gt, ALU.mult
                )
                nc.gpsimd.tensor_tensor(
                    words_of(da[:, 4 + n, :]), words_of(masked[:]), by_slot(half(a3_of[2 * g], n)), ALU.mult
                )
            for n in range(2):
                nc.vector.tensor_tensor(
                    words_of(da[:, n, :]), by_slot(dh_cols[j0 + n][:]), words_of(even[:, n, :]), ALU.mult
                )
            for n in (2, 3):
                product(da[:, n, :], j0 + n, odd[:])
            for n in (2, 3):
                product(da[:, 4 + n, :], j0 + n, a3_of[2 * g + 1])
            word_tile = held([P, 8, P], U32, "words%d" % g)
            scale_tile = held([P, 8, P], U8, "scales%d" % g, "a3_%d" % (2 * g + g // 2))
            name_parts(g, 0, 0, 4, word_tile, scale_tile)
            name_parts(g, 4, 0, 4, word_tile[:, 4:, :], scale_tile[:, 4:, :])

            def quantise_range(n0, n1):
                quantise(word_tile[:, n0:n1, :], scale_tile[:, n0:n1, :], da[:, n0:n1, :])

            if g == PAIRS - 1:
                quantise_range(0, 4)
                quantise_range(4, 6)
            for n in (2, 3):
                nc.vector.tensor_tensor(da[:, 4 + n, :], da[:, 4 + n, :], mask[:, n - 2, :], ALU.mult)
            for n0, n1 in ((6, 7), (7, 8)) if g == PAIRS - 1 else ((0, 4), (4, 8)):
                quantise_range(n0, n1)

        factors = prepare(0)
        make_dh(0)
        make_da(0, *factors)
        for g in range(1, PAIRS):
            make_dh(g)
            factors = prepare(g)
            if g == PAIRS - 1:
                for kt in range(KT):
                    second_product(kt, 0, 2, "sums", nc.scalar.copy)
            make_da(g, *factors)
        for kt in range(KT):
            second_product(kt, 2, 4, "sums", nc.scalar.copy)

        steps = ((4, 0, 2), (5, 0, 1), (5, 1, 2))
        last = [bank([P, (t1 - t0) * P], "acc_last", "turned") for e, t0, t1 in steps]
        for acc, (e, t0, t1) in zip(last, steps):
            second_pass(acc[:], 0, e, 0, t0, t1)
        for acc, (e, t0, t1) in zip(last, steps):
            second_pass(acc[:], 0, e, 4, t0, t1)
            nc.scalar.copy(dx[0][:, e * C + t0 * P : e * C + t1 * P], acc[:])
        second_product(1, 4, 5, "turned", nc.vector.tensor_copy)
        second_product(2, 4, 5, "sums", nc.vector.tensor_copy)

        def fetch(kt, t0, t1):
            first = row_tile([P, t1 - t0], "first")
            window = dx[kt][:].indirect(offsets(pos1_sb, t0, t1))
            if (kt, t0) == (0, 0):
                nc.vector.tensor_copy(first[:], window)
            else:
                nc.scalar.activation(first[:], window, ACT.Copy)
            return first

        def add_and_store(kt, t0, t1, first):
            total = row_tile([P, t1 - t0], "total")
            second = dx[kt][:].indirect(offsets(pos2_sb, t0, t1))
            if (kt, t1) == (KT - 1, T):
                fetched = row_tile([P, t1 - t0], "second")
                nc.scalar.activation(fetched[:], second, ACT.Copy)
                second = fetched[:]
            nc.vector.tensor_tensor(total[:], second, first, ALU.add)
            nc.sync.dma_start(out[kt * P : (kt + 1) * P, t0:t1], total[:])

        for kt in range(KT):
            if kt > 0:
                second_product(kt, 5 if kt < KT - 1 else 4, E, "sums", nc.scalar.copy)
            cuts = {0: (0, 11 * T // 12, T), KT - 1: (0, 2 * T // 3, T)}.get(kt, (0, T))
            pieces = [(t0, t1, fetch(kt, t0, t1)) for t0, t1 in zip(cuts, cuts[1:])]
            for t0, t1, first in pieces[::-1] if kt == 0 else pieces:
                add_and_store(kt, t0, t1, first[:])
